import numpy as np
import ml_dtypes


def mxq(x, axis, fmt="e4m3"):
    dtype, down = {"e4m3": (ml_dtypes.float8_e4m3fn, 7), "e5m2": (ml_dtypes.float8_e5m2, 14)}[fmt]
    v = np.moveaxis(np.asarray(x, np.float32).astype(ml_dtypes.bfloat16).astype(np.float64), axis, -1)
    blocks = v.reshape(v.shape[:-1] + (-1, 32))
    amax = np.abs(blocks).max(-1, keepdims=True)
    byte = np.maximum(np.where(amax > 0, np.frexp(amax)[1] - 1 + 127, 0) - down, 1)
    scale = np.exp2(byte - 127.0)
    codes = (blocks / scale).astype(np.float32).astype(dtype).astype(np.float64)
    return np.moveaxis((codes * scale).reshape(v.shape), -1, axis)


WIDE = False


def mx_kscale(k):
    if not WIDE:
        return np.ones(k)
    levels = np.array([24, -24, 12, -12, 0])
    if k % 512:
        return np.exp2(np.random.permutation(np.resize(levels, k // 32))).repeat(32)
    a = np.empty((k // 512, 16))
    for p in range(k // 512):
        a[p, :8] = np.random.permutation(np.resize(levels, 8))
        for g in range(8):
            far = levels[np.abs(levels - a[p, g]) >= 10]
            a[p, g + 8] = far[np.random.randint(len(far))]
    return np.exp2(a.ravel()).repeat(32)


def f64(x):
    return np.asarray(x).astype(np.float64)


def striped(idx):
    return np.tile(idx.reshape(-1, 16).T, (8, 1)).astype(np.uint16)


def unstriped(offs):
    return offs[:16].T.reshape(-1).astype(np.int64)


E2M1 = np.array([0.0, 0.5, 1.0, 1.5, 2.0, 3.0, 4.0, 6.0, -0.0, -0.5, -1.0, -1.5, -2.0, -3.0, -4.0, -6.0])


def pack_weight(w, fmt):
    k, n = w.shape
    w = f64(np.asarray(w, np.float32).astype(ml_dtypes.bfloat16)).reshape(k // 32, 32, n)
    amax = np.abs(w).max(1)
    if fmt == "e4m3":
        byte = np.frexp(amax)[1] - 1 + 127 - 7
    else:
        mant, ex = np.frexp(amax / 6.0)
        byte = np.where(mant > 0.5, ex, ex - 1) + 127
    byte = np.clip(np.where(amax > 0, byte, 1), 1, 254)
    scaled = (w * np.exp2(127.0 - byte)[:, None, :]).reshape(k, n).astype(np.float32)
    by_word = np.ascontiguousarray(scaled.reshape(k // 512, 128, 4, n).transpose(0, 1, 3, 2))
    if fmt == "e4m3":
        words = by_word.astype(ml_dtypes.float8_e4m3fn).view(np.uint8)
    else:
        c = by_word.astype(ml_dtypes.float4_e2m1fn).view(np.uint8) & 0xF
        words = (c[..., 0::2] | (c[..., 1::2] << 4)).reshape(k // 512, 128, 2 * n)
    return np.ascontiguousarray(words), np.ascontiguousarray(byte.astype(np.uint8).reshape(k // 512, 16, n))


def unpack_weight(words, scales, fmt):
    g, _, n = scales.shape
    words = np.ascontiguousarray(words).reshape(g, 128, n, -1)
    if fmt == "e4m3":
        vals = words.view(ml_dtypes.float8_e4m3fn).astype(np.float64)
    else:
        nib = np.empty((g, 128, n, 4), np.uint8)
        nib[..., 0::2] = words & 0xF
        nib[..., 1::2] = words >> 4
        vals = E2M1[nib]
    vals = vals * np.repeat(np.exp2(scales.astype(np.float64) - 127.0), 8, axis=1)[..., None]
    return vals.transpose(0, 1, 3, 2).reshape(g * 512, n)


def pack_table4(v):
    words, scales = pack_weight(v, "e2m1")
    g, t = words.shape[0] // 2, v.shape[1]
    return np.ascontiguousarray(words.reshape(g, 2, 128, t, 2).transpose(0, 2, 3, 1, 4).reshape(g, 128, t, 4)), scales


def unpack_table4(words, scales):
    g, _, t, _ = words.shape
    return unpack_weight(words.reshape(g, 128, t, 2, 2).transpose(0, 3, 1, 2, 4).reshape(2 * g, 128, 2 * t), scales, "e2m1")


def sigm(f):
    return 1.0 / (1.0 + np.exp(-np.maximum(f, -700.0)))


K, N, T, J = 1024, 512, 2048, 1024


def setup_inputs():
    n = np.random.standard_normal
    s = mx_kscale(K)[:, None]
    p_tab = pack_table4(n((K, T)) * s)
    p_wa = pack_weight(n((K, N)) / np.sqrt(2 * K) / s, "e2m1")
    p_wb = pack_weight(n((K, N)) / np.sqrt(2 * K) / s, "e4m3")
    return {
        "tab_words": p_tab[0],
        "tab_scales": p_tab[1],
        "wa_words": p_wa[0],
        "wa_scales": p_wa[1],
        "wb_words": p_wb[0],
        "wb_scales": p_wb[1],
        "wc": (n((K, N)) / np.sqrt(K) / s).astype(np.float32),
        "wgo": np.tile(np.random.uniform(0.5, 2.0, J), (128, 1)).astype(np.float32),
        "offs": striped(np.random.permutation(T)[:J]),
        "offs2": striped(np.random.permutation(T)[:J]),
    }


def reference(tab_words, tab_scales, wa_words, wa_scales, wb_words, wb_scales, wc, wgo, offs, offs2):
    idx = unstriped(offs)
    idx2 = unstriped(offs2)
    tab_ = unpack_table4(tab_words, tab_scales)[:, idx]
    tabb_ = unpack_table4(tab_words, tab_scales)[:, idx2]
    wa_ = unpack_weight(wa_words, wa_scales, "e2m1")
    wb_ = unpack_weight(wb_words, wb_scales, "e4m3")
    za = wa_.T @ tabb_ + wb_.T @ tab_
    eta = sigm(za)
    wc_ = mxq(f64(wc), 0, "e4m3")
    ms = wc_.T @ tab_
    out = np.zeros((N, T))
    out[:, idx2] = f64(wgo)[0] * (eta * ms)
    return out

@@ -1,0 +1,233 @@
+from contextlib import ExitStack
+
+import concourse.mybir as mybir
+from concourse.masks import make_identity
+
+K, N, T, J = 1024, 512, 2048, 1024
+FLOPS = 3 * 2 * K * N * J
+
+F32 = mybir.dt.float32
+BF16 = mybir.dt.bfloat16
+I32 = mybir.dt.int32
+U32 = mybir.dt.uint32
+U16 = mybir.dt.uint16
+U8 = mybir.dt.uint8
+FP8X4 = mybir.dt.float8_e4m3fn_x4
+FP4X4 = mybir.dt.float4_e2m1fn_x4
+ACT = mybir.ActivationFunctionType
+MULT = mybir.AluOpType.mult
+
+P = 128
+PACK = 4
+K_PASS = P * PACK
+PASSES = K // K_PASS
+HALF = 512
+HALVES = J // HALF
+N_TILES = N // P
+BLOCKS = HALF // P
+WC_COLS = 256
+
+
+def tile_list_rgg_none_kernel(
+    tc, tab_words, tab_scales, wa_words, wa_scales, wb_words, wb_scales, wc, wgo, offs, offs2, out
+):
+    nc = tc.nc
+    with ExitStack() as ctx:
+        lists = ctx.enter_context(tc.tile_pool(name="lists", bufs=1))
+        keep = ctx.enter_context(tc.tile_pool(name="keep", bufs=1))
+        ring = ctx.enter_context(tc.tile_pool(name="ring", bufs=3))
+        psum = ctx.enter_context(tc.psum_pool(name="psum", bufs=2))
+        psum_ms = ctx.enter_context(tc.psum_pool(name="psum_ms", bufs=4))
+
+        src_list = lists.tile([P, J // 16], U16, name="src_list")
+        dst_list = lists.tile([P, J // 16], U16, name="dst_list")
+        nc.sync.dma_start(src_list[:], offs)
+        nc.sync.dma_start(dst_list[:], offs2)
+
+        table_scales = keep.tile([P, T], U8, name="table_scales", align_bytes=64)
+        nc.vector.memset(table_scales[:].bitcast(I32), 0)
+        for q in range(4):
+            nc.sync.dma_start(
+                table_scales[32 * q : 32 * q + 8, :].bitcast(I32),
+                tab_scales[:, 4 * q : 4 * q + 4, :].bitcast(I32),
+            )
+
+        wa_planes = keep.tile([P, PASSES, N], U8, name="wa_planes", align_bytes=64)
+        wb_planes = keep.tile([P, PASSES, N], U8, name="wb_planes", align_bytes=64)
+        moved = [keep.tile([P, J], U8, name="moved%d" % i, align_bytes=64) for i in range(2)]
+        warm_in = keep.tile([P, 1], F32, name="warm_in")
+        warm_out = keep.tile([P, 1], F32, name="warm_out")
+        nc.gpsimd.memset(warm_in[:], 0.0)
+        nc.scalar.activation(warm_out[:], warm_in[:], ACT.Sigmoid)
+        ident = keep.tile([P, P], F32, name="ident")
+        make_identity(nc, ident[:])
+        for planes, scales in ((wb_planes, wb_scales), (wa_planes, wa_scales)):
+            nc.gpsimd.memset(planes[:].bitcast(I32), 0)
+            for q in range(4):
+                nc.gpsimd.dma_start(
+                    planes[32 * q : 32 * q + 4, :, :].bitcast(I32),
+                    scales[:, 4 * q : 4 * q + 4, :].rearrange("a r n -> r a n").bitcast(I32),
+                )
+        for plane in moved:
+            nc.vector.memset(plane[:].bitcast(I32), 0)
+
+        windows = [keep.tile([P, T], F32, name="window%d" % i) for i in range(2)]
+        for window in windows:
+            nc.vector.memset(window[:], 0.0)
+
+        wc_raw = {}
+
+        def load_wc(a, c):
+            raw = keep.tile([P, PACK, WC_COLS], F32, name="wc_raw%d%d" % (a, c))
+            nc.sync.dma_start(
+                raw[:],
+                wc[a * K_PASS : (a + 1) * K_PASS, c * WC_COLS : (c + 1) * WC_COLS].rearrange(
+                    "(p i) n -> p i n", i=PACK
+                ),
+            )
+            wc_raw[a, c] = raw
+
+        table_words = keep.tile([P, T], I32, name="table_words", align_bytes=64)
+        load_wc(0, 0)
+        load_wc(0, 1)
+        nc.sync.dma_start(table_words[:], tab_words[0].rearrange("p t b -> p (t b)").bitcast(I32))
+        load_wc(1, 0)
+        load_wc(1, 1)
+        wb_codes = keep.tile([P, PASSES, N], I32, name="wb_codes", align_bytes=64)
+        nc.sync.dma_start(wb_codes[:], wb_words.rearrange("a p n i -> p a (n i)").bitcast(I32))
+        wa_codes = keep.tile([P, PASSES, 2 * N], U8, name="wa_codes", align_bytes=64)
+        nc.sync.dma_start(wa_codes[:].bitcast(I32), wa_words.rearrange("a p c -> p a c").bitcast(I32))
+        wgo_rows = keep.tile([P, P], F32, name="wgo_rows")
+        nc.sync.dma_start(wgo_rows[:], wgo[0 : P * P // J, :].rearrange("r (c p) -> (r c) p", p=P))
+
+        wgo_psum = psum.tile([P, HALF], F32, name="turned")
+        nc.tensor.transpose(wgo_psum[:, 0:P], wgo_rows[:], ident[:])
+        wgo_cols = keep.tile([P, J // P], F32, name="wgo_cols")
+        nc.scalar.copy(wgo_cols[:], wgo_psum[:, 0 : J // P])
+
+        wc_codes = keep.tile([P, PASSES, N], U32, name="wc_codes", align_bytes=64)
+        wc_planes = keep.tile([P, PASSES, N], U8, name="wc_planes", align_bytes=64)
+        wc_bf16 = [keep.tile([P, N, PACK], BF16, name="wc_bf16_%d" % a, align_bytes=64) for a in range(PASSES)]
+        for a in range(PASSES):
+            for c in range(N // WC_COLS):
+                nc.scalar.copy(
+                    wc_bf16[a][:, c * WC_COLS : (c + 1) * WC_COLS, :],
+                    wc_raw[a, c][:].rearrange("p i n -> p n i"),
+                )
+
+        def quantise_wc(a):
+            nc.vector.quantize_mx(
+                out=wc_codes[:, a, :].bitcast(FP8X4),
+                scales=wc_planes[:, a, :],
+                in_=wc_bf16[a][:].rearrange("p n i -> p (n i)"),
+            )
+
+        planes_of = []
+        for i, offsets in enumerate((src_list, dst_list)):
+            picked = keep.tile([P, J], U8, name="picked_scales%d" % i, align_bytes=64)
+            nc.vector.tensor_copy(picked[:], table_scales[:].indirect(offsets[:]))
+            nc.gpsimd.dma_start(moved[i][0 : P - 4, :].bitcast(I32), picked[4:P, :].bitcast(I32))
+            planes_of.append((picked, moved[i]))
+
+        codes_of = {}
+
+        def gather_words(i, h):
+            offsets = (src_list, dst_list)[i]
+            pairs = ring.tile([P, HALF], U32, name="pairs")
+            nc.vector.tensor_copy(
+                pairs[:], table_words[:].bitcast(U32).indirect(offsets[:, h * HALF // 16 : (h + 1) * HALF // 16])
+            )
+            return pairs
+
+        def part_words(i, h, pairs):
+            codes = keep.tile([P, PASSES, 2 * HALF], U8, name="codes%d%d" % (i, h), align_bytes=64)
+            nc.vector.tensor_copy(
+                codes[:].bitcast(U16), pairs[:].bitcast(U16).rearrange("p (j d) -> p d j", d=PASSES)
+            )
+            codes_of[i, h] = codes
+
+        def gather_half(h):
+            src_pairs = gather_words(0, h)
+            dst_pairs = gather_words(1, h)
+            part_words(0, h, src_pairs)
+            part_words(1, h, dst_pairs)
+
+        weighted = {}
+
+        def messages(h):
+            banks = [psum_ms.tile([P, N], F32, name="ms_bank") for b in range(BLOCKS)]
+            for a in range(PASSES):
+                for b in range(BLOCKS):
+                    j0 = h * HALF + b * P
+                    nc.tensor.matmul_mx(
+                        out=banks[b][:],
+                        lhsT=codes_of[0, h][:, a, 2 * b * P : 2 * (b + 1) * P].bitcast(FP4X4),
+                        lhsT_scale=planes_of[0][a][:, j0 : j0 + P],
+                        rhs=wc_codes[:, a, :].bitcast(FP8X4),
+                        rhs_scale=wc_planes[:, a, :],
+                        start=(a == 0),
+                        stop=(a == PASSES - 1),
+                    )
+            for b in range(BLOCKS):
+                c = h * BLOCKS + b
+                rows = keep.tile([P, N], F32, name="weighted%d" % c)
+                nc.scalar.activation(rows[:], banks[b][:], ACT.Copy, scale=wgo_cols[:, c : c + 1])
+                weighted[h, b] = rows
+
+        def gate(t, h):
+            cols = slice(h * HALF, (h + 1) * HALF)
+            rows = slice(t * P, (t + 1) * P)
+            za = psum.tile([P, HALF], F32, name="za")
+            for a in range(PASSES):
+                nc.tensor.matmul_mx(
+                    out=za[:],
+                    lhsT=wb_codes[:, a, rows].bitcast(FP8X4),
+                    lhsT_scale=wb_planes[:, a, rows],
+                    rhs=codes_of[0, h][:, a, :].bitcast(FP4X4),
+                    rhs_scale=planes_of[0][a][:, cols],
+                    start=(a == 0),
+                    stop=False,
+                )
+                nc.tensor.matmul_mx(
+                    out=za[:],
+                    lhsT=wa_codes[:, a, 2 * t * P : 2 * (t + 1) * P].bitcast(FP4X4),
+                    lhsT_scale=wa_planes[:, a, rows],
+                    rhs=codes_of[1, h][:, a, :].bitcast(FP4X4),
+                    rhs_scale=planes_of[1][a][:, cols],
+                    start=False,
+                    stop=(a == PASSES - 1),
+                )
+            eta = ring.tile([P, HALF], F32, name="eta")
+            nc.scalar.activation(eta[:], za[:], ACT.Sigmoid)
+            return eta
+
+        def turn(t, h):
+            bank = psum.tile([P, HALF], F32, name="turned")
+            for b in range(BLOCKS):
+                nc.tensor.transpose(bank[:, b * P : (b + 1) * P], weighted[h, b][:, t * P : (t + 1) * P], ident[:])
+            message = ring.tile([P, HALF], F32, name="message")
+            nc.scalar.copy(message[:], bank[:])
+            return message
+
+        def place(t, h, eta, message):
+            window = windows[t % 2]
+            nc.vector.tensor_tensor(
+                window[:].indirect(dst_list[:, h * HALF // 16 : (h + 1) * HALF // 16]), eta[:], message[:], MULT
+            )
+            if h == HALVES - 1:
+                nc.sync.dma_start(out[t * P : (t + 1) * P, :], window[:])
+
+        quantise_wc(0)
+        gather_half(0)
+        quantise_wc(1)
+        gather_half(1)
+        first_eta = gate(0, 0)
+        messages(0)
+        first_message = turn(0, 0)
+        messages(1)
+        place(0, 0, first_eta, first_message)
+        for u in range(1, N_TILES * HALVES):
+            t, h = divmod(u, HALVES)
+            eta = gate(t, h)
+            message = turn(t, h)
+            place(t, h, eta, message)

@@ -37,14 +37,21 @@ def tile_list_rgg_none_kernel(
         keep = ctx.enter_context(tc.tile_pool(name="keep", bufs=1))
         ring = ctx.enter_context(tc.tile_pool(name="ring", bufs=3))
         psum = ctx.enter_context(tc.psum_pool(name="psum", bufs=2))
-        psum_ms = ctx.enter_context(tc.psum_pool(name="psum_ms", bufs=4))
+        psum_mx = ctx.enter_context(tc.psum_pool(name="psum_mx", bufs=2))
+        stage = ctx.enter_context(tc.tile_pool(name="stage", bufs=2))
 
         src_list = lists.tile([P, J // 16], U16, name="src_list")
         dst_list = lists.tile([P, J // 16], U16, name="dst_list")
         nc.sync.dma_start(src_list[:], offs)
         nc.sync.dma_start(dst_list[:], offs2)
 
-        table_scales = keep.tile([P, T], U8, name="table_scales", align_bytes=64)
+        shared = ctx.enter_context(tc.tile_pool(name="shared", bufs=1))
+        table_words = shared.tile([P, T], I32, name="table_words", offset=8192, align_bytes=64)
+        nc.sync.dma_start(table_words[:], tab_words[0].rearrange("p t b -> p (t b)").bitcast(I32))
+        wgo_rows = keep.tile([P, P], F32, name="wgo_rows")
+        nc.sync.dma_start(wgo_rows[:], wgo[0 : P * P // J, :].rearrange("r (c p) -> (r c) p", p=P))
+
+        table_scales = shared.tile([P, T], U8, name="table_scales", offset=5120, align_bytes=64)
         nc.vector.memset(table_scales[:].bitcast(I32), 0)
         for q in range(4):
             nc.sync.dma_start(
@@ -55,19 +62,22 @@ def tile_list_rgg_none_kernel(
         wa_planes = keep.tile([P, PASSES, N], U8, name="wa_planes", align_bytes=64)
         wb_planes = keep.tile([P, PASSES, N], U8, name="wb_planes", align_bytes=64)
         moved = [keep.tile([P, J], U8, name="moved%d" % i, align_bytes=64) for i in range(2)]
-        warm_in = keep.tile([P, 1], F32, name="warm_in")
-        warm_out = keep.tile([P, 1], F32, name="warm_out")
-        nc.gpsimd.memset(warm_in[:], 0.0)
-        nc.scalar.activation(warm_out[:], warm_in[:], ACT.Sigmoid)
+        warm_tile = keep.tile([P, 16], F32, name="warm_tile")
+        nc.gpsimd.memset(warm_tile[:, 0:1], 0.0)
+        nc.scalar.activation(warm_tile[:, 8:9], warm_tile[:, 0:1], ACT.Sigmoid)
         ident = keep.tile([P, P], F32, name="ident")
         make_identity(nc, ident[:])
-        for planes, scales in ((wb_planes, wb_scales), (wa_planes, wa_scales)):
-            nc.gpsimd.memset(planes[:].bitcast(I32), 0)
+
+        def load_planes(queue, planes, scales):
             for q in range(4):
-                nc.gpsimd.dma_start(
+                queue.dma_start(
                     planes[32 * q : 32 * q + 4, :, :].bitcast(I32),
                     scales[:, 4 * q : 4 * q + 4, :].rearrange("a r n -> r a n").bitcast(I32),
                 )
+
+        nc.gpsimd.memset(wa_planes[:].bitcast(I32), 0)
+        nc.gpsimd.memset(wb_planes[:].bitcast(I32), 0)
+        load_planes(nc.gpsimd, wa_planes, wa_scales)
         for plane in moved:
             nc.vector.memset(plane[:].bitcast(I32), 0)
 
@@ -78,7 +88,7 @@ def tile_list_rgg_none_kernel(
         wc_raw = {}
 
         def load_wc(a, c):
-            raw = keep.tile([P, PACK, WC_COLS], F32, name="wc_raw%d%d" % (a, c))
+            raw = stage.tile([P, PACK, WC_COLS], F32, name="wc_raw")
             nc.sync.dma_start(
                 raw[:],
                 wc[a * K_PASS : (a + 1) * K_PASS, c * WC_COLS : (c + 1) * WC_COLS].rearrange(
@@ -87,53 +97,60 @@ def tile_list_rgg_none_kernel(
             )
             wc_raw[a, c] = raw
 
-        table_words = keep.tile([P, T], I32, name="table_words", align_bytes=64)
         load_wc(0, 0)
-        load_wc(0, 1)
-        nc.sync.dma_start(table_words[:], tab_words[0].rearrange("p t b -> p (t b)").bitcast(I32))
         load_wc(1, 0)
-        load_wc(1, 1)
         wb_codes = keep.tile([P, PASSES, N], I32, name="wb_codes", align_bytes=64)
         nc.sync.dma_start(wb_codes[:], wb_words.rearrange("a p n i -> p a (n i)").bitcast(I32))
         wa_codes = keep.tile([P, PASSES, 2 * N], U8, name="wa_codes", align_bytes=64)
         nc.sync.dma_start(wa_codes[:].bitcast(I32), wa_words.rearrange("a p c -> p a c").bitcast(I32))
-        wgo_rows = keep.tile([P, P], F32, name="wgo_rows")
-        nc.sync.dma_start(wgo_rows[:], wgo[0 : P * P // J, :].rearrange("r (c p) -> (r c) p", p=P))
+        load_planes(nc.sync, wb_planes, wb_scales)
 
         wgo_psum = psum.tile([P, HALF], F32, name="turned")
         nc.tensor.transpose(wgo_psum[:, 0:P], wgo_rows[:], ident[:])
         wgo_cols = keep.tile([P, J // P], F32, name="wgo_cols")
         nc.scalar.copy(wgo_cols[:], wgo_psum[:, 0 : J // P])
 
-        wc_codes = keep.tile([P, PASSES, N], U32, name="wc_codes", align_bytes=64)
-        wc_planes = keep.tile([P, PASSES, N], U8, name="wc_planes", align_bytes=64)
-        wc_bf16 = [keep.tile([P, N, PACK], BF16, name="wc_bf16_%d" % a, align_bytes=64) for a in range(PASSES)]
-        for a in range(PASSES):
-            for c in range(N // WC_COLS):
-                nc.scalar.copy(
-                    wc_bf16[a][:, c * WC_COLS : (c + 1) * WC_COLS, :],
-                    wc_raw[a, c][:].rearrange("p i n -> p n i"),
-                )
+        wc_codes = {}
+        wc_planes = {}
 
-        def quantise_wc(a):
+        def cast_wc(c, grouped):
+            for a in range(PASSES):
+                nc.scalar.copy(
+                    grouped[:, a, :, :].rearrange("p (g m) i -> p g i m", m=4),
+                    wc_raw[a, c][:].rearrange("p i (g m) -> p g i m", m=4),
+                )
+            return grouped
+
+        def quantise_wc(c, grouped):
+            wc_codes[c] = keep.tile([P, PASSES, WC_COLS], U32, name="wc_codes%d" % c, align_bytes=64)
+            wc_planes[c] = keep.tile([P, PASSES, WC_COLS], U8, name="wc_planes%d" % c, align_bytes=64)
             nc.vector.quantize_mx(
-                out=wc_codes[:, a, :].bitcast(FP8X4),
-                scales=wc_planes[:, a, :],
-                in_=wc_bf16[a][:].rearrange("p n i -> p (n i)"),
+                out=wc_codes[c][:].rearrange("p a n -> p (a n)").bitcast(FP8X4),
+                scales=wc_planes[c][:].rearrange("p a n -> p (a n)"),
+                in_=grouped[:].rearrange("p a n i -> p (a n i)"),
             )
 
-        planes_of = []
-        for i, offsets in enumerate((src_list, dst_list)):
+        early = cast_wc(0, shared.tile([P, PASSES, WC_COLS, PACK], BF16, name="wc_early", offset=1024, align_bytes=64))
+        load_wc(0, 1)
+        load_wc(1, 1)
+        later = cast_wc(1, keep.tile([P, PASSES, WC_COLS, PACK], BF16, name="wc_later", align_bytes=64))
+
+        planes_of = {}
+
+        def gather_scales(i):
+            offsets = (src_list, dst_list)[i]
             picked = keep.tile([P, J], U8, name="picked_scales%d" % i, align_bytes=64)
             nc.vector.tensor_copy(picked[:], table_scales[:].indirect(offsets[:]))
-            nc.gpsimd.dma_start(moved[i][0 : P - 4, :].bitcast(I32), picked[4:P, :].bitcast(I32))
-            planes_of.append((picked, moved[i]))
+            for q in range(4):
+                nc.sync.dma_start(
+                    moved[i][32 * q : 32 * q + 4, :].bitcast(I32), picked[32 * q + 4 : 32 * q + 8, :].bitcast(I32)
+                )
+            planes_of[i] = (picked, moved[i])
 
         codes_of = {}
 
-        def gather_words(i, h):
+        def gather_words(i, h, pairs):
             offsets = (src_list, dst_list)[i]
-            pairs = ring.tile([P, HALF], U32, name="pairs")
             nc.vector.tensor_copy(
                 pairs[:], table_words[:].bitcast(U32).indirect(offsets[:, h * HALF // 16 : (h + 1) * HALF // 16])
             )
@@ -146,48 +163,42 @@ def tile_list_rgg_none_kernel(
             )
             codes_of[i, h] = codes
 
-        def gather_half(h):
-            src_pairs = gather_words(0, h)
-            dst_pairs = gather_words(1, h)
-            part_words(0, h, src_pairs)
-            part_words(1, h, dst_pairs)
-
-        weighted = {}
-
-        def messages(h):
-            banks = [psum_ms.tile([P, N], F32, name="ms_bank") for b in range(BLOCKS)]
-            for a in range(PASSES):
-                for b in range(BLOCKS):
-                    j0 = h * HALF + b * P
+        def messages(t, h):
+            c, n0 = divmod(t * P, WC_COLS)
+            bank = psum_mx.tile([P, BLOCKS, P], F32, name="ms_bank")
+            for b in range(BLOCKS):
+                j0 = h * HALF + b * P
+                for a in (1, 0):
                     nc.tensor.matmul_mx(
-                        out=banks[b][:],
+                        out=bank[:, b, :],
                         lhsT=codes_of[0, h][:, a, 2 * b * P : 2 * (b + 1) * P].bitcast(FP4X4),
                         lhsT_scale=planes_of[0][a][:, j0 : j0 + P],
-                        rhs=wc_codes[:, a, :].bitcast(FP8X4),
-                        rhs_scale=wc_planes[:, a, :],
-                        start=(a == 0),
-                        stop=(a == PASSES - 1),
+                        rhs=wc_codes[c][:, a, n0 : n0 + P].bitcast(FP8X4),
+                        rhs_scale=wc_planes[c][:, a, n0 : n0 + P],
+                        start=(a == 1),
+                        stop=(a == 0),
                     )
+            weighted = ring.tile([P, BLOCKS, P], F32, name="weighted")
             for b in range(BLOCKS):
-                c = h * BLOCKS + b
-                rows = keep.tile([P, N], F32, name="weighted%d" % c)
-                nc.scalar.activation(rows[:], banks[b][:], ACT.Copy, scale=wgo_cols[:, c : c + 1])
-                weighted[h, b] = rows
+                col = h * BLOCKS + b
+                nc.scalar.activation(weighted[:, b, :], bank[:, b, :], ACT.Copy, scale=wgo_cols[:, col : col + 1])
+            return weighted
 
         def gate(t, h):
             cols = slice(h * HALF, (h + 1) * HALF)
             rows = slice(t * P, (t + 1) * P)
-            za = psum.tile([P, HALF], F32, name="za")
-            for a in range(PASSES):
+            za = psum_mx.tile([P, HALF], F32, name="za")
+            for a in (1, 0):
                 nc.tensor.matmul_mx(
                     out=za[:],
                     lhsT=wb_codes[:, a, rows].bitcast(FP8X4),
                     lhsT_scale=wb_planes[:, a, rows],
                     rhs=codes_of[0, h][:, a, :].bitcast(FP4X4),
                     rhs_scale=planes_of[0][a][:, cols],
-                    start=(a == 0),
+                    start=(a == 1),
                     stop=False,
                 )
+            for a in range(PASSES):
                 nc.tensor.matmul_mx(
                     out=za[:],
                     lhsT=wa_codes[:, a, 2 * t * P : 2 * (t + 1) * P].bitcast(FP4X4),
@@ -201,33 +212,38 @@ def tile_list_rgg_none_kernel(
             nc.scalar.activation(eta[:], za[:], ACT.Sigmoid)
             return eta
 
-        def turn(t, h):
+        def turn(weighted):
             bank = psum.tile([P, HALF], F32, name="turned")
             for b in range(BLOCKS):
-                nc.tensor.transpose(bank[:, b * P : (b + 1) * P], weighted[h, b][:, t * P : (t + 1) * P], ident[:])
+                nc.tensor.transpose(bank[:, b * P : (b + 1) * P], weighted[:, b, :], ident[:])
             message = ring.tile([P, HALF], F32, name="message")
             nc.scalar.copy(message[:], bank[:])
             return message
 
         def place(t, h, eta, message):
-            window = windows[t % 2]
+            window = windows[t % 3]
             nc.vector.tensor_tensor(
                 window[:].indirect(dst_list[:, h * HALF // 16 : (h + 1) * HALF // 16]), eta[:], message[:], MULT
             )
             if h == HALVES - 1:
                 nc.sync.dma_start(out[t * P : (t + 1) * P, :], window[:])
 
-        quantise_wc(0)
-        gather_half(0)
-        quantise_wc(1)
-        gather_half(1)
-        first_eta = gate(0, 0)
-        messages(0)
-        first_message = turn(0, 0)
-        messages(1)
-        place(0, 0, first_eta, first_message)
-        for u in range(1, N_TILES * HALVES):
-            t, h = divmod(u, HALVES)
+        first = gather_words(0, 0, keep.tile([P, HALF], U32, name="pairs_first"))
+        gather_scales(0)
+        gather_scales(1)
+        part_words(0, 0, first)
+        quantise_wc(0, early)
+        low = gather_words(1, 0, shared.tile([P, HALF], U32, name="pairs_low", offset=4096, align_bytes=64))
+        high = gather_words(0, 1, shared.tile([P, HALF], U32, name="pairs_high", offset=0, align_bytes=64))
+        part_words(1, 0, low)
+        last = gather_words(1, 1, shared.tile([P, HALF], U32, name="pairs_last", offset=2048, align_bytes=64))
+        part_words(0, 1, high)
+        quantise_wc(1, later)
+        part_words(1, 1, last)
+        third = shared.tile([P, T], F32, name="window2", offset=8192, align_bytes=64)
+        nc.gpsimd.memset(third[:], 0.0)
+        windows.append(third)
+        for t, h in ((0, 0), (1, 0), (0, 1), (1, 1), (2, 0), (2, 1), (3, 0), (3, 1)):
+            weighted = messages(t, h)
             eta = gate(t, h)
-            message = turn(t, h)
-            place(t, h, eta, message)
+            place(t, h, eta, turn(weighted))

@@ -59,9 +59,11 @@ def tile_list_rgg_none_kernel(
                 tab_scales[:, 4 * q : 4 * q + 4, :].bitcast(I32),
             )
 
-        wa_planes = keep.tile([P, PASSES, N], U8, name="wa_planes", align_bytes=64)
-        wb_planes = keep.tile([P, PASSES, N], U8, name="wb_planes", align_bytes=64)
-        moved = [keep.tile([P, J], U8, name="moved%d" % i, align_bytes=64) for i in range(2)]
+        loaded_planes = keep.tile([P, 4, J], U8, name="loaded_planes", align_bytes=64)
+        nc.vector.memset(loaded_planes[:].bitcast(I32), 0)
+        wa_planes = loaded_planes[:, 0, :].rearrange("p (a n) -> p a n", a=PASSES)
+        wb_planes = loaded_planes[:, 1, :].rearrange("p (a n) -> p a n", a=PASSES)
+        moved = [loaded_planes[:, 2 + i, :] for i in range(2)]
         warm_tile = keep.tile([P, 16], F32, name="warm_tile")
         nc.gpsimd.memset(warm_tile[:, 0:1], 0.0)
         nc.scalar.activation(warm_tile[:, 8:9], warm_tile[:, 0:1], ACT.Sigmoid)
@@ -75,15 +77,9 @@ def tile_list_rgg_none_kernel(
                     scales[:, 4 * q : 4 * q + 4, :].rearrange("a r n -> r a n").bitcast(I32),
                 )
 
-        nc.gpsimd.memset(wa_planes[:].bitcast(I32), 0)
-        nc.gpsimd.memset(wb_planes[:].bitcast(I32), 0)
-        load_planes(nc.gpsimd, wa_planes, wa_scales)
-        for plane in moved:
-            nc.vector.memset(plane[:].bitcast(I32), 0)
-
         windows = [keep.tile([P, T], F32, name="window%d" % i) for i in range(2)]
         for window in windows:
-            nc.vector.memset(window[:], 0.0)
+            nc.vector.memset(window[:].bitcast(I32), 0)
 
         wc_raw = {}
 
@@ -104,6 +100,7 @@ def tile_list_rgg_none_kernel(
         wa_codes = keep.tile([P, PASSES, 2 * N], U8, name="wa_codes", align_bytes=64)
         nc.sync.dma_start(wa_codes[:].bitcast(I32), wa_words.rearrange("a p c -> p a c").bitcast(I32))
         load_planes(nc.sync, wb_planes, wb_scales)
+        load_planes(nc.sync, wa_planes, wa_scales)
 
         wgo_psum = psum.tile([P, HALF], F32, name="turned")
         nc.tensor.transpose(wgo_psum[:, 0:P], wgo_rows[:], ident[:])
@@ -184,7 +181,7 @@ def tile_list_rgg_none_kernel(
                 nc.scalar.activation(weighted[:, b, :], bank[:, b, :], ACT.Copy, scale=wgo_cols[:, col : col + 1])
             return weighted
 
-        def gate(t, h):
+        def gate(t, h, eta):
             cols = slice(h * HALF, (h + 1) * HALF)
             rows = slice(t * P, (t + 1) * P)
             za = psum_mx.tile([P, HALF], F32, name="za")
@@ -208,25 +205,18 @@ def tile_list_rgg_none_kernel(
                     start=False,
                     stop=(a == PASSES - 1),
                 )
-            eta = ring.tile([P, HALF], F32, name="eta")
-            nc.scalar.activation(eta[:], za[:], ACT.Sigmoid)
-            return eta
+            nc.scalar.activation(eta[:, cols], za[:], ACT.Sigmoid)
 
-        def turn(weighted):
+        def turn(h, weighted, message):
             bank = psum.tile([P, HALF], F32, name="turned")
             for b in range(BLOCKS):
                 nc.tensor.transpose(bank[:, b * P : (b + 1) * P], weighted[:, b, :], ident[:])
-            message = ring.tile([P, HALF], F32, name="message")
-            nc.scalar.copy(message[:], bank[:])
-            return message
+            nc.scalar.copy(message[:, h * HALF : (h + 1) * HALF], bank[:])
 
-        def place(t, h, eta, message):
-            window = windows[t % 3]
+        def place(window, j0, j1, eta, message):
             nc.vector.tensor_tensor(
-                window[:].indirect(dst_list[:, h * HALF // 16 : (h + 1) * HALF // 16]), eta[:], message[:], MULT
+                window[:].indirect(dst_list[:, j0 // 16 : j1 // 16]), eta[:, j0:j1], message[:, j0:j1], MULT
             )
-            if h == HALVES - 1:
-                nc.sync.dma_start(out[t * P : (t + 1) * P, :], window[:])
 
         first = gather_words(0, 0, keep.tile([P, HALF], U32, name="pairs_first"))
         gather_scales(0)
@@ -236,14 +226,20 @@ def tile_list_rgg_none_kernel(
         low = gather_words(1, 0, shared.tile([P, HALF], U32, name="pairs_low", offset=4096, align_bytes=64))
         high = gather_words(0, 1, shared.tile([P, HALF], U32, name="pairs_high", offset=0, align_bytes=64))
         part_words(1, 0, low)
-        last = gather_words(1, 1, shared.tile([P, HALF], U32, name="pairs_last", offset=2048, align_bytes=64))
         part_words(0, 1, high)
+        last = gather_words(1, 1, shared.tile([P, HALF], U32, name="pairs_last", offset=2048, align_bytes=64))
         quantise_wc(1, later)
         part_words(1, 1, last)
-        third = shared.tile([P, T], F32, name="window2", offset=8192, align_bytes=64)
-        nc.gpsimd.memset(third[:], 0.0)
-        windows.append(third)
-        for t, h in ((0, 0), (1, 0), (0, 1), (1, 1), (2, 0), (2, 1), (3, 0), (3, 1)):
-            weighted = messages(t, h)
-            eta = gate(t, h)
-            place(t, h, eta, turn(weighted))
+        for t in range(N_TILES):
+            window = windows[t % 2]
+            eta = stage.tile([P, J], F32, name="eta")
+            message = stage.tile([P, J], F32, name="message")
+            for h in range(HALVES):
+                weighted = messages(t, h)
+                gate(t, h, eta)
+                turn(h, weighted, message)
+                if t == 0:
+                    place(window, h * HALF, (h + 1) * HALF, eta, message)
+            if t > 0:
+                place(window, 0, J, eta, message)
+            nc.sync.dma_start(out[t * P : (t + 1) * P, :], window[:])

@@ -60,7 +60,6 @@ def tile_list_rgg_none_kernel(
             )
 
         loaded_planes = keep.tile([P, 4, J], U8, name="loaded_planes", align_bytes=64)
-        nc.vector.memset(loaded_planes[:].bitcast(I32), 0)
         wa_planes = loaded_planes[:, 0, :].rearrange("p (a n) -> p a n", a=PASSES)
         wb_planes = loaded_planes[:, 1, :].rearrange("p (a n) -> p a n", a=PASSES)
         moved = [loaded_planes[:, 2 + i, :] for i in range(2)]
@@ -78,29 +77,21 @@ def tile_list_rgg_none_kernel(
                 )
 
         windows = [keep.tile([P, T], F32, name="window%d" % i) for i in range(2)]
-        for window in windows:
-            nc.vector.memset(window[:].bitcast(I32), 0)
+        nc.vector.memset(windows[0][:].bitcast(I32), 0)
+        nc.vector.memset(loaded_planes[:].bitcast(I32), 0)
+        nc.vector.memset(windows[1][:].bitcast(I32), 0)
+        load_planes(nc.gpsimd, wb_planes, wb_scales)
+        load_planes(nc.gpsimd, wa_planes, wa_scales)
 
-        wc_raw = {}
-
-        def load_wc(a, c):
-            raw = stage.tile([P, PACK, WC_COLS], F32, name="wc_raw")
+        wc_raw = [keep.tile([P, PACK, N], F32, name="wc_raw%d" % a) for a in range(PASSES)]
+        for a in range(PASSES):
             nc.sync.dma_start(
-                raw[:],
-                wc[a * K_PASS : (a + 1) * K_PASS, c * WC_COLS : (c + 1) * WC_COLS].rearrange(
-                    "(p i) n -> p i n", i=PACK
-                ),
+                wc_raw[a][:], wc[a * K_PASS : (a + 1) * K_PASS, :].rearrange("(p i) n -> p i n", i=PACK)
             )
-            wc_raw[a, c] = raw
-
-        load_wc(0, 0)
-        load_wc(1, 0)
         wb_codes = keep.tile([P, PASSES, N], I32, name="wb_codes", align_bytes=64)
         nc.sync.dma_start(wb_codes[:], wb_words.rearrange("a p n i -> p a (n i)").bitcast(I32))
         wa_codes = keep.tile([P, PASSES, 2 * N], U8, name="wa_codes", align_bytes=64)
         nc.sync.dma_start(wa_codes[:].bitcast(I32), wa_words.rearrange("a p c -> p a c").bitcast(I32))
-        load_planes(nc.sync, wb_planes, wb_scales)
-        load_planes(nc.sync, wa_planes, wa_scales)
 
         wgo_psum = psum.tile([P, HALF], F32, name="turned")
         nc.tensor.transpose(wgo_psum[:, 0:P], wgo_rows[:], ident[:])
@@ -114,7 +105,7 @@ def tile_list_rgg_none_kernel(
             for a in range(PASSES):
                 nc.scalar.copy(
                     grouped[:, a, :, :].rearrange("p (g m) i -> p g i m", m=4),
-                    wc_raw[a, c][:].rearrange("p i (g m) -> p g i m", m=4),
+                    wc_raw[a][:, :, c * WC_COLS : (c + 1) * WC_COLS].rearrange("p i (g m) -> p g i m", m=4),
                 )
             return grouped
 
@@ -128,8 +119,6 @@ def tile_list_rgg_none_kernel(
             )
 
         early = cast_wc(0, shared.tile([P, PASSES, WC_COLS, PACK], BF16, name="wc_early", offset=1024, align_bytes=64))
-        load_wc(0, 1)
-        load_wc(1, 1)
         later = cast_wc(1, keep.tile([P, PASSES, WC_COLS, PACK], BF16, name="wc_later", align_bytes=64))
 
         planes_of = {}
@@ -138,9 +127,9 @@ def tile_list_rgg_none_kernel(
             offsets = (src_list, dst_list)[i]
             picked = keep.tile([P, J], U8, name="picked_scales%d" % i, align_bytes=64)
             nc.vector.tensor_copy(picked[:], table_scales[:].indirect(offsets[:]))
-            for q in range(4):
+            for p0, count in ((0, 64), (64, 32), (96, 4)):
                 nc.sync.dma_start(
-                    moved[i][32 * q : 32 * q + 4, :].bitcast(I32), picked[32 * q + 4 : 32 * q + 8, :].bitcast(I32)
+                    moved[i][p0 : p0 + count, :].bitcast(I32), picked[p0 + 4 : p0 + 4 + count, :].bitcast(I32)
                 )
             planes_of[i] = (picked, moved[i])
 

@@ -25,7 +25,8 @@ HALF = 512
 HALVES = J // HALF
 N_TILES = N // P
 BLOCKS = HALF // P
-WC_COLS = 256
+WC_CHUNKS = ((0, 1), (1, 2), (2, 4))
+SHIFT = 16
 
 
 def tile_list_rgg_none_kernel(
@@ -39,59 +40,66 @@ def tile_list_rgg_none_kernel(
         psum = ctx.enter_context(tc.psum_pool(name="psum", bufs=2))
         psum_mx = ctx.enter_context(tc.psum_pool(name="psum_mx", bufs=2))
         stage = ctx.enter_context(tc.tile_pool(name="stage", bufs=2))
+        shared = ctx.enter_context(tc.tile_pool(name="shared", bufs=1))
 
         src_list = lists.tile([P, J // 16], U16, name="src_list")
         dst_list = lists.tile([P, J // 16], U16, name="dst_list")
-        nc.sync.dma_start(src_list[:], offs)
-        nc.sync.dma_start(dst_list[:], offs2)
-
-        shared = ctx.enter_context(tc.tile_pool(name="shared", bufs=1))
-        table_words = shared.tile([P, T], I32, name="table_words", offset=8192, align_bytes=64)
-        nc.sync.dma_start(table_words[:], tab_words[0].rearrange("p t b -> p (t b)").bitcast(I32))
-        wgo_rows = keep.tile([P, P], F32, name="wgo_rows")
-        nc.sync.dma_start(wgo_rows[:], wgo[0 : P * P // J, :].rearrange("r (c p) -> (r c) p", p=P))
-
-        table_scales = shared.tile([P, T], U8, name="table_scales", offset=5120, align_bytes=64)
-        nc.vector.memset(table_scales[:].bitcast(I32), 0)
-        for q in range(4):
-            nc.sync.dma_start(
-                table_scales[32 * q : 32 * q + 8, :].bitcast(I32),
-                tab_scales[:, 4 * q : 4 * q + 4, :].bitcast(I32),
-            )
-
+        table_scales = keep.tile([P, T], U8, name="table_scales", align_bytes=64)
         loaded_planes = keep.tile([P, 4, J], U8, name="loaded_planes", align_bytes=64)
         wa_planes = loaded_planes[:, 0, :].rearrange("p (a n) -> p a n", a=PASSES)
         wb_planes = loaded_planes[:, 1, :].rearrange("p (a n) -> p a n", a=PASSES)
         moved = [loaded_planes[:, 2 + i, :] for i in range(2)]
+        windows = [keep.tile([P, T], F32, name="window%d" % i) for i in range(2)]
+        nc.vector.memset(table_scales[:].bitcast(I32), 0)
+        nc.vector.memset(loaded_planes[:].bitcast(I32), 0)
+        nc.vector.memset(windows[0][:].bitcast(I32), 0)
+        nc.vector.memset(windows[1][:].bitcast(I32), 0)
+
         warm_tile = keep.tile([P, 16], F32, name="warm_tile")
         nc.gpsimd.memset(warm_tile[:, 0:1], 0.0)
         nc.scalar.activation(warm_tile[:, 8:9], warm_tile[:, 0:1], ACT.Sigmoid)
+        wgo_rows = keep.tile([P, P], F32, name="wgo_rows")
+        nc.gpsimd.memset(wgo_rows[:], 0.0)
         ident = keep.tile([P, P], F32, name="ident")
         make_identity(nc, ident[:])
+        nc.gpsimd.dma_start(wgo_rows[0 : J // P, :], wgo[0, :].rearrange("(c p) -> c p", p=P))
 
-        def load_planes(queue, planes, scales):
+        wc_raw = {}
+
+        def load_wc(c, a):
+            t0, t1 = WC_CHUNKS[c]
+            raw = keep.tile([P, PACK, (t1 - t0) * P], F32, name="wc_raw%d%d" % (c, a))
+            nc.sync.dma_start(
+                raw[:], wc[a * K_PASS : (a + 1) * K_PASS, t0 * P : t1 * P].rearrange("(p i) n -> p i n", i=PACK)
+            )
+            for t in range(t0, t1):
+                wc_raw[t, a] = raw[:, :, (t - t0) * P : (t - t0 + 1) * P]
+
+        def load_planes(planes, scales):
             for q in range(4):
-                queue.dma_start(
+                nc.sync.dma_start(
                     planes[32 * q : 32 * q + 4, :, :].bitcast(I32),
                     scales[:, 4 * q : 4 * q + 4, :].rearrange("a r n -> r a n").bitcast(I32),
                 )
 
-        windows = [keep.tile([P, T], F32, name="window%d" % i) for i in range(2)]
-        nc.vector.memset(windows[0][:].bitcast(I32), 0)
-        nc.vector.memset(loaded_planes[:].bitcast(I32), 0)
-        nc.vector.memset(windows[1][:].bitcast(I32), 0)
-        load_planes(nc.gpsimd, wb_planes, wb_scales)
-        load_planes(nc.gpsimd, wa_planes, wa_scales)
-
-        wc_raw = [keep.tile([P, PACK, N], F32, name="wc_raw%d" % a) for a in range(PASSES)]
-        for a in range(PASSES):
-            nc.sync.dma_start(
-                wc_raw[a][:], wc[a * K_PASS : (a + 1) * K_PASS, :].rearrange("(p i) n -> p i n", i=PACK)
-            )
+        nc.sync.dma_start(src_list[:], offs)
+        nc.sync.dma_start(dst_list[:], offs2)
+        load_wc(0, 0)
+        by_row = tab_scales.rearrange("a (q r) t -> r q a t", r=4)
+        for r in range(4):
+            nc.sync.dma_start(table_scales[r:P:SHIFT, :].bitcast(I32), by_row[r].bitcast(I32))
+        table_words = keep.tile([P, T], I32, name="table_words", align_bytes=64)
+        nc.sync.dma_start(table_words[:], tab_words[0].rearrange("p t b -> p (t b)").bitcast(I32))
+        load_wc(0, 1)
+        load_planes(wb_planes, wb_scales)
         wb_codes = keep.tile([P, PASSES, N], I32, name="wb_codes", align_bytes=64)
         nc.sync.dma_start(wb_codes[:], wb_words.rearrange("a p n i -> p a (n i)").bitcast(I32))
         wa_codes = keep.tile([P, PASSES, 2 * N], U8, name="wa_codes", align_bytes=64)
         nc.sync.dma_start(wa_codes[:].bitcast(I32), wa_words.rearrange("a p c -> p a c").bitcast(I32))
+        load_planes(wa_planes, wa_scales)
+        for c in range(1, len(WC_CHUNKS)):
+            for a in range(PASSES):
+                load_wc(c, a)
 
         wgo_psum = psum.tile([P, HALF], F32, name="turned")
         nc.tensor.transpose(wgo_psum[:, 0:P], wgo_rows[:], ident[:])
@@ -101,25 +109,25 @@ def tile_list_rgg_none_kernel(
         wc_codes = {}
         wc_planes = {}
 
-        def cast_wc(c, grouped):
+        def cast_wc(t, grouped):
             for a in range(PASSES):
                 nc.scalar.copy(
                     grouped[:, a, :, :].rearrange("p (g m) i -> p g i m", m=4),
-                    wc_raw[a][:, :, c * WC_COLS : (c + 1) * WC_COLS].rearrange("p i (g m) -> p g i m", m=4),
+                    wc_raw[t, a].rearrange("p i (g m) -> p g i m", m=4),
                 )
             return grouped
 
-        def quantise_wc(c, grouped):
-            wc_codes[c] = keep.tile([P, PASSES, WC_COLS], U32, name="wc_codes%d" % c, align_bytes=64)
-            wc_planes[c] = keep.tile([P, PASSES, WC_COLS], U8, name="wc_planes%d" % c, align_bytes=64)
+        def quantise_wc(t, grouped):
+            wc_codes[t] = keep.tile([P, PASSES, P], U32, name="wc_codes%d" % t, align_bytes=64)
+            wc_planes[t] = keep.tile([P, PASSES, P], U8, name="wc_planes%d" % t, align_bytes=64)
             nc.vector.quantize_mx(
-                out=wc_codes[c][:].rearrange("p a n -> p (a n)").bitcast(FP8X4),
-                scales=wc_planes[c][:].rearrange("p a n -> p (a n)"),
+                out=wc_codes[t][:].rearrange("p a n -> p (a n)").bitcast(FP8X4),
+                scales=wc_planes[t][:].rearrange("p a n -> p (a n)"),
                 in_=grouped[:].rearrange("p a n i -> p (a n i)"),
             )
 
-        early = cast_wc(0, shared.tile([P, PASSES, WC_COLS, PACK], BF16, name="wc_early", offset=1024, align_bytes=64))
-        later = cast_wc(1, keep.tile([P, PASSES, WC_COLS, PACK], BF16, name="wc_later", align_bytes=64))
+        def grouped_tile(t):
+            return keep.tile([P, PASSES, P, PACK], BF16, name="wc_grouped%d" % t, align_bytes=64)
 
         planes_of = {}
 
@@ -127,10 +135,7 @@ def tile_list_rgg_none_kernel(
             offsets = (src_list, dst_list)[i]
             picked = keep.tile([P, J], U8, name="picked_scales%d" % i, align_bytes=64)
             nc.vector.tensor_copy(picked[:], table_scales[:].indirect(offsets[:]))
-            for p0, count in ((0, 64), (64, 32), (96, 4)):
-                nc.sync.dma_start(
-                    moved[i][p0 : p0 + count, :].bitcast(I32), picked[p0 + 4 : p0 + 4 + count, :].bitcast(I32)
-                )
+            nc.gpsimd.dma_start(moved[i][0 : P - SHIFT, :].bitcast(I32), picked[SHIFT:P, :].bitcast(I32))
             planes_of[i] = (picked, moved[i])
 
         codes_of = {}
@@ -150,7 +155,6 @@ def tile_list_rgg_none_kernel(
             codes_of[i, h] = codes
 
         def messages(t, h):
-            c, n0 = divmod(t * P, WC_COLS)
             bank = psum_mx.tile([P, BLOCKS, P], F32, name="ms_bank")
             for b in range(BLOCKS):
                 j0 = h * HALF + b * P
@@ -159,8 +163,8 @@ def tile_list_rgg_none_kernel(
                         out=bank[:, b, :],
                         lhsT=codes_of[0, h][:, a, 2 * b * P : 2 * (b + 1) * P].bitcast(FP4X4),
                         lhsT_scale=planes_of[0][a][:, j0 : j0 + P],
-                        rhs=wc_codes[c][:, a, n0 : n0 + P].bitcast(FP8X4),
-                        rhs_scale=wc_planes[c][:, a, n0 : n0 + P],
+                        rhs=wc_codes[t][:, a, :].bitcast(FP8X4),
+                        rhs_scale=wc_planes[t][:, a, :],
                         start=(a == 1),
                         stop=(a == 0),
                     )
@@ -207,28 +211,38 @@ def tile_list_rgg_none_kernel(
                 window[:].indirect(dst_list[:, j0 // 16 : j1 // 16]), eta[:, j0:j1], message[:, j0:j1], MULT
             )
 
-        first = gather_words(0, 0, keep.tile([P, HALF], U32, name="pairs_first"))
+        def unit(t, h, eta, message):
+            weighted = messages(t, h)
+            gate(t, h, eta)
+            turn(h, weighted, message)
+
+        def pairs_at(name, offset):
+            return shared.tile([P, HALF], U32, name=name, offset=offset, align_bytes=64)
+
+        grouped = {0: cast_wc(0, shared.tile([P, PASSES, P, PACK], BF16, name="wc_first", offset=1024, align_bytes=64))}
         gather_scales(0)
         gather_scales(1)
-        part_words(0, 0, first)
-        quantise_wc(0, early)
-        low = gather_words(1, 0, shared.tile([P, HALF], U32, name="pairs_low", offset=4096, align_bytes=64))
-        high = gather_words(0, 1, shared.tile([P, HALF], U32, name="pairs_high", offset=0, align_bytes=64))
-        part_words(1, 0, low)
-        part_words(0, 1, high)
-        last = gather_words(1, 1, shared.tile([P, HALF], U32, name="pairs_last", offset=2048, align_bytes=64))
-        quantise_wc(1, later)
-        part_words(1, 1, last)
+        src_low = gather_words(0, 0, keep.tile([P, HALF], U32, name="src_low"))
+        quantise_wc(0, grouped[0])
+        part_words(0, 0, src_low)
+        dst_low = gather_words(1, 0, pairs_at("dst_low", 0))
+        src_high = gather_words(0, 1, pairs_at("src_high", 2048))
+        part_words(1, 0, dst_low)
+        part_words(0, 1, src_high)
+        dst_high = gather_words(1, 1, pairs_at("dst_high", 0))
+        grouped[1] = cast_wc(1, grouped_tile(1))
+        quantise_wc(1, grouped[1])
+        part_words(1, 1, dst_high)
         for t in range(N_TILES):
             window = windows[t % 2]
             eta = stage.tile([P, J], F32, name="eta")
             message = stage.tile([P, J], F32, name="message")
             for h in range(HALVES):
-                weighted = messages(t, h)
-                gate(t, h, eta)
-                turn(h, weighted, message)
-                if t == 0:
+                unit(t, h, eta, message)
+                if t < 2:
                     place(window, h * HALF, (h + 1) * HALF, eta, message)
-            if t > 0:
+                    if h == 0:
+                        quantise_wc(t + 2, cast_wc(t + 2, grouped_tile(t + 2)))
+            if t >= 2:
                 place(window, 0, J, eta, message)
             nc.sync.dma_start(out[t * P : (t + 1) * P, :], window[:])

@@ -25,8 +25,9 @@ HALF = 512
 HALVES = J // HALF
 N_TILES = N // P
 BLOCKS = HALF // P
-WC_CHUNKS = ((0, 1), (1, 2), (2, 4))
+WC_CHUNKS = ((0, 2), (2, 4))
 SHIFT = 16
+BANK = 2048
 
 
 def tile_list_rgg_none_kernel(
@@ -37,69 +38,74 @@ def tile_list_rgg_none_kernel(
         lists = ctx.enter_context(tc.tile_pool(name="lists", bufs=1))
         keep = ctx.enter_context(tc.tile_pool(name="keep", bufs=1))
         ring = ctx.enter_context(tc.tile_pool(name="ring", bufs=3))
-        psum = ctx.enter_context(tc.psum_pool(name="psum", bufs=2))
-        psum_mx = ctx.enter_context(tc.psum_pool(name="psum_mx", bufs=2))
+        psum = ctx.enter_context(tc.psum_pool(name="psum", bufs=1))
+        psum_mx = ctx.enter_context(tc.psum_pool(name="psum_mx", bufs=1))
         stage = ctx.enter_context(tc.tile_pool(name="stage", bufs=2))
+        turns = ctx.enter_context(tc.tile_pool(name="turns", bufs=1))
         shared = ctx.enter_context(tc.tile_pool(name="shared", bufs=1))
 
         src_list = lists.tile([P, J // 16], U16, name="src_list")
         dst_list = lists.tile([P, J // 16], U16, name="dst_list")
-        table_scales = keep.tile([P, T], U8, name="table_scales", align_bytes=64)
-        loaded_planes = keep.tile([P, 4, J], U8, name="loaded_planes", align_bytes=64)
-        wa_planes = loaded_planes[:, 0, :].rearrange("p (a n) -> p a n", a=PASSES)
-        wb_planes = loaded_planes[:, 1, :].rearrange("p (a n) -> p a n", a=PASSES)
-        moved = [loaded_planes[:, 2 + i, :] for i in range(2)]
+        later = ctx.enter_context(tc.tile_pool(name="later", bufs=1))
+        table_scales = later.tile([P, T], U8, name="table_scales", offset=3072, align_bytes=64)
+        loaded_planes = keep.tile([P, 3, J], U8, name="loaded_planes", align_bytes=64)
+        wa_planes = keep.tile([P, PASSES, N], U8, name="wa_planes", align_bytes=64)
+        wb_planes = loaded_planes[:, 0, :].rearrange("p (a n) -> p a n", a=PASSES)
+        moved = [loaded_planes[:, 1 + i, :] for i in range(2)]
         windows = [keep.tile([P, T], F32, name="window%d" % i) for i in range(2)]
         nc.vector.memset(table_scales[:].bitcast(I32), 0)
         nc.vector.memset(loaded_planes[:].bitcast(I32), 0)
-        nc.vector.memset(windows[0][:].bitcast(I32), 0)
-        nc.vector.memset(windows[1][:].bitcast(I32), 0)
 
         warm_tile = keep.tile([P, 16], F32, name="warm_tile")
         nc.gpsimd.memset(warm_tile[:, 0:1], 0.0)
         nc.scalar.activation(warm_tile[:, 8:9], warm_tile[:, 0:1], ACT.Sigmoid)
+
+        def load_planes(queue, planes, scales):
+            for q in range(4):
+                queue.dma_start(
+                    planes[32 * q : 32 * q + 4, :, :].bitcast(I32),
+                    scales[:, 4 * q : 4 * q + 4, :].rearrange("a r n -> r a n").bitcast(I32),
+                )
+
+        nc.gpsimd.memset(wa_planes[:].bitcast(I32), 0)
+        load_planes(nc.gpsimd, wa_planes, wa_scales)
         wgo_rows = keep.tile([P, P], F32, name="wgo_rows")
         nc.gpsimd.memset(wgo_rows[:], 0.0)
         ident = keep.tile([P, P], F32, name="ident")
         make_identity(nc, ident[:])
         nc.gpsimd.dma_start(wgo_rows[0 : J // P, :], wgo[0, :].rearrange("(c p) -> c p", p=P))
+        nc.gpsimd.memset(windows[0][:], 0.0)
+        nc.gpsimd.memset(windows[1][:], 0.0)
 
         wc_raw = {}
 
         def load_wc(c, a):
             t0, t1 = WC_CHUNKS[c]
-            raw = keep.tile([P, PACK, (t1 - t0) * P], F32, name="wc_raw%d%d" % (c, a))
+            shape = [P, PACK, (t1 - t0) * P]
+            if c == 0:
+                raw = keep.tile(shape, F32, name="wc_first%d" % a)
+            else:
+                raw = later.tile(shape, F32, name="wc_rest%d" % a, offset=4096 * a, align_bytes=64)
             nc.sync.dma_start(
                 raw[:], wc[a * K_PASS : (a + 1) * K_PASS, t0 * P : t1 * P].rearrange("(p i) n -> p i n", i=PACK)
             )
             for t in range(t0, t1):
                 wc_raw[t, a] = raw[:, :, (t - t0) * P : (t - t0 + 1) * P]
 
-        def load_planes(planes, scales):
-            for q in range(4):
-                nc.sync.dma_start(
-                    planes[32 * q : 32 * q + 4, :, :].bitcast(I32),
-                    scales[:, 4 * q : 4 * q + 4, :].rearrange("a r n -> r a n").bitcast(I32),
-                )
-
         nc.sync.dma_start(src_list[:], offs)
         nc.sync.dma_start(dst_list[:], offs2)
-        load_wc(0, 0)
+        wa_codes = keep.tile([P, PASSES, 2 * N], U8, name="wa_codes", align_bytes=64)
+        nc.sync.dma_start(wa_codes[:].bitcast(I32), wa_words.rearrange("a p c -> p a c").bitcast(I32))
         by_row = tab_scales.rearrange("a (q r) t -> r q a t", r=4)
         for r in range(4):
             nc.sync.dma_start(table_scales[r:P:SHIFT, :].bitcast(I32), by_row[r].bitcast(I32))
         table_words = keep.tile([P, T], I32, name="table_words", align_bytes=64)
         nc.sync.dma_start(table_words[:], tab_words[0].rearrange("p t b -> p (t b)").bitcast(I32))
+        load_wc(0, 0)
         load_wc(0, 1)
-        load_planes(wb_planes, wb_scales)
+        load_planes(nc.sync, wb_planes, wb_scales)
         wb_codes = keep.tile([P, PASSES, N], I32, name="wb_codes", align_bytes=64)
         nc.sync.dma_start(wb_codes[:], wb_words.rearrange("a p n i -> p a (n i)").bitcast(I32))
-        wa_codes = keep.tile([P, PASSES, 2 * N], U8, name="wa_codes", align_bytes=64)
-        nc.sync.dma_start(wa_codes[:].bitcast(I32), wa_words.rearrange("a p c -> p a c").bitcast(I32))
-        load_planes(wa_planes, wa_scales)
-        for c in range(1, len(WC_CHUNKS)):
-            for a in range(PASSES):
-                load_wc(c, a)
 
         wgo_psum = psum.tile([P, HALF], F32, name="turned")
         nc.tensor.transpose(wgo_psum[:, 0:P], wgo_rows[:], ident[:])
@@ -127,7 +133,7 @@ def tile_list_rgg_none_kernel(
             )
 
         def grouped_tile(t):
-            return keep.tile([P, PASSES, P, PACK], BF16, name="wc_grouped%d" % t, align_bytes=64)
+            return turns.tile([P, PASSES, P, PACK], BF16, name="wc_grouped%d" % t, offset=2048 * (t - 2), align_bytes=64)
 
         planes_of = {}
 
@@ -135,7 +141,7 @@ def tile_list_rgg_none_kernel(
             offsets = (src_list, dst_list)[i]
             picked = keep.tile([P, J], U8, name="picked_scales%d" % i, align_bytes=64)
             nc.vector.tensor_copy(picked[:], table_scales[:].indirect(offsets[:]))
-            nc.gpsimd.dma_start(moved[i][0 : P - SHIFT, :].bitcast(I32), picked[SHIFT:P, :].bitcast(I32))
+            nc.scalar.dma_start(moved[i][0 : P - SHIFT, :].bitcast(I32), picked[SHIFT:P, :].bitcast(I32))
             planes_of[i] = (picked, moved[i])
 
         codes_of = {}
@@ -154,8 +160,12 @@ def tile_list_rgg_none_kernel(
             )
             codes_of[i, h] = codes
 
+        def next_bank(shape, kind, t, h, step):
+            turn_number = 3 * (t * HALVES + h) + step
+            return psum_mx.tile(shape, F32, name="%s%d%d" % (kind, t, h), offset=BANK * (turn_number % 2))
+
         def messages(t, h):
-            bank = psum_mx.tile([P, BLOCKS, P], F32, name="ms_bank")
+            bank = next_bank([P, BLOCKS, P], "ms", t, h, 0)
             for b in range(BLOCKS):
                 j0 = h * HALF + b * P
                 for a in (1, 0):
@@ -168,7 +178,11 @@ def tile_list_rgg_none_kernel(
                         start=(a == 1),
                         stop=(a == 0),
                     )
-            weighted = ring.tile([P, BLOCKS, P], F32, name="weighted")
+            u = t * HALVES + h
+            if u in (1, 2):
+                weighted = turns.tile([P, BLOCKS, P], F32, name="weighted%d" % u, offset=2048 * (u - 1), align_bytes=64)
+            else:
+                weighted = ring.tile([P, BLOCKS, P], F32, name="weighted")
             for b in range(BLOCKS):
                 col = h * BLOCKS + b
                 nc.scalar.activation(weighted[:, b, :], bank[:, b, :], ACT.Copy, scale=wgo_cols[:, col : col + 1])
@@ -177,7 +191,7 @@ def tile_list_rgg_none_kernel(
         def gate(t, h, eta):
             cols = slice(h * HALF, (h + 1) * HALF)
             rows = slice(t * P, (t + 1) * P)
-            za = psum_mx.tile([P, HALF], F32, name="za")
+            za = next_bank([P, HALF], "za", t, h, 1)
             for a in (1, 0):
                 nc.tensor.matmul_mx(
                     out=za[:],
@@ -200,8 +214,8 @@ def tile_list_rgg_none_kernel(
                 )
             nc.scalar.activation(eta[:, cols], za[:], ACT.Sigmoid)
 
-        def turn(h, weighted, message):
-            bank = psum.tile([P, HALF], F32, name="turned")
+        def turn(t, h, weighted, message):
+            bank = next_bank([P, HALF], "turned", t, h, 2)
             for b in range(BLOCKS):
                 nc.tensor.transpose(bank[:, b * P : (b + 1) * P], weighted[:, b, :], ident[:])
             nc.scalar.copy(message[:, h * HALF : (h + 1) * HALF], bank[:])
@@ -214,7 +228,7 @@ def tile_list_rgg_none_kernel(
         def unit(t, h, eta, message):
             weighted = messages(t, h)
             gate(t, h, eta)
-            turn(h, weighted, message)
+            turn(t, h, weighted, message)
 
         def pairs_at(name, offset):
             return shared.tile([P, HALF], U32, name=name, offset=offset, align_bytes=64)
@@ -222,16 +236,18 @@ def tile_list_rgg_none_kernel(
         grouped = {0: cast_wc(0, shared.tile([P, PASSES, P, PACK], BF16, name="wc_first", offset=1024, align_bytes=64))}
         gather_scales(0)
         gather_scales(1)
+        for a in range(PASSES):
+            load_wc(1, a)
         src_low = gather_words(0, 0, keep.tile([P, HALF], U32, name="src_low"))
-        quantise_wc(0, grouped[0])
+        dst_low = gather_words(1, 0, keep.tile([P, HALF], U32, name="dst_low"))
         part_words(0, 0, src_low)
-        dst_low = gather_words(1, 0, pairs_at("dst_low", 0))
-        src_high = gather_words(0, 1, pairs_at("src_high", 2048))
         part_words(1, 0, dst_low)
+        quantise_wc(0, grouped[0])
+        src_high = gather_words(0, 1, pairs_at("src_high", 0))
+        dst_high = gather_words(1, 1, pairs_at("dst_high", 2048))
         part_words(0, 1, src_high)
-        dst_high = gather_words(1, 1, pairs_at("dst_high", 0))
-        grouped[1] = cast_wc(1, grouped_tile(1))
-        quantise_wc(1, grouped[1])
+        second = keep.tile([P, PASSES, P, PACK], BF16, name="wc_second", align_bytes=64)
+        quantise_wc(1, cast_wc(1, second))
         part_words(1, 1, dst_high)
         for t in range(N_TILES):
             window = windows[t % 2]
@@ -241,8 +257,9 @@ def tile_list_rgg_none_kernel(
                 unit(t, h, eta, message)
                 if t < 2:
                     place(window, h * HALF, (h + 1) * HALF, eta, message)
-                    if h == 0:
-                        quantise_wc(t + 2, cast_wc(t + 2, grouped_tile(t + 2)))
+                    following = t * HALVES + h + 1
+                    if 2 <= following < N_TILES:
+                        quantise_wc(following, cast_wc(following, grouped_tile(following)))
             if t >= 2:
                 place(window, 0, J, eta, message)
             nc.sync.dma_start(out[t * P : (t + 1) * P, :], window[:])

@@ -47,7 +47,7 @@ def tile_list_rgg_none_kernel(
         src_list = lists.tile([P, J // 16], U16, name="src_list")
         dst_list = lists.tile([P, J // 16], U16, name="dst_list")
         later = ctx.enter_context(tc.tile_pool(name="later", bufs=1))
-        table_scales = later.tile([P, T], U8, name="table_scales", offset=3072, align_bytes=64)
+        table_scales = keep.tile([P, T], U8, name="table_scales", align_bytes=64)
         loaded_planes = keep.tile([P, 3, J], U8, name="loaded_planes", align_bytes=64)
         wa_planes = keep.tile([P, PASSES, N], U8, name="wa_planes", align_bytes=64)
         wb_planes = loaded_planes[:, 0, :].rearrange("p (a n) -> p a n", a=PASSES)
@@ -141,7 +141,7 @@ def tile_list_rgg_none_kernel(
             offsets = (src_list, dst_list)[i]
             picked = keep.tile([P, J], U8, name="picked_scales%d" % i, align_bytes=64)
             nc.vector.tensor_copy(picked[:], table_scales[:].indirect(offsets[:]))
-            nc.scalar.dma_start(moved[i][0 : P - SHIFT, :].bitcast(I32), picked[SHIFT:P, :].bitcast(I32))
+            nc.sync.dma_start(moved[i][0 : P - SHIFT, :].bitcast(I32), picked[SHIFT:P, :].bitcast(I32))
             planes_of[i] = (picked, moved[i])
 
         codes_of = {}
@@ -161,8 +161,12 @@ def tile_list_rgg_none_kernel(
             codes_of[i, h] = codes
 
         def next_bank(shape, kind, t, h, step):
-            turn_number = 3 * (t * HALVES + h) + step
-            return psum_mx.tile(shape, F32, name="%s%d%d" % (kind, t, h), offset=BANK * (turn_number % 2))
+            u = t * HALVES + h
+            if step == 2:
+                bank = 0 if u == 0 else 2 + u % 2
+            else:
+                bank = 1 - step if u == 1 else step
+            return psum_mx.tile(shape, F32, name="%s%d%d" % (kind, t, h), offset=BANK * bank)
 
         def messages(t, h):
             bank = next_bank([P, BLOCKS, P], "ms", t, h, 0)
@@ -236,15 +240,15 @@ def tile_list_rgg_none_kernel(
         grouped = {0: cast_wc(0, shared.tile([P, PASSES, P, PACK], BF16, name="wc_first", offset=1024, align_bytes=64))}
         gather_scales(0)
         gather_scales(1)
+        src_low = gather_words(0, 0, later.tile([P, HALF], U32, name="src_low", offset=3072, align_bytes=64))
+        quantise_wc(0, grouped[0])
+        part_words(0, 0, src_low)
         for a in range(PASSES):
             load_wc(1, a)
-        src_low = gather_words(0, 0, keep.tile([P, HALF], U32, name="src_low"))
-        dst_low = gather_words(1, 0, keep.tile([P, HALF], U32, name="dst_low"))
-        part_words(0, 0, src_low)
+        dst_low = gather_words(1, 0, pairs_at("dst_low", 0))
+        src_high = gather_words(0, 1, pairs_at("src_high", 2048))
         part_words(1, 0, dst_low)
-        quantise_wc(0, grouped[0])
-        src_high = gather_words(0, 1, pairs_at("src_high", 0))
-        dst_high = gather_words(1, 1, pairs_at("dst_high", 2048))
+        dst_high = gather_words(1, 1, pairs_at("dst_high", 0))
         part_words(0, 1, src_high)
         second = keep.tile([P, PASSES, P, PACK], BF16, name="wc_second", align_bytes=64)
         quantise_wc(1, cast_wc(1, second))

@@ -55,6 +55,8 @@ def tile_list_rgg_none_kernel(
         windows = [keep.tile([P, T], F32, name="window%d" % i) for i in range(2)]
         nc.vector.memset(table_scales[:].bitcast(I32), 0)
         nc.vector.memset(loaded_planes[:].bitcast(I32), 0)
+        nc.vector.memset(windows[0][:].bitcast(I32), 0)
+        nc.vector.memset(windows[1][:].bitcast(I32), 0)
 
         warm_tile = keep.tile([P, 16], F32, name="warm_tile")
         nc.gpsimd.memset(warm_tile[:, 0:1], 0.0)
@@ -74,8 +76,6 @@ def tile_list_rgg_none_kernel(
         ident = keep.tile([P, P], F32, name="ident")
         make_identity(nc, ident[:])
         nc.gpsimd.dma_start(wgo_rows[0 : J // P, :], wgo[0, :].rearrange("(c p) -> c p", p=P))
-        nc.gpsimd.memset(windows[0][:], 0.0)
-        nc.gpsimd.memset(windows[1][:], 0.0)
 
         wc_raw = {}
 

@@ -156,7 +156,8 @@ def tile_list_rgg_none_kernel(
         def part_words(i, h, pairs):
             codes = keep.tile([P, PASSES, 2 * HALF], U8, name="codes%d%d" % (i, h), align_bytes=64)
             nc.vector.tensor_copy(
-                codes[:].bitcast(U16), pairs[:].bitcast(U16).rearrange("p (j d) -> p d j", d=PASSES)
+                codes[:].bitcast(U16).rearrange("p d (g j) -> p g d j", g=2),
+                pairs[:].bitcast(U16).rearrange("p (g j d) -> p g d j", g=2, d=PASSES),
             )
             codes_of[i, h] = codes
 
@@ -246,12 +247,12 @@ def tile_list_rgg_none_kernel(
         for a in range(PASSES):
             load_wc(1, a)
         dst_low = gather_words(1, 0, pairs_at("dst_low", 0))
-        src_high = gather_words(0, 1, pairs_at("src_high", 2048))
-        part_words(1, 0, dst_low)
-        dst_high = gather_words(1, 1, pairs_at("dst_high", 0))
-        part_words(0, 1, src_high)
-        second = keep.tile([P, PASSES, P, PACK], BF16, name="wc_second", align_bytes=64)
+        second = shared.tile([P, PASSES, P, PACK], BF16, name="wc_second", offset=5120, align_bytes=64)
         quantise_wc(1, cast_wc(1, second))
+        part_words(1, 0, dst_low)
+        src_high = gather_words(0, 1, pairs_at("src_high", 4096))
+        dst_high = gather_words(1, 1, pairs_at("dst_high", 6144))
+        part_words(0, 1, src_high)
         part_words(1, 1, dst_high)
         for t in range(N_TILES):
             window = windows[t % 2]

@@ -28,6 +28,7 @@ BLOCKS = HALF // P
 WC_CHUNKS = ((0, 2), (2, 4))
 SHIFT = 16
 BANK = 2048
+UNITS = [(0, 0), (1, 0), (0, 1), (1, 1), (2, 0), (2, 1), (3, 0), (3, 1)]
 
 
 def tile_list_rgg_none_kernel(
@@ -40,7 +41,7 @@ def tile_list_rgg_none_kernel(
         ring = ctx.enter_context(tc.tile_pool(name="ring", bufs=3))
         psum = ctx.enter_context(tc.psum_pool(name="psum", bufs=1))
         psum_mx = ctx.enter_context(tc.psum_pool(name="psum_mx", bufs=1))
-        stage = ctx.enter_context(tc.tile_pool(name="stage", bufs=2))
+        stage = ctx.enter_context(tc.tile_pool(name="stage", bufs=3))
         turns = ctx.enter_context(tc.tile_pool(name="turns", bufs=1))
         shared = ctx.enter_context(tc.tile_pool(name="shared", bufs=1))
 
@@ -162,7 +163,7 @@ def tile_list_rgg_none_kernel(
             codes_of[i, h] = codes
 
         def next_bank(shape, kind, t, h, step):
-            u = t * HALVES + h
+            u = UNITS.index((t, h))
             if step == 2:
                 bank = 0 if u == 0 else 2 + u % 2
             else:
@@ -183,9 +184,9 @@ def tile_list_rgg_none_kernel(
                         start=(a == 1),
                         stop=(a == 0),
                     )
-            u = t * HALVES + h
-            if u in (1, 2):
-                weighted = turns.tile([P, BLOCKS, P], F32, name="weighted%d" % u, offset=2048 * (u - 1), align_bytes=64)
+            u = UNITS.index((t, h))
+            if u in (1, 3):
+                weighted = turns.tile([P, BLOCKS, P], F32, name="weighted%d" % u, offset=2048 * (u // 2), align_bytes=64)
             else:
                 weighted = ring.tile([P, BLOCKS, P], F32, name="weighted")
             for b in range(BLOCKS):
@@ -254,17 +255,19 @@ def tile_list_rgg_none_kernel(
         dst_high = gather_words(1, 1, pairs_at("dst_high", 6144))
         part_words(0, 1, src_high)
         part_words(1, 1, dst_high)
-        for t in range(N_TILES):
+        staged = {}
+        for u, (t, h) in enumerate(UNITS):
             window = windows[t % 2]
-            eta = stage.tile([P, J], F32, name="eta")
-            message = stage.tile([P, J], F32, name="message")
-            for h in range(HALVES):
-                unit(t, h, eta, message)
-                if t < 2:
-                    place(window, h * HALF, (h + 1) * HALF, eta, message)
-                    following = t * HALVES + h + 1
-                    if 2 <= following < N_TILES:
-                        quantise_wc(following, cast_wc(following, grouped_tile(following)))
-            if t >= 2:
+            if h == 0:
+                staged[t] = (stage.tile([P, J], F32, name="eta"), stage.tile([P, J], F32, name="message"))
+            eta, message = staged[t]
+            unit(t, h, eta, message)
+            if t < 2:
+                place(window, h * HALF, (h + 1) * HALF, eta, message)
+            elif h == 1:
                 place(window, 0, J, eta, message)
-            nc.sync.dma_start(out[t * P : (t + 1) * P, :], window[:])
+            if h == 1:
+                nc.sync.dma_start(out[t * P : (t + 1) * P, :], window[:])
+            if u in (1, 3):
+                following = 2 + u // 2
+                quantise_wc(following, cast_wc(following, grouped_tile(following)))

@@ -53,11 +53,10 @@ def tile_list_rgg_none_kernel(
         wa_planes = keep.tile([P, PASSES, N], U8, name="wa_planes", align_bytes=64)
         wb_planes = loaded_planes[:, 0, :].rearrange("p (a n) -> p a n", a=PASSES)
         moved = [loaded_planes[:, 1 + i, :] for i in range(2)]
-        windows = [keep.tile([P, T], F32, name="window%d" % i) for i in range(2)]
+        windows = {0: keep.tile([P, T], F32, name="window0")}
         nc.vector.memset(table_scales[:].bitcast(I32), 0)
         nc.vector.memset(loaded_planes[:].bitcast(I32), 0)
         nc.vector.memset(windows[0][:].bitcast(I32), 0)
-        nc.vector.memset(windows[1][:].bitcast(I32), 0)
 
         warm_tile = keep.tile([P, 16], F32, name="warm_tile")
         nc.gpsimd.memset(warm_tile[:, 0:1], 0.0)
@@ -185,8 +184,8 @@ def tile_list_rgg_none_kernel(
                         stop=(a == 0),
                     )
             u = UNITS.index((t, h))
-            if u in (1, 3):
-                weighted = turns.tile([P, BLOCKS, P], F32, name="weighted%d" % u, offset=2048 * (u // 2), align_bytes=64)
+            if u in (1, 2):
+                weighted = turns.tile([P, BLOCKS, P], F32, name="weighted%d" % u, offset=2048 * (u - 1), align_bytes=64)
             else:
                 weighted = ring.tile([P, BLOCKS, P], F32, name="weighted")
             for b in range(BLOCKS):
@@ -255,9 +254,11 @@ def tile_list_rgg_none_kernel(
         dst_high = gather_words(1, 1, pairs_at("dst_high", 6144))
         part_words(0, 1, src_high)
         part_words(1, 1, dst_high)
+        windows[1] = shared.tile([P, T], F32, name="window1", offset=0, align_bytes=64)
+        nc.gpsimd.memset(windows[1][:], 0.0)
         staged = {}
         for u, (t, h) in enumerate(UNITS):
-            window = windows[t % 2]
+            window = windows[t % 3]
             if h == 0:
                 staged[t] = (stage.tile([P, J], F32, name="eta"), stage.tile([P, J], F32, name="message"))
             eta, message = staged[t]
@@ -268,6 +269,9 @@ def tile_list_rgg_none_kernel(
                 place(window, 0, J, eta, message)
             if h == 1:
                 nc.sync.dma_start(out[t * P : (t + 1) * P, :], window[:])
-            if u in (1, 3):
-                following = 2 + u // 2
+            if u in (1, 2):
+                following = 1 + u
                 quantise_wc(following, cast_wc(following, grouped_tile(following)))
+            if u == 2:
+                windows[2] = turns.tile([P, T], F32, name="window2", offset=0, align_bytes=64)
+                nc.gpsimd.memset(windows[2][:], 0.0)

@@ -25,7 +25,7 @@ HALF = 512
 HALVES = J // HALF
 N_TILES = N // P
 BLOCKS = HALF // P
-WC_CHUNKS = ((0, 2), (2, 4))
+WC_CHUNKS = ((0, 1), (1, 2), (2, 4))
 SHIFT = 16
 BANK = 2048
 UNITS = [(0, 0), (1, 0), (0, 1), (1, 1), (2, 0), (2, 1), (3, 0), (3, 1)]
@@ -48,14 +48,16 @@ def tile_list_rgg_none_kernel(
         src_list = lists.tile([P, J // 16], U16, name="src_list")
         dst_list = lists.tile([P, J // 16], U16, name="dst_list")
         later = ctx.enter_context(tc.tile_pool(name="later", bufs=1))
+        early = ctx.enter_context(tc.tile_pool(name="early", bufs=1))
         table_scales = keep.tile([P, T], U8, name="table_scales", align_bytes=64)
-        loaded_planes = keep.tile([P, 3, J], U8, name="loaded_planes", align_bytes=64)
         wa_planes = keep.tile([P, PASSES, N], U8, name="wa_planes", align_bytes=64)
-        wb_planes = loaded_planes[:, 0, :].rearrange("p (a n) -> p a n", a=PASSES)
-        moved = [loaded_planes[:, 1 + i, :] for i in range(2)]
+        wb_planes = keep.tile([P, PASSES, N], U8, name="wb_planes", align_bytes=64)
+        moved_planes = keep.tile([P, 2, J], U8, name="moved_planes", align_bytes=64)
+        moved = [moved_planes[:, i, :] for i in range(2)]
         windows = {0: keep.tile([P, T], F32, name="window0")}
         nc.vector.memset(table_scales[:].bitcast(I32), 0)
-        nc.vector.memset(loaded_planes[:].bitcast(I32), 0)
+        nc.vector.memset(wb_planes[:].bitcast(I32), 0)
+        nc.vector.memset(moved_planes[:].bitcast(I32), 0)
         nc.vector.memset(windows[0][:].bitcast(I32), 0)
 
         warm_tile = keep.tile([P, 16], F32, name="warm_tile")
@@ -69,21 +71,20 @@ def tile_list_rgg_none_kernel(
                     scales[:, 4 * q : 4 * q + 4, :].rearrange("a r n -> r a n").bitcast(I32),
                 )
 
-        nc.gpsimd.memset(wa_planes[:].bitcast(I32), 0)
-        load_planes(nc.gpsimd, wa_planes, wa_scales)
         wgo_rows = keep.tile([P, P], F32, name="wgo_rows")
         nc.gpsimd.memset(wgo_rows[:], 0.0)
+        nc.gpsimd.memset(wa_planes[:].bitcast(I32), 0)
+        load_planes(nc.gpsimd, wa_planes, wa_scales)
         ident = keep.tile([P, P], F32, name="ident")
         make_identity(nc, ident[:])
-        nc.gpsimd.dma_start(wgo_rows[0 : J // P, :], wgo[0, :].rearrange("(c p) -> c p", p=P))
 
         wc_raw = {}
 
         def load_wc(c, a):
             t0, t1 = WC_CHUNKS[c]
             shape = [P, PACK, (t1 - t0) * P]
-            if c == 0:
-                raw = keep.tile(shape, F32, name="wc_first%d" % a)
+            if c < 2:
+                raw = early.tile(shape, F32, name="wc_first%d%d" % (c, a), offset=2048 * (2 * c + a), align_bytes=64)
             else:
                 raw = later.tile(shape, F32, name="wc_rest%d" % a, offset=4096 * a, align_bytes=64)
             nc.sync.dma_start(
@@ -94,18 +95,37 @@ def tile_list_rgg_none_kernel(
 
         nc.sync.dma_start(src_list[:], offs)
         nc.sync.dma_start(dst_list[:], offs2)
-        wa_codes = keep.tile([P, PASSES, 2 * N], U8, name="wa_codes", align_bytes=64)
-        nc.sync.dma_start(wa_codes[:].bitcast(I32), wa_words.rearrange("a p c -> p a c").bitcast(I32))
         by_row = tab_scales.rearrange("a (q r) t -> r q a t", r=4)
         for r in range(4):
             nc.sync.dma_start(table_scales[r:P:SHIFT, :].bitcast(I32), by_row[r].bitcast(I32))
+        load_planes(nc.sync, wb_planes, wb_scales)
+        nc.sync.dma_start(wgo_rows[0 : J // P, :], wgo[0, :].rearrange("(c p) -> c p", p=P))
         table_words = keep.tile([P, T], I32, name="table_words", align_bytes=64)
         nc.sync.dma_start(table_words[:], tab_words[0].rearrange("p t b -> p (t b)").bitcast(I32))
         load_wc(0, 0)
         load_wc(0, 1)
-        load_planes(nc.sync, wb_planes, wb_scales)
-        wb_codes = keep.tile([P, PASSES, N], I32, name="wb_codes", align_bytes=64)
-        nc.sync.dma_start(wb_codes[:], wb_words.rearrange("a p n i -> p a (n i)").bitcast(I32))
+        load_wc(1, 0)
+        load_wc(1, 1)
+        wb_codes = {}
+        wa_codes = {}
+
+        def load_gate_weights(c):
+            cols = slice(c * 2 * P, (c + 1) * 2 * P)
+            if c == 0:
+                wb_part = keep.tile([P, PASSES, 2 * P], I32, name="wb_first", align_bytes=64)
+                wa_part = keep.tile([P, PASSES, 4 * P], U8, name="wa_first", align_bytes=64)
+            else:
+                wb_part = early.tile([P, PASSES, 2 * P], I32, name="wb_rest", offset=0, align_bytes=64)
+                wa_part = early.tile([P, PASSES, 4 * P], U8, name="wa_rest", offset=2048, align_bytes=64)
+            nc.sync.dma_start(wb_part[:], wb_words.rearrange("a p n i -> p a (n i)").bitcast(I32)[:, :, cols])
+            nc.sync.dma_start(
+                wa_part[:].bitcast(I32), wa_words.rearrange("a p c -> p a c").bitcast(I32)[:, :, c * P : (c + 1) * P]
+            )
+            for t in range(2):
+                wb_codes[2 * c + t] = wb_part[:, :, t * P : (t + 1) * P]
+                wa_codes[2 * c + t] = wa_part[:, :, 2 * t * P : 2 * (t + 1) * P]
+
+        load_gate_weights(0)
 
         wgo_psum = psum.tile([P, HALF], F32, name="turned")
         nc.tensor.transpose(wgo_psum[:, 0:P], wgo_rows[:], ident[:])
@@ -141,7 +161,7 @@ def tile_list_rgg_none_kernel(
             offsets = (src_list, dst_list)[i]
             picked = keep.tile([P, J], U8, name="picked_scales%d" % i, align_bytes=64)
             nc.vector.tensor_copy(picked[:], table_scales[:].indirect(offsets[:]))
-            nc.sync.dma_start(moved[i][0 : P - SHIFT, :].bitcast(I32), picked[SHIFT:P, :].bitcast(I32))
+            (nc.scalar, nc.sync)[i].dma_start(moved[i][0 : P - SHIFT, :].bitcast(I32), picked[SHIFT:P, :].bitcast(I32))
             planes_of[i] = (picked, moved[i])
 
         codes_of = {}
@@ -200,7 +220,7 @@ def tile_list_rgg_none_kernel(
             for a in (1, 0):
                 nc.tensor.matmul_mx(
                     out=za[:],
-                    lhsT=wb_codes[:, a, rows].bitcast(FP8X4),
+                    lhsT=wb_codes[t][:, a, :].bitcast(FP8X4),
                     lhsT_scale=wb_planes[:, a, rows],
                     rhs=codes_of[0, h][:, a, :].bitcast(FP4X4),
                     rhs_scale=planes_of[0][a][:, cols],
@@ -210,7 +230,7 @@ def tile_list_rgg_none_kernel(
             for a in range(PASSES):
                 nc.tensor.matmul_mx(
                     out=za[:],
-                    lhsT=wa_codes[:, a, 2 * t * P : 2 * (t + 1) * P].bitcast(FP4X4),
+                    lhsT=wa_codes[t][:, a, :].bitcast(FP4X4),
                     lhsT_scale=wa_planes[:, a, rows],
                     rhs=codes_of[1, h][:, a, :].bitcast(FP4X4),
                     rhs_scale=planes_of[1][a][:, cols],
@@ -245,7 +265,8 @@ def tile_list_rgg_none_kernel(
         quantise_wc(0, grouped[0])
         part_words(0, 0, src_low)
         for a in range(PASSES):
-            load_wc(1, a)
+            load_wc(2, a)
+        load_gate_weights(1)
         dst_low = gather_words(1, 0, pairs_at("dst_low", 0))
         second = shared.tile([P, PASSES, P, PACK], BF16, name="wc_second", offset=5120, align_bytes=64)
         quantise_wc(1, cast_wc(1, second))

@@ -28,6 +28,7 @@ BLOCKS = HALF // P
 WC_CHUNKS = ((0, 1), (1, 2), (2, 4))
 SHIFT = 16
 BANK = 2048
+RAW_AT = {(0, 0): 0, (1, 0): 2048, (1, 1): 5120, (0, 1): 9216}
 UNITS = [(0, 0), (1, 0), (0, 1), (1, 1), (2, 0), (2, 1), (3, 0), (3, 1)]
 
 
@@ -73,10 +74,11 @@ def tile_list_rgg_none_kernel(
 
         wgo_rows = keep.tile([P, P], F32, name="wgo_rows")
         nc.gpsimd.memset(wgo_rows[:], 0.0)
-        nc.gpsimd.memset(wa_planes[:].bitcast(I32), 0)
-        load_planes(nc.gpsimd, wa_planes, wa_scales)
+        nc.scalar.dma_start(wgo_rows[0 : J // P, :], wgo[0, :].rearrange("(c p) -> c p", p=P))
         ident = keep.tile([P, P], F32, name="ident")
         make_identity(nc, ident[:])
+        nc.gpsimd.memset(wa_planes[:].bitcast(I32), 0)
+        load_planes(nc.gpsimd, wa_planes, wa_scales)
 
         wc_raw = {}
 
@@ -84,7 +86,7 @@ def tile_list_rgg_none_kernel(
             t0, t1 = WC_CHUNKS[c]
             shape = [P, PACK, (t1 - t0) * P]
             if c < 2:
-                raw = early.tile(shape, F32, name="wc_first%d%d" % (c, a), offset=2048 * (2 * c + a), align_bytes=64)
+                raw = early.tile(shape, F32, name="wc_first%d%d" % (c, a), offset=RAW_AT[c, a], align_bytes=64)
             else:
                 raw = later.tile(shape, F32, name="wc_rest%d" % a, offset=4096 * a, align_bytes=64)
             nc.sync.dma_start(
@@ -98,14 +100,13 @@ def tile_list_rgg_none_kernel(
         by_row = tab_scales.rearrange("a (q r) t -> r q a t", r=4)
         for r in range(4):
             nc.sync.dma_start(table_scales[r:P:SHIFT, :].bitcast(I32), by_row[r].bitcast(I32))
-        load_planes(nc.sync, wb_planes, wb_scales)
-        nc.sync.dma_start(wgo_rows[0 : J // P, :], wgo[0, :].rearrange("(c p) -> c p", p=P))
         table_words = keep.tile([P, T], I32, name="table_words", align_bytes=64)
         nc.sync.dma_start(table_words[:], tab_words[0].rearrange("p t b -> p (t b)").bitcast(I32))
         load_wc(0, 0)
         load_wc(0, 1)
         load_wc(1, 0)
         load_wc(1, 1)
+        load_planes(nc.sync, wb_planes, wb_scales)
         wb_codes = {}
         wa_codes = {}
 
@@ -115,8 +116,8 @@ def tile_list_rgg_none_kernel(
                 wb_part = keep.tile([P, PASSES, 2 * P], I32, name="wb_first", align_bytes=64)
                 wa_part = keep.tile([P, PASSES, 4 * P], U8, name="wa_first", align_bytes=64)
             else:
-                wb_part = early.tile([P, PASSES, 2 * P], I32, name="wb_rest", offset=0, align_bytes=64)
-                wa_part = early.tile([P, PASSES, 4 * P], U8, name="wa_rest", offset=2048, align_bytes=64)
+                wb_part = shared.tile([P, PASSES, 2 * P], I32, name="wb_rest", offset=0, align_bytes=64)
+                wa_part = shared.tile([P, PASSES, 4 * P], U8, name="wa_rest", offset=2048, align_bytes=64)
             nc.sync.dma_start(wb_part[:], wb_words.rearrange("a p n i -> p a (n i)").bitcast(I32)[:, :, cols])
             nc.sync.dma_start(
                 wa_part[:].bitcast(I32), wa_words.rearrange("a p c -> p a c").bitcast(I32)[:, :, c * P : (c + 1) * P]
@@ -161,7 +162,7 @@ def tile_list_rgg_none_kernel(
             offsets = (src_list, dst_list)[i]
             picked = keep.tile([P, J], U8, name="picked_scales%d" % i, align_bytes=64)
             nc.vector.tensor_copy(picked[:], table_scales[:].indirect(offsets[:]))
-            (nc.scalar, nc.sync)[i].dma_start(moved[i][0 : P - SHIFT, :].bitcast(I32), picked[SHIFT:P, :].bitcast(I32))
+            nc.sync.dma_start(moved[i][0 : P - SHIFT, :].bitcast(I32), picked[SHIFT:P, :].bitcast(I32))
             planes_of[i] = (picked, moved[i])
 
         codes_of = {}
@@ -174,7 +175,11 @@ def tile_list_rgg_none_kernel(
             return pairs
 
         def part_words(i, h, pairs):
-            codes = keep.tile([P, PASSES, 2 * HALF], U8, name="codes%d%d" % (i, h), align_bytes=64)
+            if h == 0:
+                offset = RAW_AT[i, 1] - 1024
+                codes = early.tile([P, PASSES, 2 * HALF], U8, name="codes%d0" % i, offset=offset, align_bytes=64)
+            else:
+                codes = keep.tile([P, PASSES, 2 * HALF], U8, name="codes%d1" % i, align_bytes=64)
             nc.vector.tensor_copy(
                 codes[:].bitcast(U16).rearrange("p d (g j) -> p g d j", g=2),
                 pairs[:].bitcast(U16).rearrange("p (g j d) -> p g d j", g=2, d=PASSES),
@@ -256,26 +261,26 @@ def tile_list_rgg_none_kernel(
             turn(t, h, weighted, message)
 
         def pairs_at(name, offset):
-            return shared.tile([P, HALF], U32, name=name, offset=offset, align_bytes=64)
+            return early.tile([P, HALF], U32, name=name, offset=offset, align_bytes=64)
 
-        grouped = {0: cast_wc(0, shared.tile([P, PASSES, P, PACK], BF16, name="wc_first", offset=1024, align_bytes=64))}
+        first = cast_wc(0, shared.tile([P, PASSES, P, PACK], BF16, name="wc_first", offset=0, align_bytes=64))
+        second = cast_wc(1, shared.tile([P, PASSES, P, PACK], BF16, name="wc_second", offset=2048, align_bytes=64))
         gather_scales(0)
         gather_scales(1)
         src_low = gather_words(0, 0, later.tile([P, HALF], U32, name="src_low", offset=3072, align_bytes=64))
-        quantise_wc(0, grouped[0])
+        quantise_wc(0, first)
         part_words(0, 0, src_low)
         for a in range(PASSES):
             load_wc(2, a)
+        dst_low = gather_words(1, 0, pairs_at("dst_low", RAW_AT[0, 1] + 1024))
+        quantise_wc(1, second)
         load_gate_weights(1)
-        dst_low = gather_words(1, 0, pairs_at("dst_low", 0))
-        second = shared.tile([P, PASSES, P, PACK], BF16, name="wc_second", offset=5120, align_bytes=64)
-        quantise_wc(1, cast_wc(1, second))
         part_words(1, 0, dst_low)
-        src_high = gather_words(0, 1, pairs_at("src_high", 4096))
-        dst_high = gather_words(1, 1, pairs_at("dst_high", 6144))
+        src_high = gather_words(0, 1, pairs_at("src_high", RAW_AT[1, 1] + 1024))
+        dst_high = gather_words(1, 1, pairs_at("dst_high", RAW_AT[0, 1] + 1024))
         part_words(0, 1, src_high)
         part_words(1, 1, dst_high)
-        windows[1] = shared.tile([P, T], F32, name="window1", offset=0, align_bytes=64)
+        windows[1] = early.tile([P, T], F32, name="window1", offset=RAW_AT[0, 1] + 1024, align_bytes=64)
         nc.gpsimd.memset(windows[1][:], 0.0)
         staged = {}
         for u, (t, h) in enumerate(UNITS):

@@ -29,7 +29,7 @@ WC_CHUNKS = ((0, 1), (1, 2), (2, 4))
 SHIFT = 16
 BANK = 2048
 RAW_AT = {(0, 0): 0, (1, 0): 2048, (1, 1): 5120, (0, 1): 9216}
-UNITS = [(0, 0), (1, 0), (0, 1), (1, 1), (2, 0), (2, 1), (3, 0), (3, 1)]
+UNITS = [(0, 0), (1, 0), (0, 1), (1, 1), (2, 0), (3, 0), (2, 1), (3, 1)]
 
 
 def tile_list_rgg_none_kernel(
@@ -50,7 +50,8 @@ def tile_list_rgg_none_kernel(
         dst_list = lists.tile([P, J // 16], U16, name="dst_list")
         later = ctx.enter_context(tc.tile_pool(name="later", bufs=1))
         early = ctx.enter_context(tc.tile_pool(name="early", bufs=1))
-        table_scales = keep.tile([P, T], U8, name="table_scales", align_bytes=64)
+        reused = ctx.enter_context(tc.tile_pool(name="reused", bufs=1))
+        table_scales = reused.tile([P, T], U8, name="table_scales", offset=1024, align_bytes=64)
         wa_planes = keep.tile([P, PASSES, N], U8, name="wa_planes", align_bytes=64)
         wb_planes = keep.tile([P, PASSES, N], U8, name="wb_planes", align_bytes=64)
         moved_planes = keep.tile([P, 2, J], U8, name="moved_planes", align_bytes=64)
@@ -113,8 +114,8 @@ def tile_list_rgg_none_kernel(
         def load_gate_weights(c):
             cols = slice(c * 2 * P, (c + 1) * 2 * P)
             if c == 0:
-                wb_part = keep.tile([P, PASSES, 2 * P], I32, name="wb_first", align_bytes=64)
-                wa_part = keep.tile([P, PASSES, 4 * P], U8, name="wa_first", align_bytes=64)
+                wb_part = reused.tile([P, PASSES, 2 * P], I32, name="wb_first", offset=0, align_bytes=64)
+                wa_part = reused.tile([P, PASSES, 4 * P], U8, name="wa_first", offset=2048, align_bytes=64)
             else:
                 wb_part = shared.tile([P, PASSES, 2 * P], I32, name="wb_rest", offset=0, align_bytes=64)
                 wa_part = shared.tile([P, PASSES, 4 * P], U8, name="wa_rest", offset=2048, align_bytes=64)
@@ -125,8 +126,6 @@ def tile_list_rgg_none_kernel(
             for t in range(2):
                 wb_codes[2 * c + t] = wb_part[:, :, t * P : (t + 1) * P]
                 wa_codes[2 * c + t] = wa_part[:, :, 2 * t * P : 2 * (t + 1) * P]
-
-        load_gate_weights(0)
 
         wgo_psum = psum.tile([P, HALF], F32, name="turned")
         nc.tensor.transpose(wgo_psum[:, 0:P], wgo_rows[:], ident[:])
@@ -162,6 +161,8 @@ def tile_list_rgg_none_kernel(
             offsets = (src_list, dst_list)[i]
             picked = keep.tile([P, J], U8, name="picked_scales%d" % i, align_bytes=64)
             nc.vector.tensor_copy(picked[:], table_scales[:].indirect(offsets[:]))
+            if i == 1:
+                load_gate_weights(0)
             nc.sync.dma_start(moved[i][0 : P - SHIFT, :].bitcast(I32), picked[SHIFT:P, :].bitcast(I32))
             planes_of[i] = (picked, moved[i])
 
@@ -289,10 +290,7 @@ def tile_list_rgg_none_kernel(
                 staged[t] = (stage.tile([P, J], F32, name="eta"), stage.tile([P, J], F32, name="message"))
             eta, message = staged[t]
             unit(t, h, eta, message)
-            if t < 2:
-                place(window, h * HALF, (h + 1) * HALF, eta, message)
-            elif h == 1:
-                place(window, 0, J, eta, message)
+            place(window, h * HALF, (h + 1) * HALF, eta, message)
             if h == 1:
                 nc.sync.dma_start(out[t * P : (t + 1) * P, :], window[:])
             if u in (1, 2):

@@ -66,8 +66,8 @@ def tile_list_rgg_none_kernel(
         nc.gpsimd.memset(warm_tile[:, 0:1], 0.0)
         nc.scalar.activation(warm_tile[:, 8:9], warm_tile[:, 0:1], ACT.Sigmoid)
 
-        def load_planes(queue, planes, scales):
-            for q in range(4):
+        def load_planes(queue, planes, scales, quadrants):
+            for q in quadrants:
                 queue.dma_start(
                     planes[32 * q : 32 * q + 4, :, :].bitcast(I32),
                     scales[:, 4 * q : 4 * q + 4, :].rearrange("a r n -> r a n").bitcast(I32),
@@ -75,11 +75,10 @@ def tile_list_rgg_none_kernel(
 
         wgo_rows = keep.tile([P, P], F32, name="wgo_rows")
         nc.gpsimd.memset(wgo_rows[:], 0.0)
-        nc.scalar.dma_start(wgo_rows[0 : J // P, :], wgo[0, :].rearrange("(c p) -> c p", p=P))
         ident = keep.tile([P, P], F32, name="ident")
         make_identity(nc, ident[:])
         nc.gpsimd.memset(wa_planes[:].bitcast(I32), 0)
-        load_planes(nc.gpsimd, wa_planes, wa_scales)
+        load_planes(nc.gpsimd, wa_planes, wa_scales, range(4))
 
         wc_raw = {}
 
@@ -101,13 +100,15 @@ def tile_list_rgg_none_kernel(
         by_row = tab_scales.rearrange("a (q r) t -> r q a t", r=4)
         for r in range(4):
             nc.sync.dma_start(table_scales[r:P:SHIFT, :].bitcast(I32), by_row[r].bitcast(I32))
+        nc.sync.dma_start(wgo_rows[0 : J // P, :], wgo[0, :].rearrange("(c p) -> c p", p=P))
+        load_planes(nc.sync, wb_planes, wb_scales, range(1))
         table_words = keep.tile([P, T], I32, name="table_words", align_bytes=64)
         nc.sync.dma_start(table_words[:], tab_words[0].rearrange("p t b -> p (t b)").bitcast(I32))
         load_wc(0, 0)
         load_wc(0, 1)
         load_wc(1, 0)
         load_wc(1, 1)
-        load_planes(nc.sync, wb_planes, wb_scales)
+        load_planes(nc.sync, wb_planes, wb_scales, range(1, 4))
         wb_codes = {}
         wa_codes = {}
 

@@ -52,13 +52,14 @@ def tile_list_rgg_none_kernel(
         early = ctx.enter_context(tc.tile_pool(name="early", bufs=1))
         reused = ctx.enter_context(tc.tile_pool(name="reused", bufs=1))
         table_scales = reused.tile([P, T], U8, name="table_scales", offset=1024, align_bytes=64)
-        wa_planes = keep.tile([P, PASSES, N], U8, name="wa_planes", align_bytes=64)
-        wb_planes = keep.tile([P, PASSES, N], U8, name="wb_planes", align_bytes=64)
+        gate_planes = keep.tile([P, 2, PASSES, N], U8, name="gate_planes", align_bytes=64)
+        wa_planes = gate_planes[:, 0, :, :]
+        wb_planes = gate_planes[:, 1, :, :]
         moved_planes = keep.tile([P, 2, J], U8, name="moved_planes", align_bytes=64)
         moved = [moved_planes[:, i, :] for i in range(2)]
         windows = {0: keep.tile([P, T], F32, name="window0")}
         nc.vector.memset(table_scales[:].bitcast(I32), 0)
-        nc.vector.memset(wb_planes[:].bitcast(I32), 0)
+        nc.vector.memset(gate_planes[:].bitcast(I32), 0)
         nc.vector.memset(moved_planes[:].bitcast(I32), 0)
         nc.vector.memset(windows[0][:].bitcast(I32), 0)
 
@@ -77,8 +78,6 @@ def tile_list_rgg_none_kernel(
         nc.gpsimd.memset(wgo_rows[:], 0.0)
         ident = keep.tile([P, P], F32, name="ident")
         make_identity(nc, ident[:])
-        nc.gpsimd.memset(wa_planes[:].bitcast(I32), 0)
-        load_planes(nc.gpsimd, wa_planes, wa_scales, range(4))
 
         wc_raw = {}
 
@@ -88,7 +87,7 @@ def tile_list_rgg_none_kernel(
             if c < 2:
                 raw = early.tile(shape, F32, name="wc_first%d%d" % (c, a), offset=RAW_AT[c, a], align_bytes=64)
             else:
-                raw = later.tile(shape, F32, name="wc_rest%d" % a, offset=4096 * a, align_bytes=64)
+                raw = later.tile(shape, F32, name="wc_rest%d" % a, offset=5120 * a, align_bytes=64)
             nc.sync.dma_start(
                 raw[:], wc[a * K_PASS : (a + 1) * K_PASS, t0 * P : t1 * P].rearrange("(p i) n -> p i n", i=PACK)
             )
@@ -100,33 +99,29 @@ def tile_list_rgg_none_kernel(
         by_row = tab_scales.rearrange("a (q r) t -> r q a t", r=4)
         for r in range(4):
             nc.sync.dma_start(table_scales[r:P:SHIFT, :].bitcast(I32), by_row[r].bitcast(I32))
-        nc.sync.dma_start(wgo_rows[0 : J // P, :], wgo[0, :].rearrange("(c p) -> c p", p=P))
-        load_planes(nc.sync, wb_planes, wb_scales, range(1))
         table_words = keep.tile([P, T], I32, name="table_words", align_bytes=64)
         nc.sync.dma_start(table_words[:], tab_words[0].rearrange("p t b -> p (t b)").bitcast(I32))
+        nc.sync.dma_start(wgo_rows[0 : J // P, :], wgo[0, :].rearrange("(c p) -> c p", p=P))
+        load_planes(nc.sync, wb_planes, wb_scales, range(4))
         load_wc(0, 0)
         load_wc(0, 1)
+        load_planes(nc.sync, wa_planes, wa_scales, range(4))
         load_wc(1, 0)
         load_wc(1, 1)
-        load_planes(nc.sync, wb_planes, wb_scales, range(1, 4))
         wb_codes = {}
         wa_codes = {}
 
-        def load_gate_weights(c):
+        def load_wb(c, part):
             cols = slice(c * 2 * P, (c + 1) * 2 * P)
-            if c == 0:
-                wb_part = reused.tile([P, PASSES, 2 * P], I32, name="wb_first", offset=0, align_bytes=64)
-                wa_part = reused.tile([P, PASSES, 4 * P], U8, name="wa_first", offset=2048, align_bytes=64)
-            else:
-                wb_part = shared.tile([P, PASSES, 2 * P], I32, name="wb_rest", offset=0, align_bytes=64)
-                wa_part = shared.tile([P, PASSES, 4 * P], U8, name="wa_rest", offset=2048, align_bytes=64)
-            nc.sync.dma_start(wb_part[:], wb_words.rearrange("a p n i -> p a (n i)").bitcast(I32)[:, :, cols])
-            nc.sync.dma_start(
-                wa_part[:].bitcast(I32), wa_words.rearrange("a p c -> p a c").bitcast(I32)[:, :, c * P : (c + 1) * P]
-            )
+            nc.sync.dma_start(part[:], wb_words.rearrange("a p n i -> p a (n i)").bitcast(I32)[:, :, cols])
             for t in range(2):
-                wb_codes[2 * c + t] = wb_part[:, :, t * P : (t + 1) * P]
-                wa_codes[2 * c + t] = wa_part[:, :, 2 * t * P : 2 * (t + 1) * P]
+                wb_codes[2 * c + t] = part[:, :, t * P : (t + 1) * P]
+
+        def load_wa(c, part):
+            cols = slice(c * P, (c + 1) * P)
+            nc.sync.dma_start(part[:].bitcast(I32), wa_words.rearrange("a p c -> p a c").bitcast(I32)[:, :, cols])
+            for t in range(2):
+                wa_codes[2 * c + t] = part[:, :, 2 * t * P : 2 * (t + 1) * P]
 
         wgo_psum = psum.tile([P, HALF], F32, name="turned")
         nc.tensor.transpose(wgo_psum[:, 0:P], wgo_rows[:], ident[:])
@@ -163,7 +158,7 @@ def tile_list_rgg_none_kernel(
             picked = keep.tile([P, J], U8, name="picked_scales%d" % i, align_bytes=64)
             nc.vector.tensor_copy(picked[:], table_scales[:].indirect(offsets[:]))
             if i == 1:
-                load_gate_weights(0)
+                load_wb(0, reused.tile([P, PASSES, 2 * P], I32, name="wb_first", offset=0, align_bytes=64))
             nc.sync.dma_start(moved[i][0 : P - SHIFT, :].bitcast(I32), picked[SHIFT:P, :].bitcast(I32))
             planes_of[i] = (picked, moved[i])
 
@@ -220,7 +215,7 @@ def tile_list_rgg_none_kernel(
                 nc.scalar.activation(weighted[:, b, :], bank[:, b, :], ACT.Copy, scale=wgo_cols[:, col : col + 1])
             return weighted
 
-        def gate(t, h, eta):
+        def gate_source(t, h):
             cols = slice(h * HALF, (h + 1) * HALF)
             rows = slice(t * P, (t + 1) * P)
             za = next_bank([P, HALF], "za", t, h, 1)
@@ -234,6 +229,11 @@ def tile_list_rgg_none_kernel(
                     start=(a == 1),
                     stop=False,
                 )
+            return za
+
+        def gate_target(t, h, za, eta):
+            cols = slice(h * HALF, (h + 1) * HALF)
+            rows = slice(t * P, (t + 1) * P)
             for a in range(PASSES):
                 nc.tensor.matmul_mx(
                     out=za[:],
@@ -259,8 +259,9 @@ def tile_list_rgg_none_kernel(
 
         def unit(t, h, eta, message):
             weighted = messages(t, h)
-            gate(t, h, eta)
+            za = gate_source(t, h)
             turn(t, h, weighted, message)
+            gate_target(t, h, za, eta)
 
         def pairs_at(name, offset):
             return early.tile([P, HALF], U32, name=name, offset=offset, align_bytes=64)
@@ -269,14 +270,16 @@ def tile_list_rgg_none_kernel(
         second = cast_wc(1, shared.tile([P, PASSES, P, PACK], BF16, name="wc_second", offset=2048, align_bytes=64))
         gather_scales(0)
         gather_scales(1)
-        src_low = gather_words(0, 0, later.tile([P, HALF], U32, name="src_low", offset=3072, align_bytes=64))
+        src_low = gather_words(0, 0, later.tile([P, HALF], U32, name="src_low", offset=3584, align_bytes=64))
         quantise_wc(0, first)
         part_words(0, 0, src_low)
+        load_wa(0, later.tile([P, PASSES, 4 * P], U8, name="wa_first", offset=4096, align_bytes=64))
         for a in range(PASSES):
             load_wc(2, a)
         dst_low = gather_words(1, 0, pairs_at("dst_low", RAW_AT[0, 1] + 1024))
         quantise_wc(1, second)
-        load_gate_weights(1)
+        load_wb(1, shared.tile([P, PASSES, 2 * P], I32, name="wb_rest", offset=0, align_bytes=64))
+        load_wa(1, shared.tile([P, PASSES, 4 * P], U8, name="wa_rest", offset=2048, align_bytes=64))
         part_words(1, 0, dst_low)
         src_high = gather_words(0, 1, pairs_at("src_high", RAW_AT[1, 1] + 1024))
         dst_high = gather_words(1, 1, pairs_at("dst_high", RAW_AT[0, 1] + 1024))

@@ -60,12 +60,17 @@ def tile_list_rgg_none_kernel(
         windows = {0: keep.tile([P, T], F32, name="window0")}
         nc.vector.memset(table_scales[:].bitcast(I32), 0)
         nc.vector.memset(gate_planes[:].bitcast(I32), 0)
+        wgo_tile = keep.tile([P, P], F32, name="wgo_tile")
+        nc.vector.memset(wgo_tile[:], 0.0)
+        wgo_rows = wgo_tile[:]
+        squares = keep.tile([P, P + 8], F32, name="squares")
+        nc.vector.memset(squares[:], 0.0)
+        ident = squares[:, 0:P]
         nc.vector.memset(moved_planes[:].bitcast(I32), 0)
         nc.vector.memset(windows[0][:].bitcast(I32), 0)
 
-        warm_tile = keep.tile([P, 16], F32, name="warm_tile")
-        nc.gpsimd.memset(warm_tile[:, 0:1], 0.0)
-        nc.scalar.activation(warm_tile[:, 8:9], warm_tile[:, 0:1], ACT.Sigmoid)
+        warm_tile = keep.tile([P, 1], F32, name="warm_tile")
+        nc.scalar.activation(warm_tile[:], squares[:, P : P + 1], ACT.Sigmoid)
 
         def load_planes(queue, planes, scales, quadrants):
             for q in quadrants:
@@ -74,10 +79,7 @@ def tile_list_rgg_none_kernel(
                     scales[:, 4 * q : 4 * q + 4, :].rearrange("a r n -> r a n").bitcast(I32),
                 )
 
-        wgo_rows = keep.tile([P, P], F32, name="wgo_rows")
-        nc.gpsimd.memset(wgo_rows[:], 0.0)
-        ident = keep.tile([P, P], F32, name="ident")
-        make_identity(nc, ident[:])
+        make_identity(nc, ident, nomemset=True)
 
         wc_raw = {}
 
@@ -124,7 +126,7 @@ def tile_list_rgg_none_kernel(
                 wa_codes[2 * c + t] = part[:, :, 2 * t * P : 2 * (t + 1) * P]
 
         wgo_psum = psum.tile([P, HALF], F32, name="turned")
-        nc.tensor.transpose(wgo_psum[:, 0:P], wgo_rows[:], ident[:])
+        nc.tensor.transpose(wgo_psum[:, 0:P], wgo_rows, ident)
         wgo_cols = keep.tile([P, J // P], F32, name="wgo_cols")
         nc.scalar.copy(wgo_cols[:], wgo_psum[:, 0 : J // P])
 
@@ -167,9 +169,20 @@ def tile_list_rgg_none_kernel(
         def gather_words(i, h, pairs):
             offsets = (src_list, dst_list)[i]
             nc.vector.tensor_copy(
-                pairs[:], table_words[:].bitcast(U32).indirect(offsets[:, h * HALF // 16 : (h + 1) * HALF // 16])
+                pairs[:, 0:HALF], table_words[:].bitcast(U32).indirect(offsets[:, h * HALF // 16 : (h + 1) * HALF // 16])
             )
             return pairs
+
+        def part_first(pairs):
+            by_pass = []
+            for a in range(PASSES):
+                offset = RAW_AT[0, 1] - 512 + 1024 * a
+                codes = early.tile([P, 2 * HALF], U8, name="codes_first%d" % a, offset=offset, align_bytes=64)
+                nc.vector.tensor_copy(
+                    codes[:].bitcast(U16), pairs[:].bitcast(U16).rearrange("p (j d) -> p d j", d=PASSES)[:, a, :]
+                )
+                by_pass.append(codes[:])
+            codes_of[0, 0] = by_pass
 
         def part_words(i, h, pairs):
             if h == 0:
@@ -179,9 +192,9 @@ def tile_list_rgg_none_kernel(
                 codes = keep.tile([P, PASSES, 2 * HALF], U8, name="codes%d1" % i, align_bytes=64)
             nc.vector.tensor_copy(
                 codes[:].bitcast(U16).rearrange("p d (g j) -> p g d j", g=2),
-                pairs[:].bitcast(U16).rearrange("p (g j d) -> p g d j", g=2, d=PASSES),
+                pairs[:, 0:HALF].bitcast(U16).rearrange("p (g j d) -> p g d j", g=2, d=PASSES),
             )
-            codes_of[i, h] = codes
+            codes_of[i, h] = [codes[:, a, :] for a in range(PASSES)]
 
         def next_bank(shape, kind, t, h, step):
             u = UNITS.index((t, h))
@@ -193,18 +206,21 @@ def tile_list_rgg_none_kernel(
 
         def messages(t, h):
             bank = next_bank([P, BLOCKS, P], "ms", t, h, 0)
-            for b in range(BLOCKS):
+            if (t, h) == UNITS[0]:
+                steps = [(b, a, b + a == 0, b + a == BLOCKS) for a in range(PASSES) for b in range(BLOCKS)]
+            else:
+                steps = [(b, a, a == 1, a == 0) for b in range(BLOCKS) for a in (1, 0)]
+            for b, a, start, stop in steps:
                 j0 = h * HALF + b * P
-                for a in (1, 0):
-                    nc.tensor.matmul_mx(
-                        out=bank[:, b, :],
-                        lhsT=codes_of[0, h][:, a, 2 * b * P : 2 * (b + 1) * P].bitcast(FP4X4),
-                        lhsT_scale=planes_of[0][a][:, j0 : j0 + P],
-                        rhs=wc_codes[t][:, a, :].bitcast(FP8X4),
-                        rhs_scale=wc_planes[t][:, a, :],
-                        start=(a == 1),
-                        stop=(a == 0),
-                    )
+                nc.tensor.matmul_mx(
+                    out=bank[:, b, :],
+                    lhsT=codes_of[0, h][a][:, 2 * b * P : 2 * (b + 1) * P].bitcast(FP4X4),
+                    lhsT_scale=planes_of[0][a][:, j0 : j0 + P],
+                    rhs=wc_codes[t][:, a, :].bitcast(FP8X4),
+                    rhs_scale=wc_planes[t][:, a, :],
+                    start=start,
+                    stop=stop,
+                )
             u = UNITS.index((t, h))
             if u in (1, 2):
                 weighted = turns.tile([P, BLOCKS, P], F32, name="weighted%d" % u, offset=2048 * (u - 1), align_bytes=64)
@@ -224,7 +240,7 @@ def tile_list_rgg_none_kernel(
                     out=za[:],
                     lhsT=wb_codes[t][:, a, :].bitcast(FP8X4),
                     lhsT_scale=wb_planes[:, a, rows],
-                    rhs=codes_of[0, h][:, a, :].bitcast(FP4X4),
+                    rhs=codes_of[0, h][a].bitcast(FP4X4),
                     rhs_scale=planes_of[0][a][:, cols],
                     start=(a == 1),
                     stop=False,
@@ -239,7 +255,7 @@ def tile_list_rgg_none_kernel(
                     out=za[:],
                     lhsT=wa_codes[t][:, a, :].bitcast(FP4X4),
                     lhsT_scale=wa_planes[:, a, rows],
-                    rhs=codes_of[1, h][:, a, :].bitcast(FP4X4),
+                    rhs=codes_of[1, h][a].bitcast(FP4X4),
                     rhs_scale=planes_of[1][a][:, cols],
                     start=False,
                     stop=(a == PASSES - 1),
@@ -249,7 +265,7 @@ def tile_list_rgg_none_kernel(
         def turn(t, h, weighted, message):
             bank = next_bank([P, HALF], "turned", t, h, 2)
             for b in range(BLOCKS):
-                nc.tensor.transpose(bank[:, b * P : (b + 1) * P], weighted[:, b, :], ident[:])
+                nc.tensor.transpose(bank[:, b * P : (b + 1) * P], weighted[:, b, :], ident)
             nc.scalar.copy(message[:, h * HALF : (h + 1) * HALF], bank[:])
 
         def place(window, j0, j1, eta, message):
@@ -263,8 +279,8 @@ def tile_list_rgg_none_kernel(
             turn(t, h, weighted, message)
             gate_target(t, h, za, eta)
 
-        def pairs_at(name, offset):
-            return early.tile([P, HALF], U32, name=name, offset=offset, align_bytes=64)
+        def pairs_at(name, offset, width=HALF):
+            return early.tile([P, width], U32, name=name, offset=offset, align_bytes=64)
 
         first = cast_wc(0, shared.tile([P, PASSES, P, PACK], BF16, name="wc_first", offset=0, align_bytes=64))
         second = cast_wc(1, shared.tile([P, PASSES, P, PACK], BF16, name="wc_second", offset=2048, align_bytes=64))
@@ -272,21 +288,23 @@ def tile_list_rgg_none_kernel(
         gather_scales(1)
         src_low = gather_words(0, 0, later.tile([P, HALF], U32, name="src_low", offset=3584, align_bytes=64))
         quantise_wc(0, first)
-        part_words(0, 0, src_low)
+        part_first(src_low)
         load_wa(0, later.tile([P, PASSES, 4 * P], U8, name="wa_first", offset=4096, align_bytes=64))
         for a in range(PASSES):
             load_wc(2, a)
-        dst_low = gather_words(1, 0, pairs_at("dst_low", RAW_AT[0, 1] + 1024))
+        dst_low = gather_words(1, 0, pairs_at("dst_low", RAW_AT[0, 1] + 1536, HALF + T))
         quantise_wc(1, second)
         load_wb(1, shared.tile([P, PASSES, 2 * P], I32, name="wb_rest", offset=0, align_bytes=64))
         load_wa(1, shared.tile([P, PASSES, 4 * P], U8, name="wa_rest", offset=2048, align_bytes=64))
         part_words(1, 0, dst_low)
         src_high = gather_words(0, 1, pairs_at("src_high", RAW_AT[1, 1] + 1024))
-        dst_high = gather_words(1, 1, pairs_at("dst_high", RAW_AT[0, 1] + 1024))
+        dst_high = gather_words(1, 1, pairs_at("dst_high", RAW_AT[0, 1] + 10240))
         part_words(0, 1, src_high)
         part_words(1, 1, dst_high)
-        windows[1] = early.tile([P, T], F32, name="window1", offset=RAW_AT[0, 1] + 1024, align_bytes=64)
+        windows[1] = early.tile([P, T], F32, name="window1", offset=RAW_AT[0, 1] + 11264, align_bytes=64)
         nc.gpsimd.memset(windows[1][:], 0.0)
+        windows[2] = early.tile([P, T], F32, name="window2", offset=RAW_AT[0, 1] + 3072, align_bytes=64)
+        nc.gpsimd.memset(windows[2][:], 0.0)
         staged = {}
         for u, (t, h) in enumerate(UNITS):
             window = windows[t % 3]
@@ -300,6 +318,3 @@ def tile_list_rgg_none_kernel(
             if u in (1, 2):
                 following = 1 + u
                 quantise_wc(following, cast_wc(following, grouped_tile(following)))
-            if u == 2:
-                windows[2] = turns.tile([P, T], F32, name="window2", offset=0, align_bytes=64)
-                nc.gpsimd.memset(windows[2][:], 0.0)

@@ -22,14 +22,13 @@ PACK = 4
 K_PASS = P * PACK
 PASSES = K // K_PASS
 HALF = 512
-HALVES = J // HALF
-N_TILES = N // P
 BLOCKS = HALF // P
 WC_CHUNKS = ((0, 1), (1, 2), (2, 4))
 SHIFT = 16
 BANK = 2048
 RAW_AT = {(0, 0): 0, (1, 0): 2048, (1, 1): 5120, (0, 1): 9216}
 UNITS = [(0, 0), (1, 0), (0, 1), (1, 1), (2, 0), (3, 0), (2, 1), (3, 1)]
+WINDOWS = 3
 
 
 def tile_list_rgg_none_kernel(
@@ -59,22 +58,20 @@ def tile_list_rgg_none_kernel(
         moved = [moved_planes[:, i, :] for i in range(2)]
         windows = {0: keep.tile([P, T], F32, name="window0")}
         nc.vector.memset(table_scales[:].bitcast(I32), 0)
-        nc.vector.memset(gate_planes[:].bitcast(I32), 0)
         wgo_tile = keep.tile([P, P], F32, name="wgo_tile")
         nc.vector.memset(wgo_tile[:], 0.0)
         wgo_rows = wgo_tile[:]
         squares = keep.tile([P, P + 8], F32, name="squares")
         nc.vector.memset(squares[:], 0.0)
         ident = squares[:, 0:P]
-        nc.vector.memset(moved_planes[:].bitcast(I32), 0)
         nc.vector.memset(windows[0][:].bitcast(I32), 0)
 
         warm_tile = keep.tile([P, 1], F32, name="warm_tile")
         nc.scalar.activation(warm_tile[:], squares[:, P : P + 1], ACT.Sigmoid)
 
-        def load_planes(queue, planes, scales, quadrants):
-            for q in quadrants:
-                queue.dma_start(
+        def load_planes(planes, scales):
+            for q in range(4):
+                nc.sync.dma_start(
                     planes[32 * q : 32 * q + 4, :, :].bitcast(I32),
                     scales[:, 4 * q : 4 * q + 4, :].rearrange("a r n -> r a n").bitcast(I32),
                 )
@@ -104,10 +101,10 @@ def tile_list_rgg_none_kernel(
         table_words = keep.tile([P, T], I32, name="table_words", align_bytes=64)
         nc.sync.dma_start(table_words[:], tab_words[0].rearrange("p t b -> p (t b)").bitcast(I32))
         nc.sync.dma_start(wgo_rows[0 : J // P, :], wgo[0, :].rearrange("(c p) -> c p", p=P))
-        load_planes(nc.sync, wb_planes, wb_scales, range(4))
+        load_planes(wb_planes, wb_scales)
         load_wc(0, 0)
         load_wc(0, 1)
-        load_planes(nc.sync, wa_planes, wa_scales, range(4))
+        load_planes(wa_planes, wa_scales)
         load_wc(1, 0)
         load_wc(1, 1)
         wb_codes = {}
@@ -125,7 +122,7 @@ def tile_list_rgg_none_kernel(
             for t in range(2):
                 wa_codes[2 * c + t] = part[:, :, 2 * t * P : 2 * (t + 1) * P]
 
-        wgo_psum = psum.tile([P, HALF], F32, name="turned")
+        wgo_psum = psum.tile([P, HALF], F32, name="wgo_psum")
         nc.tensor.transpose(wgo_psum[:, 0:P], wgo_rows, ident)
         wgo_cols = keep.tile([P, J // P], F32, name="wgo_cols")
         nc.scalar.copy(wgo_cols[:], wgo_psum[:, 0 : J // P])
@@ -307,7 +304,7 @@ def tile_list_rgg_none_kernel(
         nc.gpsimd.memset(windows[2][:], 0.0)
         staged = {}
         for u, (t, h) in enumerate(UNITS):
-            window = windows[t % 3]
+            window = windows[t % WINDOWS]
             if h == 0:
                 staged[t] = (stage.tile([P, J], F32, name="eta"), stage.tile([P, J], F32, name="message"))
             eta, message = staged[t]

@@ -24,7 +24,7 @@ PASSES = K // K_PASS
 HALF = 512
 BLOCKS = HALF // P
 WC_CHUNKS = ((0, 1), (1, 2), (2, 4))
-SHIFT = 16
+SPREAD = 4
 BANK = 2048
 RAW_AT = {(0, 0): 0, (1, 0): 2048, (1, 1): 5120, (0, 1): 9216}
 UNITS = [(0, 0), (1, 0), (0, 1), (1, 1), (2, 0), (3, 0), (2, 1), (3, 1)]
@@ -54,8 +54,7 @@ def tile_list_rgg_none_kernel(
         gate_planes = keep.tile([P, 2, PASSES, N], U8, name="gate_planes", align_bytes=64)
         wa_planes = gate_planes[:, 0, :, :]
         wb_planes = gate_planes[:, 1, :, :]
-        moved_planes = keep.tile([P, 2, J], U8, name="moved_planes", align_bytes=64)
-        moved = [moved_planes[:, i, :] for i in range(2)]
+        moved = [keep.tile([P, PASSES, J], U8, name="moved%d" % i, align_bytes=64) for i in range(2)]
         windows = {0: keep.tile([P, T], F32, name="window0")}
         nc.vector.memset(table_scales[:].bitcast(I32), 0)
         wgo_tile = keep.tile([P, P], F32, name="wgo_tile")
@@ -93,20 +92,6 @@ def tile_list_rgg_none_kernel(
             for t in range(t0, t1):
                 wc_raw[t, a] = raw[:, :, (t - t0) * P : (t - t0 + 1) * P]
 
-        nc.sync.dma_start(src_list[:], offs)
-        nc.sync.dma_start(dst_list[:], offs2)
-        by_row = tab_scales.rearrange("a (q r) t -> r q a t", r=4)
-        for r in range(4):
-            nc.sync.dma_start(table_scales[r:P:SHIFT, :].bitcast(I32), by_row[r].bitcast(I32))
-        table_words = keep.tile([P, T], I32, name="table_words", align_bytes=64)
-        nc.sync.dma_start(table_words[:], tab_words[0].rearrange("p t b -> p (t b)").bitcast(I32))
-        nc.sync.dma_start(wgo_rows[0 : J // P, :], wgo[0, :].rearrange("(c p) -> c p", p=P))
-        load_planes(wb_planes, wb_scales)
-        load_wc(0, 0)
-        load_wc(0, 1)
-        load_planes(wa_planes, wa_scales)
-        load_wc(1, 0)
-        load_wc(1, 1)
         wb_codes = {}
         wa_codes = {}
 
@@ -121,6 +106,20 @@ def tile_list_rgg_none_kernel(
             nc.sync.dma_start(part[:].bitcast(I32), wa_words.rearrange("a p c -> p a c").bitcast(I32)[:, :, cols])
             for t in range(2):
                 wa_codes[2 * c + t] = part[:, :, 2 * t * P : 2 * (t + 1) * P]
+
+        nc.sync.dma_start(src_list[:], offs)
+        nc.sync.dma_start(dst_list[:], offs2)
+        nc.sync.dma_start(table_scales[0:P:SPREAD, :].bitcast(I32), tab_scales.rearrange("a g t -> g a t").bitcast(I32))
+        table_words = keep.tile([P, T], I32, name="table_words", align_bytes=64)
+        nc.sync.dma_start(table_words[:], tab_words[0].rearrange("p t b -> p (t b)").bitcast(I32))
+        nc.sync.dma_start(wgo_rows[0 : J // P, :], wgo[0, :].rearrange("(c p) -> c p", p=P))
+        load_planes(wb_planes, wb_scales)
+        load_wc(0, 0)
+        load_wc(0, 1)
+        load_planes(wa_planes, wa_scales)
+        load_wa(0, keep.tile([P, PASSES, 4 * P], U8, name="wa_first", align_bytes=64))
+        load_wc(1, 0)
+        load_wc(1, 1)
 
         wgo_psum = psum.tile([P, HALF], F32, name="wgo_psum")
         nc.tensor.transpose(wgo_psum[:, 0:P], wgo_rows, ident)
@@ -156,10 +155,14 @@ def tile_list_rgg_none_kernel(
             offsets = (src_list, dst_list)[i]
             picked = keep.tile([P, J], U8, name="picked_scales%d" % i, align_bytes=64)
             nc.vector.tensor_copy(picked[:], table_scales[:].indirect(offsets[:]))
+            for q in range(4):
+                nc.sync.dma_start(
+                    moved[i][32 * q : 32 * q + 4, :, :].bitcast(I32),
+                    picked[32 * q : 32 * (q + 1) : SPREAD, :].bitcast(I32),
+                )
+            planes_of[i] = (moved[i][:, 0, :], moved[i][:, 1, :])
             if i == 1:
                 load_wb(0, reused.tile([P, PASSES, 2 * P], I32, name="wb_first", offset=0, align_bytes=64))
-            nc.sync.dma_start(moved[i][0 : P - SHIFT, :].bitcast(I32), picked[SHIFT:P, :].bitcast(I32))
-            planes_of[i] = (picked, moved[i])
 
         codes_of = {}
 
@@ -286,7 +289,6 @@ def tile_list_rgg_none_kernel(
         src_low = gather_words(0, 0, later.tile([P, HALF], U32, name="src_low", offset=3584, align_bytes=64))
         quantise_wc(0, first)
         part_first(src_low)
-        load_wa(0, later.tile([P, PASSES, 4 * P], U8, name="wa_first", offset=4096, align_bytes=64))
         for a in range(PASSES):
             load_wc(2, a)
         dst_low = gather_words(1, 0, pairs_at("dst_low", RAW_AT[0, 1] + 1536, HALF + T))

@@ -41,7 +41,7 @@ def tile_list_rgg_none_kernel(
         ring = ctx.enter_context(tc.tile_pool(name="ring", bufs=3))
         psum = ctx.enter_context(tc.psum_pool(name="psum", bufs=1))
         psum_mx = ctx.enter_context(tc.psum_pool(name="psum_mx", bufs=1))
-        stage = ctx.enter_context(tc.tile_pool(name="stage", bufs=3))
+        stage = ctx.enter_context(tc.tile_pool(name="stage", bufs=4))
         turns = ctx.enter_context(tc.tile_pool(name="turns", bufs=1))
         shared = ctx.enter_context(tc.tile_pool(name="shared", bufs=1))
 
@@ -50,7 +50,7 @@ def tile_list_rgg_none_kernel(
         later = ctx.enter_context(tc.tile_pool(name="later", bufs=1))
         early = ctx.enter_context(tc.tile_pool(name="early", bufs=1))
         reused = ctx.enter_context(tc.tile_pool(name="reused", bufs=1))
-        table_scales = reused.tile([P, T], U8, name="table_scales", offset=1024, align_bytes=64)
+        table_scales = reused.tile([P, T], U8, name="table_scales", offset=2048, align_bytes=64)
         gate_planes = keep.tile([P, 2, PASSES, N], U8, name="gate_planes", align_bytes=64)
         wa_planes = gate_planes[:, 0, :, :]
         wb_planes = gate_planes[:, 1, :, :]
@@ -78,12 +78,15 @@ def tile_list_rgg_none_kernel(
         make_identity(nc, ident, nomemset=True)
 
         wc_raw = {}
+        wc_second_raw = reused.tile([P, PASSES, PACK, P], F32, name="wc_second_raw", offset=4032, align_bytes=64)
 
         def load_wc(c, a):
             t0, t1 = WC_CHUNKS[c]
             shape = [P, PACK, (t1 - t0) * P]
-            if c < 2:
-                raw = early.tile(shape, F32, name="wc_first%d%d" % (c, a), offset=RAW_AT[c, a], align_bytes=64)
+            if c == 0:
+                raw = early.tile(shape, F32, name="wc_first%d" % a, offset=RAW_AT[c, a], align_bytes=64)
+            elif c == 1:
+                raw = wc_second_raw[:, a, :, :]
             else:
                 raw = later.tile(shape, F32, name="wc_rest%d" % a, offset=5120 * a, align_bytes=64)
             nc.sync.dma_start(
@@ -118,8 +121,6 @@ def tile_list_rgg_none_kernel(
         load_wc(0, 1)
         load_planes(wa_planes, wa_scales)
         load_wa(0, keep.tile([P, PASSES, 4 * P], U8, name="wa_first", align_bytes=64))
-        load_wc(1, 0)
-        load_wc(1, 1)
 
         wgo_psum = psum.tile([P, HALF], F32, name="wgo_psum")
         nc.tensor.transpose(wgo_psum[:, 0:P], wgo_rows, ident)
@@ -162,7 +163,9 @@ def tile_list_rgg_none_kernel(
                 )
             planes_of[i] = (moved[i][:, 0, :], moved[i][:, 1, :])
             if i == 1:
-                load_wb(0, reused.tile([P, PASSES, 2 * P], I32, name="wb_first", offset=0, align_bytes=64))
+                load_wb(0, reused.tile([P, PASSES, 2 * P], I32, name="wb_first", offset=64, align_bytes=64))
+                load_wc(1, 0)
+                load_wc(1, 1)
 
         codes_of = {}
 
@@ -185,11 +188,10 @@ def tile_list_rgg_none_kernel(
             codes_of[0, 0] = by_pass
 
         def part_words(i, h, pairs):
-            if h == 0:
-                offset = RAW_AT[i, 1] - 1024
-                codes = early.tile([P, PASSES, 2 * HALF], U8, name="codes%d0" % i, offset=offset, align_bytes=64)
+            if (i, h) == (1, 1):
+                codes = reused.tile([P, PASSES, 2 * HALF], U8, name="codes11", offset=2112, align_bytes=64)
             else:
-                codes = keep.tile([P, PASSES, 2 * HALF], U8, name="codes%d1" % i, align_bytes=64)
+                codes = keep.tile([P, PASSES, 2 * HALF], U8, name="codes%d%d" % (i, h), align_bytes=64)
             nc.vector.tensor_copy(
                 codes[:].bitcast(U16).rearrange("p d (g j) -> p g d j", g=2),
                 pairs[:, 0:HALF].bitcast(U16).rearrange("p (g j d) -> p g d j", g=2, d=PASSES),
@@ -260,17 +262,17 @@ def tile_list_rgg_none_kernel(
                     start=False,
                     stop=(a == PASSES - 1),
                 )
-            nc.scalar.activation(eta[:, cols], za[:], ACT.Sigmoid)
+            nc.scalar.activation(eta[:], za[:], ACT.Sigmoid)
 
         def turn(t, h, weighted, message):
             bank = next_bank([P, HALF], "turned", t, h, 2)
             for b in range(BLOCKS):
                 nc.tensor.transpose(bank[:, b * P : (b + 1) * P], weighted[:, b, :], ident)
-            nc.scalar.copy(message[:, h * HALF : (h + 1) * HALF], bank[:])
+            nc.scalar.copy(message[:], bank[:])
 
         def place(window, j0, j1, eta, message):
             nc.vector.tensor_tensor(
-                window[:].indirect(dst_list[:, j0 // 16 : j1 // 16]), eta[:, j0:j1], message[:, j0:j1], MULT
+                window[:].indirect(dst_list[:, j0 // 16 : j1 // 16]), eta[:], message[:], MULT
             )
 
         def unit(t, h, eta, message):
@@ -283,7 +285,6 @@ def tile_list_rgg_none_kernel(
             return early.tile([P, width], U32, name=name, offset=offset, align_bytes=64)
 
         first = cast_wc(0, shared.tile([P, PASSES, P, PACK], BF16, name="wc_first", offset=0, align_bytes=64))
-        second = cast_wc(1, shared.tile([P, PASSES, P, PACK], BF16, name="wc_second", offset=2048, align_bytes=64))
         gather_scales(0)
         gather_scales(1)
         src_low = gather_words(0, 0, later.tile([P, HALF], U32, name="src_low", offset=3584, align_bytes=64))
@@ -292,24 +293,27 @@ def tile_list_rgg_none_kernel(
         for a in range(PASSES):
             load_wc(2, a)
         dst_low = gather_words(1, 0, pairs_at("dst_low", RAW_AT[0, 1] + 1536, HALF + T))
+        src_high = gather_words(0, 1, shared.tile([P, HALF], U32, name="src_high", offset=0, align_bytes=64))
+        part_words(1, 0, dst_low)
+        part_words(0, 1, src_high)
+        dst_high = gather_words(1, 1, pairs_at("dst_high", RAW_AT[0, 1] + 10240))
+        second = cast_wc(1, shared.tile([P, PASSES, P, PACK], BF16, name="wc_second", offset=2048, align_bytes=64))
         quantise_wc(1, second)
+        part_words(1, 1, dst_high)
         load_wb(1, shared.tile([P, PASSES, 2 * P], I32, name="wb_rest", offset=0, align_bytes=64))
         load_wa(1, shared.tile([P, PASSES, 4 * P], U8, name="wa_rest", offset=2048, align_bytes=64))
-        part_words(1, 0, dst_low)
-        src_high = gather_words(0, 1, pairs_at("src_high", RAW_AT[1, 1] + 1024))
-        dst_high = gather_words(1, 1, pairs_at("dst_high", RAW_AT[0, 1] + 10240))
-        part_words(0, 1, src_high)
-        part_words(1, 1, dst_high)
         windows[1] = early.tile([P, T], F32, name="window1", offset=RAW_AT[0, 1] + 11264, align_bytes=64)
         nc.gpsimd.memset(windows[1][:], 0.0)
         windows[2] = early.tile([P, T], F32, name="window2", offset=RAW_AT[0, 1] + 3072, align_bytes=64)
         nc.gpsimd.memset(windows[2][:], 0.0)
-        staged = {}
         for u, (t, h) in enumerate(UNITS):
             window = windows[t % WINDOWS]
-            if h == 0:
-                staged[t] = (stage.tile([P, J], F32, name="eta"), stage.tile([P, J], F32, name="message"))
-            eta, message = staged[t]
+            if u == 0:
+                message = reused.tile([P, HALF], F32, name="message_first", offset=4160, align_bytes=64)
+                eta = reused.tile([P, HALF], F32, name="eta_first", offset=6208, align_bytes=64)
+            else:
+                message = stage.tile([P, HALF], F32, name="message")
+                eta = stage.tile([P, HALF], F32, name="eta")
             unit(t, h, eta, message)
             place(window, h * HALF, (h + 1) * HALF, eta, message)
             if h == 1:

@@ -25,6 +25,7 @@ HALF = 512
 BLOCKS = HALF // P
 WC_CHUNKS = ((0, 1), (1, 2), (2, 4))
 SPREAD = 4
+AT = 8192
 BANK = 2048
 RAW_AT = {(0, 0): 0, (1, 0): 2048, (1, 1): 5120, (0, 1): 9216}
 UNITS = [(0, 0), (1, 0), (0, 1), (1, 1), (2, 0), (3, 0), (2, 1), (3, 1)]
@@ -41,7 +42,7 @@ def tile_list_rgg_none_kernel(
         ring = ctx.enter_context(tc.tile_pool(name="ring", bufs=3))
         psum = ctx.enter_context(tc.psum_pool(name="psum", bufs=1))
         psum_mx = ctx.enter_context(tc.psum_pool(name="psum_mx", bufs=1))
-        stage = ctx.enter_context(tc.tile_pool(name="stage", bufs=4))
+        stage = ctx.enter_context(tc.tile_pool(name="stage", bufs=5))
         turns = ctx.enter_context(tc.tile_pool(name="turns", bufs=1))
         shared = ctx.enter_context(tc.tile_pool(name="shared", bufs=1))
 
@@ -50,11 +51,8 @@ def tile_list_rgg_none_kernel(
         later = ctx.enter_context(tc.tile_pool(name="later", bufs=1))
         early = ctx.enter_context(tc.tile_pool(name="early", bufs=1))
         reused = ctx.enter_context(tc.tile_pool(name="reused", bufs=1))
-        table_scales = reused.tile([P, T], U8, name="table_scales", offset=2048, align_bytes=64)
-        gate_planes = keep.tile([P, 2, PASSES, N], U8, name="gate_planes", align_bytes=64)
-        wa_planes = gate_planes[:, 0, :, :]
-        wb_planes = gate_planes[:, 1, :, :]
-        moved = [keep.tile([P, PASSES, J], U8, name="moved%d" % i, align_bytes=64) for i in range(2)]
+        table_scales = keep.tile([P, T], U8, name="table_scales", align_bytes=64)
+        wb_planes = keep.tile([P, PASSES, N], U8, name="wb_planes", align_bytes=64)
         windows = {0: keep.tile([P, T], F32, name="window0")}
         nc.vector.memset(table_scales[:].bitcast(I32), 0)
         wgo_tile = keep.tile([P, P], F32, name="wgo_tile")
@@ -78,12 +76,14 @@ def tile_list_rgg_none_kernel(
         make_identity(nc, ident, nomemset=True)
 
         wc_raw = {}
-        wc_second_raw = reused.tile([P, PASSES, PACK, P], F32, name="wc_second_raw", offset=4032, align_bytes=64)
+        wc_second_raw = reused.tile([P, PASSES, PACK, P], F32, name="wc_second_raw", offset=AT + 1984, align_bytes=64)
 
         def load_wc(c, a):
             t0, t1 = WC_CHUNKS[c]
             shape = [P, PACK, (t1 - t0) * P]
-            if c == 0:
+            if (c, a) == (0, 0):
+                raw = reused.tile(shape, F32, name="wc_first0", offset=AT + 6016, align_bytes=64)
+            elif c == 0:
                 raw = early.tile(shape, F32, name="wc_first%d" % a, offset=RAW_AT[c, a], align_bytes=64)
             elif c == 1:
                 raw = wc_second_raw[:, a, :, :]
@@ -119,8 +119,9 @@ def tile_list_rgg_none_kernel(
         load_planes(wb_planes, wb_scales)
         load_wc(0, 0)
         load_wc(0, 1)
+        wa_planes = keep.tile([P, PASSES, N], U8, name="wa_planes", align_bytes=64)
         load_planes(wa_planes, wa_scales)
-        load_wa(0, keep.tile([P, PASSES, 4 * P], U8, name="wa_first", align_bytes=64))
+        load_wb(0, keep.tile([P, PASSES, 2 * P], I32, name="wb_first", align_bytes=64))
 
         wgo_psum = psum.tile([P, HALF], F32, name="wgo_psum")
         nc.tensor.transpose(wgo_psum[:, 0:P], wgo_rows, ident)
@@ -152,20 +153,22 @@ def tile_list_rgg_none_kernel(
 
         planes_of = {}
 
-        def gather_scales(i):
-            offsets = (src_list, dst_list)[i]
-            picked = keep.tile([P, J], U8, name="picked_scales%d" % i, align_bytes=64)
-            nc.vector.tensor_copy(picked[:], table_scales[:].indirect(offsets[:]))
+        def gather_scales(halves, picked, moved):
+            for i in range(2):
+                mine = [c for c, (j, h) in enumerate(halves) if j == i]
+                if mine:
+                    h0 = halves[mine[0]][1]
+                    offsets = (src_list, dst_list)[i][:, h0 * HALF // 16 : (h0 + len(mine)) * HALF // 16]
+                    nc.vector.tensor_copy(
+                        picked[:, mine[0] * HALF : (mine[-1] + 1) * HALF], table_scales[:].indirect(offsets)
+                    )
             for q in range(4):
                 nc.sync.dma_start(
-                    moved[i][32 * q : 32 * q + 4, :, :].bitcast(I32),
+                    moved[32 * q : 32 * q + 4, :, :].bitcast(I32),
                     picked[32 * q : 32 * (q + 1) : SPREAD, :].bitcast(I32),
                 )
-            planes_of[i] = (moved[i][:, 0, :], moved[i][:, 1, :])
-            if i == 1:
-                load_wb(0, reused.tile([P, PASSES, 2 * P], I32, name="wb_first", offset=64, align_bytes=64))
-                load_wc(1, 0)
-                load_wc(1, 1)
+            for c, half in enumerate(halves):
+                planes_of[half] = [moved[:, a, c * HALF : (c + 1) * HALF] for a in range(PASSES)]
 
         codes_of = {}
 
@@ -179,8 +182,7 @@ def tile_list_rgg_none_kernel(
         def part_first(pairs):
             by_pass = []
             for a in range(PASSES):
-                offset = RAW_AT[0, 1] - 512 + 1024 * a
-                codes = early.tile([P, 2 * HALF], U8, name="codes_first%d" % a, offset=offset, align_bytes=64)
+                codes = keep.tile([P, 2 * HALF], U8, name="codes_first%d" % a, align_bytes=64)
                 nc.vector.tensor_copy(
                     codes[:].bitcast(U16), pairs[:].bitcast(U16).rearrange("p (j d) -> p d j", d=PASSES)[:, a, :]
                 )
@@ -188,10 +190,12 @@ def tile_list_rgg_none_kernel(
             codes_of[0, 0] = by_pass
 
         def part_words(i, h, pairs):
-            if (i, h) == (1, 1):
-                codes = reused.tile([P, PASSES, 2 * HALF], U8, name="codes11", offset=2112, align_bytes=64)
+            if (i, h) == (1, 0):
+                codes = early.tile([P, PASSES, 2 * HALF], U8, name="codes10", offset=RAW_AT[0, 1] + 1536, align_bytes=64)
+            elif (i, h) == (0, 1):
+                codes = shared.tile([P, PASSES, 2 * HALF], U8, name="codes01", offset=AT + 3136, align_bytes=64)
             else:
-                codes = keep.tile([P, PASSES, 2 * HALF], U8, name="codes%d%d" % (i, h), align_bytes=64)
+                codes = keep.tile([P, PASSES, 2 * HALF], U8, name="codes11", align_bytes=64)
             nc.vector.tensor_copy(
                 codes[:].bitcast(U16).rearrange("p d (g j) -> p g d j", g=2),
                 pairs[:, 0:HALF].bitcast(U16).rearrange("p (g j d) -> p g d j", g=2, d=PASSES),
@@ -201,9 +205,11 @@ def tile_list_rgg_none_kernel(
         def next_bank(shape, kind, t, h, step):
             u = UNITS.index((t, h))
             if step == 2:
-                bank = 0 if u == 0 else 2 + u % 2
+                bank = 3 * (u % 2)
+            elif step == 1:
+                bank = 1
             else:
-                bank = 1 - step if u == 1 else step
+                bank = 0 if u == 0 else 2
             return psum_mx.tile(shape, F32, name="%s%d%d" % (kind, t, h), offset=BANK * bank)
 
         def messages(t, h):
@@ -213,18 +219,19 @@ def tile_list_rgg_none_kernel(
             else:
                 steps = [(b, a, a == 1, a == 0) for b in range(BLOCKS) for a in (1, 0)]
             for b, a, start, stop in steps:
-                j0 = h * HALF + b * P
                 nc.tensor.matmul_mx(
                     out=bank[:, b, :],
                     lhsT=codes_of[0, h][a][:, 2 * b * P : 2 * (b + 1) * P].bitcast(FP4X4),
-                    lhsT_scale=planes_of[0][a][:, j0 : j0 + P],
+                    lhsT_scale=planes_of[0, h][a][:, b * P : (b + 1) * P],
                     rhs=wc_codes[t][:, a, :].bitcast(FP8X4),
                     rhs_scale=wc_planes[t][:, a, :],
                     start=start,
                     stop=stop,
                 )
             u = UNITS.index((t, h))
-            if u in (1, 2):
+            if u == 0:
+                weighted = reused.tile([P, BLOCKS, P], F32, name="weighted0", offset=AT + 2048, align_bytes=64)
+            elif u in (1, 2):
                 weighted = turns.tile([P, BLOCKS, P], F32, name="weighted%d" % u, offset=2048 * (u - 1), align_bytes=64)
             else:
                 weighted = ring.tile([P, BLOCKS, P], F32, name="weighted")
@@ -236,15 +243,16 @@ def tile_list_rgg_none_kernel(
         def gate_source(t, h):
             cols = slice(h * HALF, (h + 1) * HALF)
             rows = slice(t * P, (t + 1) * P)
-            za = next_bank([P, HALF], "za", t, h, 1)
-            for a in (1, 0):
+            width = 2 * HALF if (t, h) == UNITS[0] else HALF
+            za = next_bank([P, width], "za", t, h, 1)[:, 0:HALF]
+            for a in range(PASSES):
                 nc.tensor.matmul_mx(
                     out=za[:],
                     lhsT=wb_codes[t][:, a, :].bitcast(FP8X4),
                     lhsT_scale=wb_planes[:, a, rows],
                     rhs=codes_of[0, h][a].bitcast(FP4X4),
-                    rhs_scale=planes_of[0][a][:, cols],
-                    start=(a == 1),
+                    rhs_scale=planes_of[0, h][a],
+                    start=(a == 0),
                     stop=False,
                 )
             return za
@@ -258,7 +266,7 @@ def tile_list_rgg_none_kernel(
                     lhsT=wa_codes[t][:, a, :].bitcast(FP4X4),
                     lhsT_scale=wa_planes[:, a, rows],
                     rhs=codes_of[1, h][a].bitcast(FP4X4),
-                    rhs_scale=planes_of[1][a][:, cols],
+                    rhs_scale=planes_of[1, h][a],
                     start=False,
                     stop=(a == PASSES - 1),
                 )
@@ -276,43 +284,58 @@ def tile_list_rgg_none_kernel(
             )
 
         def unit(t, h, eta, message):
-            weighted = messages(t, h)
-            za = gate_source(t, h)
-            turn(t, h, weighted, message)
-            gate_target(t, h, za, eta)
+            if (t, h) == UNITS[0]:
+                za = gate_source(t, h)
+                weighted = messages(t, h)
+            else:
+                weighted = messages(t, h)
+                za = gate_source(t, h)
+            if (t, h) in UNITS[:2]:
+                gate_target(t, h, za, eta)
+                turn(t, h, weighted, message)
+            else:
+                turn(t, h, weighted, message)
+                gate_target(t, h, za, eta)
 
-        def pairs_at(name, offset, width=HALF):
-            return early.tile([P, width], U32, name=name, offset=offset, align_bytes=64)
-
-        first = cast_wc(0, shared.tile([P, PASSES, P, PACK], BF16, name="wc_first", offset=0, align_bytes=64))
-        gather_scales(0)
-        gather_scales(1)
-        src_low = gather_words(0, 0, later.tile([P, HALF], U32, name="src_low", offset=3584, align_bytes=64))
-        quantise_wc(0, first)
+        first = cast_wc(0, shared.tile([P, PASSES, P, PACK], BF16, name="wc_first", offset=AT, align_bytes=64))
+        gather_scales(
+            [(0, 0), (0, 1), (1, 0)],
+            keep.tile([P, 3 * HALF], U8, name="picked_early", align_bytes=64),
+            keep.tile([P, PASSES, 3 * HALF], U8, name="moved_early", align_bytes=64),
+        )
+        load_wa(0, reused.tile([P, PASSES, 4 * P], U8, name="wa_first", offset=AT + 8000, align_bytes=64))
+        load_wc(1, 0)
+        load_wc(1, 1)
+        src_low = gather_words(0, 0, keep.tile([P, HALF], U32, name="src_low", align_bytes=64))
+        dst_low = gather_words(1, 0, later.tile([P, HALF], U32, name="dst_low", offset=3584, align_bytes=64))
         part_first(src_low)
+        quantise_wc(0, first)
+        part_words(1, 0, dst_low)
         for a in range(PASSES):
             load_wc(2, a)
-        dst_low = gather_words(1, 0, pairs_at("dst_low", RAW_AT[0, 1] + 1536, HALF + T))
-        src_high = gather_words(0, 1, shared.tile([P, HALF], U32, name="src_high", offset=0, align_bytes=64))
-        part_words(1, 0, dst_low)
-        part_words(0, 1, src_high)
-        dst_high = gather_words(1, 1, pairs_at("dst_high", RAW_AT[0, 1] + 10240))
-        second = cast_wc(1, shared.tile([P, PASSES, P, PACK], BF16, name="wc_second", offset=2048, align_bytes=64))
+        src_high = gather_words(0, 1, shared.tile([P, HALF], U32, name="src_high", offset=AT, align_bytes=64))
+        gather_scales(
+            [(1, 1)],
+            later.tile([P, HALF], U8, name="picked_late", offset=4096, align_bytes=64),
+            keep.tile([P, PASSES, HALF], U8, name="moved_late", align_bytes=64),
+        )
+        second = cast_wc(1, shared.tile([P, PASSES, P, PACK], BF16, name="wc_second", offset=AT + 2048, align_bytes=64))
         quantise_wc(1, second)
+        dst_high = gather_words(1, 1, reused.tile([P, HALF], U32, name="dst_high", offset=AT, align_bytes=64))
+        part_words(0, 1, src_high)
         part_words(1, 1, dst_high)
-        load_wb(1, shared.tile([P, PASSES, 2 * P], I32, name="wb_rest", offset=0, align_bytes=64))
-        load_wa(1, shared.tile([P, PASSES, 4 * P], U8, name="wa_rest", offset=2048, align_bytes=64))
-        windows[1] = early.tile([P, T], F32, name="window1", offset=RAW_AT[0, 1] + 11264, align_bytes=64)
+        load_wb(1, shared.tile([P, PASSES, 2 * P], I32, name="wb_rest", offset=AT + 64, align_bytes=64))
+        load_wa(1, shared.tile([P, PASSES, 4 * P], U8, name="wa_rest", offset=AT + 2112, align_bytes=64))
+        windows[1] = shared.tile([P, T], F32, name="window1", offset=64, align_bytes=64)
         nc.gpsimd.memset(windows[1][:], 0.0)
-        windows[2] = early.tile([P, T], F32, name="window2", offset=RAW_AT[0, 1] + 3072, align_bytes=64)
+        windows[2] = reused.tile([P, T], F32, name="window2", offset=64, align_bytes=64)
         nc.gpsimd.memset(windows[2][:], 0.0)
         for u, (t, h) in enumerate(UNITS):
             window = windows[t % WINDOWS]
+            message = stage.tile([P, HALF], F32, name="message")
             if u == 0:
-                message = reused.tile([P, HALF], F32, name="message_first", offset=4160, align_bytes=64)
-                eta = reused.tile([P, HALF], F32, name="eta_first", offset=6208, align_bytes=64)
+                eta = reused.tile([P, HALF], F32, name="eta_first", offset=AT + 4096, align_bytes=64)
             else:
-                message = stage.tile([P, HALF], F32, name="message")
                 eta = stage.tile([P, HALF], F32, name="eta")
             unit(t, h, eta, message)
             place(window, h * HALF, (h + 1) * HALF, eta, message)

@@ -24,7 +24,7 @@ PASSES = K // K_PASS
 HALF = 512
 BLOCKS = HALF // P
 WC_CHUNKS = ((0, 1), (1, 2), (2, 4))
-SPREAD = 4
+ROWS_AT = 96
 AT = 8192
 BANK = 2048
 RAW_AT = {(0, 0): 0, (1, 0): 2048, (1, 1): 5120, (0, 1): 9216}
@@ -54,7 +54,7 @@ def tile_list_rgg_none_kernel(
         table_scales = keep.tile([P, T], U8, name="table_scales", align_bytes=64)
         wb_planes = keep.tile([P, PASSES, N], U8, name="wb_planes", align_bytes=64)
         windows = {0: keep.tile([P, T], F32, name="window0")}
-        nc.vector.memset(table_scales[:].bitcast(I32), 0)
+        nc.vector.memset(table_scales[0:ROWS_AT, :].bitcast(I32), 0)
         wgo_tile = keep.tile([P, P], F32, name="wgo_tile")
         nc.vector.memset(wgo_tile[:], 0.0)
         wgo_rows = wgo_tile[:]
@@ -110,9 +110,9 @@ def tile_list_rgg_none_kernel(
             for t in range(2):
                 wa_codes[2 * c + t] = part[:, :, 2 * t * P : 2 * (t + 1) * P]
 
+        nc.sync.dma_start(table_scales[ROWS_AT:P, :].bitcast(I32), tab_scales.rearrange("a g t -> g a t").bitcast(I32))
         nc.sync.dma_start(src_list[:], offs)
         nc.sync.dma_start(dst_list[:], offs2)
-        nc.sync.dma_start(table_scales[0:P:SPREAD, :].bitcast(I32), tab_scales.rearrange("a g t -> g a t").bitcast(I32))
         table_words = keep.tile([P, T], I32, name="table_words", align_bytes=64)
         nc.sync.dma_start(table_words[:], tab_words[0].rearrange("p t b -> p (t b)").bitcast(I32))
         nc.sync.dma_start(wgo_rows[0 : J // P, :], wgo[0, :].rearrange("(c p) -> c p", p=P))
@@ -165,7 +165,7 @@ def tile_list_rgg_none_kernel(
             for q in range(4):
                 nc.sync.dma_start(
                     moved[32 * q : 32 * q + 4, :, :].bitcast(I32),
-                    picked[32 * q : 32 * (q + 1) : SPREAD, :].bitcast(I32),
+                    picked[ROWS_AT + 8 * q : ROWS_AT + 8 * (q + 1), :].bitcast(I32),
                 )
             for c, half in enumerate(halves):
                 planes_of[half] = [moved[:, a, c * HALF : (c + 1) * HALF] for a in range(PASSES)]

@@ -53,15 +53,14 @@ def tile_list_rgg_none_kernel(
         reused = ctx.enter_context(tc.tile_pool(name="reused", bufs=1))
         table_scales = keep.tile([P, T], U8, name="table_scales", align_bytes=64)
         wb_planes = keep.tile([P, PASSES, N], U8, name="wb_planes", align_bytes=64)
-        windows = {0: keep.tile([P, T], F32, name="window0")}
+        head = ctx.enter_context(tc.tile_pool(name="head", bufs=1))
         nc.vector.memset(table_scales[0:ROWS_AT, :].bitcast(I32), 0)
-        wgo_tile = keep.tile([P, P], F32, name="wgo_tile")
+        wgo_tile = head.tile([P, P], F32, name="wgo_tile", offset=0)
         nc.vector.memset(wgo_tile[:], 0.0)
         wgo_rows = wgo_tile[:]
         squares = keep.tile([P, P + 8], F32, name="squares")
         nc.vector.memset(squares[:], 0.0)
         ident = squares[:, 0:P]
-        nc.vector.memset(windows[0][:].bitcast(I32), 0)
 
         warm_tile = keep.tile([P, 1], F32, name="warm_tile")
         nc.scalar.activation(warm_tile[:], squares[:, P : P + 1], ACT.Sigmoid)
@@ -127,6 +126,8 @@ def tile_list_rgg_none_kernel(
         nc.tensor.transpose(wgo_psum[:, 0:P], wgo_rows, ident)
         wgo_cols = keep.tile([P, J // P], F32, name="wgo_cols")
         nc.scalar.copy(wgo_cols[:], wgo_psum[:, 0 : J // P])
+        windows = {0: head.tile([P, T], F32, name="window0", offset=0)}
+        nc.gpsimd.memset(windows[0][:], 0.0)
 
         wc_codes = {}
         wc_planes = {}

@@ -23,12 +23,15 @@ K_PASS = P * PACK
 PASSES = K // K_PASS
 HALF = 512
 BLOCKS = HALF // P
+SRC, DST = 0, 1
 WC_CHUNKS = ((0, 1), (1, 2), (2, 4))
 ROWS_AT = 96
-AT = 8192
 BANK = 2048
-RAW_AT = {(0, 0): 0, (1, 0): 2048, (1, 1): 5120, (0, 1): 9216}
-UNITS = [(0, 0), (1, 0), (0, 1), (1, 1), (2, 0), (3, 0), (2, 1), (3, 1)]
+SLOT = 2048
+LAP = 64
+AT = 4 * T
+UNITS = [(0, 0), (1, 0), (0, 1), (1, 1), (2, 0), (2, 1), (3, 0), (3, 1)]
+BY_HALVES = 2
 WINDOWS = 3
 
 
@@ -42,22 +45,23 @@ def tile_list_rgg_none_kernel(
         ring = ctx.enter_context(tc.tile_pool(name="ring", bufs=3))
         psum = ctx.enter_context(tc.psum_pool(name="psum", bufs=1))
         psum_mx = ctx.enter_context(tc.psum_pool(name="psum_mx", bufs=1))
-        stage = ctx.enter_context(tc.tile_pool(name="stage", bufs=5))
-        turns = ctx.enter_context(tc.tile_pool(name="turns", bufs=1))
-        shared = ctx.enter_context(tc.tile_pool(name="shared", bufs=1))
+        on_wgo = ctx.enter_context(tc.tile_pool(name="on_wgo", bufs=1))
+        on_raw = ctx.enter_context(tc.tile_pool(name="on_raw", bufs=1))
+        on_raw_last = ctx.enter_context(tc.tile_pool(name="on_raw_last", bufs=1))
+        on_grouped = ctx.enter_context(tc.tile_pool(name="on_grouped", bufs=1))
+        on_dst_low = ctx.enter_context(tc.tile_pool(name="on_dst_low", bufs=1))
+        on_weighted = ctx.enter_context(tc.tile_pool(name="on_weighted", bufs=1))
 
         src_list = lists.tile([P, J // 16], U16, name="src_list")
         dst_list = lists.tile([P, J // 16], U16, name="dst_list")
-        later = ctx.enter_context(tc.tile_pool(name="later", bufs=1))
-        early = ctx.enter_context(tc.tile_pool(name="early", bufs=1))
-        reused = ctx.enter_context(tc.tile_pool(name="reused", bufs=1))
+
+        def entries(i, j0, j1):
+            return (src_list, dst_list)[i][:, j0 // 16 : j1 // 16]
+
         table_scales = keep.tile([P, T], U8, name="table_scales", align_bytes=64)
-        wb_planes = keep.tile([P, PASSES, N], U8, name="wb_planes", align_bytes=64)
-        head = ctx.enter_context(tc.tile_pool(name="head", bufs=1))
         nc.vector.memset(table_scales[0:ROWS_AT, :].bitcast(I32), 0)
-        wgo_tile = head.tile([P, P], F32, name="wgo_tile", offset=0)
-        nc.vector.memset(wgo_tile[:], 0.0)
-        wgo_rows = wgo_tile[:]
+        wgo_rows = on_wgo.tile([P, P], F32, name="wgo_rows", offset=0)
+        nc.vector.memset(wgo_rows[:], 0.0)
         squares = keep.tile([P, P + 8], F32, name="squares")
         nc.vector.memset(squares[:], 0.0)
         ident = squares[:, 0:P]
@@ -65,31 +69,23 @@ def tile_list_rgg_none_kernel(
         warm_tile = keep.tile([P, 1], F32, name="warm_tile")
         nc.scalar.activation(warm_tile[:], squares[:, P : P + 1], ACT.Sigmoid)
 
-        def load_planes(planes, scales):
+        make_identity(nc, ident, nomemset=True)
+
+        def load_planes(name, scales):
+            planes = keep.tile([P, PASSES, N], U8, name=name, align_bytes=64)
             for q in range(4):
                 nc.sync.dma_start(
                     planes[32 * q : 32 * q + 4, :, :].bitcast(I32),
                     scales[:, 4 * q : 4 * q + 4, :].rearrange("a r n -> r a n").bitcast(I32),
                 )
-
-        make_identity(nc, ident, nomemset=True)
+            return planes
 
         wc_raw = {}
-        wc_second_raw = reused.tile([P, PASSES, PACK, P], F32, name="wc_second_raw", offset=AT + 1984, align_bytes=64)
 
-        def load_wc(c, a):
+        def load_wc(c, a, raw):
             t0, t1 = WC_CHUNKS[c]
-            shape = [P, PACK, (t1 - t0) * P]
-            if (c, a) == (0, 0):
-                raw = reused.tile(shape, F32, name="wc_first0", offset=AT + 6016, align_bytes=64)
-            elif c == 0:
-                raw = early.tile(shape, F32, name="wc_first%d" % a, offset=RAW_AT[c, a], align_bytes=64)
-            elif c == 1:
-                raw = wc_second_raw[:, a, :, :]
-            else:
-                raw = later.tile(shape, F32, name="wc_rest%d" % a, offset=5120 * a, align_bytes=64)
             nc.sync.dma_start(
-                raw[:], wc[a * K_PASS : (a + 1) * K_PASS, t0 * P : t1 * P].rearrange("(p i) n -> p i n", i=PACK)
+                raw, wc[a * K_PASS : (a + 1) * K_PASS, t0 * P : t1 * P].rearrange("(p i) n -> p i n", i=PACK)
             )
             for t in range(t0, t1):
                 wc_raw[t, a] = raw[:, :, (t - t0) * P : (t - t0 + 1) * P]
@@ -115,24 +111,26 @@ def tile_list_rgg_none_kernel(
         table_words = keep.tile([P, T], I32, name="table_words", align_bytes=64)
         nc.sync.dma_start(table_words[:], tab_words[0].rearrange("p t b -> p (t b)").bitcast(I32))
         nc.sync.dma_start(wgo_rows[0 : J // P, :], wgo[0, :].rearrange("(c p) -> c p", p=P))
-        load_planes(wb_planes, wb_scales)
-        load_wc(0, 0)
-        load_wc(0, 1)
-        wa_planes = keep.tile([P, PASSES, N], U8, name="wa_planes", align_bytes=64)
-        load_planes(wa_planes, wa_scales)
+        wb_planes = load_planes("wb_planes", wb_scales)
+        raw00 = on_raw.tile([P, PACK, P], F32, name="raw00", offset=AT + 3 * SLOT - 2 * LAP, align_bytes=64)
+        load_wc(0, 0, raw00[:])
+        raw01 = on_raw_last.tile([P, PACK, P], F32, name="raw01", offset=0, align_bytes=64)
+        load_wc(0, 1, raw01[:])
+        wa_planes = load_planes("wa_planes", wa_scales)
         load_wb(0, keep.tile([P, PASSES, 2 * P], I32, name="wb_first", align_bytes=64))
 
         wgo_psum = psum.tile([P, HALF], F32, name="wgo_psum")
-        nc.tensor.transpose(wgo_psum[:, 0:P], wgo_rows, ident)
+        nc.tensor.transpose(wgo_psum[:, 0:P], wgo_rows[:], ident)
         wgo_cols = keep.tile([P, J // P], F32, name="wgo_cols")
         nc.scalar.copy(wgo_cols[:], wgo_psum[:, 0 : J // P])
-        windows = {0: head.tile([P, T], F32, name="window0", offset=0)}
+        windows = {0: on_wgo.tile([P, T], F32, name="window0", offset=0)}
         nc.gpsimd.memset(windows[0][:], 0.0)
 
         wc_codes = {}
         wc_planes = {}
 
-        def cast_wc(t, grouped):
+        def cast_wc(t, pool, offset):
+            grouped = pool.tile([P, PASSES, P, PACK], BF16, name="grouped%d" % t, offset=offset, align_bytes=64)
             for a in range(PASSES):
                 nc.scalar.copy(
                     grouped[:, a, :, :].rearrange("p (g m) i -> p g i m", m=4),
@@ -149,35 +147,28 @@ def tile_list_rgg_none_kernel(
                 in_=grouped[:].rearrange("p a n i -> p (a n i)"),
             )
 
-        def grouped_tile(t):
-            return turns.tile([P, PASSES, P, PACK], BF16, name="wc_grouped%d" % t, offset=2048 * (t - 2), align_bytes=64)
-
         planes_of = {}
 
-        def gather_scales(halves, picked, moved):
-            for i in range(2):
-                mine = [c for c, (j, h) in enumerate(halves) if j == i]
-                if mine:
-                    h0 = halves[mine[0]][1]
-                    offsets = (src_list, dst_list)[i][:, h0 * HALF // 16 : (h0 + len(mine)) * HALF // 16]
-                    nc.vector.tensor_copy(
-                        picked[:, mine[0] * HALF : (mine[-1] + 1) * HALF], table_scales[:].indirect(offsets)
-                    )
+        def gather_scales(name, runs, picked):
+            width = sum(j1 - j0 for i, j0, j1 in runs)
+            moved = keep.tile([P, PASSES, width], U8, name=name, align_bytes=64)
+            c0 = 0
+            for i, j0, j1 in runs:
+                nc.vector.tensor_copy(picked[:, c0 : c0 + j1 - j0], table_scales[:].indirect(entries(i, j0, j1)))
+                for j in range(j0, j1, HALF):
+                    cols = slice(c0 + j - j0, c0 + j - j0 + HALF)
+                    planes_of[i, j // HALF] = [moved[:, a, cols] for a in range(PASSES)]
+                c0 = c0 + j1 - j0
             for q in range(4):
                 nc.sync.dma_start(
                     moved[32 * q : 32 * q + 4, :, :].bitcast(I32),
                     picked[ROWS_AT + 8 * q : ROWS_AT + 8 * (q + 1), :].bitcast(I32),
                 )
-            for c, half in enumerate(halves):
-                planes_of[half] = [moved[:, a, c * HALF : (c + 1) * HALF] for a in range(PASSES)]
 
         codes_of = {}
 
         def gather_words(i, h, pairs):
-            offsets = (src_list, dst_list)[i]
-            nc.vector.tensor_copy(
-                pairs[:, 0:HALF], table_words[:].bitcast(U32).indirect(offsets[:, h * HALF // 16 : (h + 1) * HALF // 16])
-            )
+            nc.vector.tensor_copy(pairs[:], table_words[:].bitcast(U32).indirect(entries(i, h * HALF, (h + 1) * HALF)))
             return pairs
 
         def part_first(pairs):
@@ -188,52 +179,38 @@ def tile_list_rgg_none_kernel(
                     codes[:].bitcast(U16), pairs[:].bitcast(U16).rearrange("p (j d) -> p d j", d=PASSES)[:, a, :]
                 )
                 by_pass.append(codes[:])
-            codes_of[0, 0] = by_pass
+            codes_of[SRC, 0] = by_pass
 
-        def part_words(i, h, pairs):
-            if (i, h) == (1, 0):
-                codes = early.tile([P, PASSES, 2 * HALF], U8, name="codes10", offset=RAW_AT[0, 1] + 1536, align_bytes=64)
-            elif (i, h) == (0, 1):
-                codes = shared.tile([P, PASSES, 2 * HALF], U8, name="codes01", offset=AT + 3136, align_bytes=64)
-            else:
-                codes = keep.tile([P, PASSES, 2 * HALF], U8, name="codes11", align_bytes=64)
+        def part_words(i, h, pairs, codes):
             nc.vector.tensor_copy(
                 codes[:].bitcast(U16).rearrange("p d (g j) -> p g d j", g=2),
-                pairs[:, 0:HALF].bitcast(U16).rearrange("p (g j d) -> p g d j", g=2, d=PASSES),
+                pairs[:].bitcast(U16).rearrange("p (g j d) -> p g d j", g=2, d=PASSES),
             )
             codes_of[i, h] = [codes[:, a, :] for a in range(PASSES)]
 
-        def next_bank(shape, kind, t, h, step):
-            u = UNITS.index((t, h))
-            if step == 2:
-                bank = 3 * (u % 2)
-            elif step == 1:
-                bank = 1
-            else:
-                bank = 0 if u == 0 else 2
-            return psum_mx.tile(shape, F32, name="%s%d%d" % (kind, t, h), offset=BANK * bank)
-
-        def messages(t, h):
-            bank = next_bank([P, BLOCKS, P], "ms", t, h, 0)
-            if (t, h) == UNITS[0]:
+        def messages(u):
+            t, h = UNITS[u]
+            bank = psum_mx.tile([P, BLOCKS, P], F32, name="ms%d" % u, offset=BANK * (0 if u == 0 else 2))
+            if u == 0:
                 steps = [(b, a, b + a == 0, b + a == BLOCKS) for a in range(PASSES) for b in range(BLOCKS)]
             else:
                 steps = [(b, a, a == 1, a == 0) for b in range(BLOCKS) for a in (1, 0)]
             for b, a, start, stop in steps:
                 nc.tensor.matmul_mx(
                     out=bank[:, b, :],
-                    lhsT=codes_of[0, h][a][:, 2 * b * P : 2 * (b + 1) * P].bitcast(FP4X4),
-                    lhsT_scale=planes_of[0, h][a][:, b * P : (b + 1) * P],
+                    lhsT=codes_of[SRC, h][a][:, 2 * b * P : 2 * (b + 1) * P].bitcast(FP4X4),
+                    lhsT_scale=planes_of[SRC, h][a][:, b * P : (b + 1) * P],
                     rhs=wc_codes[t][:, a, :].bitcast(FP8X4),
                     rhs_scale=wc_planes[t][:, a, :],
                     start=start,
                     stop=stop,
                 )
-            u = UNITS.index((t, h))
             if u == 0:
-                weighted = reused.tile([P, BLOCKS, P], F32, name="weighted0", offset=AT + 2048, align_bytes=64)
+                weighted = on_raw.tile([P, BLOCKS, P], F32, name="weighted0", offset=AT + SLOT, align_bytes=64)
             elif u in (1, 2):
-                weighted = turns.tile([P, BLOCKS, P], F32, name="weighted%d" % u, offset=2048 * (u - 1), align_bytes=64)
+                weighted = on_weighted.tile(
+                    [P, BLOCKS, P], F32, name="weighted%d" % u, offset=SLOT * (u - 1), align_bytes=64
+                )
             else:
                 weighted = ring.tile([P, BLOCKS, P], F32, name="weighted")
             for b in range(BLOCKS):
@@ -241,107 +218,115 @@ def tile_list_rgg_none_kernel(
                 nc.scalar.activation(weighted[:, b, :], bank[:, b, :], ACT.Copy, scale=wgo_cols[:, col : col + 1])
             return weighted
 
-        def gate_source(t, h):
-            cols = slice(h * HALF, (h + 1) * HALF)
+        def gate_source(u):
+            t, h = UNITS[u]
             rows = slice(t * P, (t + 1) * P)
-            width = 2 * HALF if (t, h) == UNITS[0] else HALF
-            za = next_bank([P, width], "za", t, h, 1)[:, 0:HALF]
+            za = psum_mx.tile([P, 2 * HALF if u == 0 else HALF], F32, name="za%d" % u, offset=BANK)[:, 0:HALF]
             for a in range(PASSES):
                 nc.tensor.matmul_mx(
-                    out=za[:],
+                    out=za,
                     lhsT=wb_codes[t][:, a, :].bitcast(FP8X4),
                     lhsT_scale=wb_planes[:, a, rows],
-                    rhs=codes_of[0, h][a].bitcast(FP4X4),
-                    rhs_scale=planes_of[0, h][a],
+                    rhs=codes_of[SRC, h][a].bitcast(FP4X4),
+                    rhs_scale=planes_of[SRC, h][a],
                     start=(a == 0),
                     stop=False,
                 )
             return za
 
-        def gate_target(t, h, za, eta):
-            cols = slice(h * HALF, (h + 1) * HALF)
+        def gate_target(u, za, eta):
+            t, h = UNITS[u]
             rows = slice(t * P, (t + 1) * P)
             for a in range(PASSES):
                 nc.tensor.matmul_mx(
-                    out=za[:],
+                    out=za,
                     lhsT=wa_codes[t][:, a, :].bitcast(FP4X4),
                     lhsT_scale=wa_planes[:, a, rows],
-                    rhs=codes_of[1, h][a].bitcast(FP4X4),
-                    rhs_scale=planes_of[1, h][a],
+                    rhs=codes_of[DST, h][a].bitcast(FP4X4),
+                    rhs_scale=planes_of[DST, h][a],
                     start=False,
                     stop=(a == PASSES - 1),
                 )
-            nc.scalar.activation(eta[:], za[:], ACT.Sigmoid)
+            nc.scalar.activation(eta, za, ACT.Sigmoid)
 
-        def turn(t, h, weighted, message):
-            bank = next_bank([P, HALF], "turned", t, h, 2)
+        def turn(u, weighted, message):
+            bank = psum_mx.tile([P, HALF], F32, name="turned%d" % u, offset=BANK * 3 * (u % 2))
             for b in range(BLOCKS):
                 nc.tensor.transpose(bank[:, b * P : (b + 1) * P], weighted[:, b, :], ident)
-            nc.scalar.copy(message[:], bank[:])
+            nc.scalar.copy(message, bank[:])
+
+        def unit(u, eta, message):
+            if u == 0:
+                za = gate_source(u)
+                weighted = messages(u)
+            else:
+                weighted = messages(u)
+                za = gate_source(u)
+            if u < 2:
+                gate_target(u, za, eta)
+                turn(u, weighted, message)
+            else:
+                turn(u, weighted, message)
+                gate_target(u, za, eta)
 
         def place(window, j0, j1, eta, message):
-            nc.vector.tensor_tensor(
-                window[:].indirect(dst_list[:, j0 // 16 : j1 // 16]), eta[:], message[:], MULT
-            )
+            nc.vector.tensor_tensor(window[:].indirect(entries(DST, j0, j1)), eta[:], message[:], MULT)
 
-        def unit(t, h, eta, message):
-            if (t, h) == UNITS[0]:
-                za = gate_source(t, h)
-                weighted = messages(t, h)
-            else:
-                weighted = messages(t, h)
-                za = gate_source(t, h)
-            if (t, h) in UNITS[:2]:
-                gate_target(t, h, za, eta)
-                turn(t, h, weighted, message)
-            else:
-                turn(t, h, weighted, message)
-                gate_target(t, h, za, eta)
-
-        first = cast_wc(0, shared.tile([P, PASSES, P, PACK], BF16, name="wc_first", offset=AT, align_bytes=64))
-        gather_scales(
-            [(0, 0), (0, 1), (1, 0)],
-            keep.tile([P, 3 * HALF], U8, name="picked_early", align_bytes=64),
-            keep.tile([P, PASSES, 3 * HALF], U8, name="moved_early", align_bytes=64),
-        )
-        load_wa(0, reused.tile([P, PASSES, 4 * P], U8, name="wa_first", offset=AT + 8000, align_bytes=64))
-        load_wc(1, 0)
-        load_wc(1, 1)
-        src_low = gather_words(0, 0, keep.tile([P, HALF], U32, name="src_low", align_bytes=64))
-        dst_low = gather_words(1, 0, later.tile([P, HALF], U32, name="dst_low", offset=3584, align_bytes=64))
-        part_first(src_low)
-        quantise_wc(0, first)
-        part_words(1, 0, dst_low)
+        grouped0 = cast_wc(0, on_grouped, AT)
+        picked_early = keep.tile([P, J + HALF], U8, name="picked_early", align_bytes=64)
+        gather_scales("moved_early", [(SRC, 0, J), (DST, 0, HALF)], picked_early)
+        load_wa(0, on_raw.tile([P, PASSES, 4 * P], U8, name="wa_first", offset=AT + 4 * SLOT - 3 * LAP, align_bytes=64))
+        raw1 = on_raw.tile([P, PASSES, PACK, P], F32, name="raw1", offset=AT + SLOT - LAP, align_bytes=64)
         for a in range(PASSES):
-            load_wc(2, a)
-        src_high = gather_words(0, 1, shared.tile([P, HALF], U32, name="src_high", offset=AT, align_bytes=64))
-        gather_scales(
-            [(1, 1)],
-            later.tile([P, HALF], U8, name="picked_late", offset=4096, align_bytes=64),
-            keep.tile([P, PASSES, HALF], U8, name="moved_late", align_bytes=64),
+            load_wc(1, a, raw1[:, a, :, :])
+        src_low = gather_words(SRC, 0, keep.tile([P, HALF], U32, name="src_low", align_bytes=64))
+        dst_low = gather_words(
+            DST, 0, on_dst_low.tile([P, HALF], U32, name="dst_low", offset=2 * SLOT - LAP, align_bytes=64)
         )
-        second = cast_wc(1, shared.tile([P, PASSES, P, PACK], BF16, name="wc_second", offset=AT + 2048, align_bytes=64))
-        quantise_wc(1, second)
-        dst_high = gather_words(1, 1, reused.tile([P, HALF], U32, name="dst_high", offset=AT, align_bytes=64))
-        part_words(0, 1, src_high)
-        part_words(1, 1, dst_high)
-        load_wb(1, shared.tile([P, PASSES, 2 * P], I32, name="wb_rest", offset=AT + 64, align_bytes=64))
-        load_wa(1, shared.tile([P, PASSES, 4 * P], U8, name="wa_rest", offset=AT + 2112, align_bytes=64))
-        windows[1] = shared.tile([P, T], F32, name="window1", offset=64, align_bytes=64)
+        part_first(src_low)
+        quantise_wc(0, grouped0)
+        part_words(DST, 0, dst_low, on_raw_last.tile([P, PASSES, 2 * HALF], U8, name="codes_dst_low", offset=0, align_bytes=64))
+        for a in range(PASSES):
+            rest = on_dst_low.tile(
+                [P, PACK, 2 * P], F32, name="raw2%d" % a, offset=a * (3 * SLOT - 2 * LAP), align_bytes=64
+            )
+            load_wc(2, a, rest[:])
+        src_high = gather_words(SRC, 1, on_grouped.tile([P, HALF], U32, name="src_high", offset=AT, align_bytes=64))
+        picked_late = on_dst_low.tile([P, HALF], U8, name="picked_late", offset=2 * SLOT, align_bytes=64)
+        gather_scales("moved_late", [(DST, HALF, J)], picked_late)
+        grouped1 = cast_wc(1, on_grouped, AT + SLOT)
+        quantise_wc(1, grouped1)
+        dst_high = gather_words(DST, 1, on_raw.tile([P, HALF], U32, name="dst_high", offset=AT, align_bytes=64))
+        codes_src_high = on_grouped.tile(
+            [P, PASSES, 2 * HALF], U8, name="codes_src_high", offset=AT + SLOT + LAP + SLOT // 2, align_bytes=64
+        )
+        part_words(SRC, 1, src_high, codes_src_high)
+        part_words(DST, 1, dst_high, keep.tile([P, PASSES, 2 * HALF], U8, name="codes_dst_high", align_bytes=64))
+        load_wb(1, on_grouped.tile([P, PASSES, 2 * P], I32, name="wb_rest", offset=AT + LAP, align_bytes=64))
+        load_wa(1, on_grouped.tile([P, PASSES, 4 * P], U8, name="wa_rest", offset=AT + SLOT + LAP, align_bytes=64))
+        windows[1] = on_grouped.tile([P, T], F32, name="window1", offset=LAP, align_bytes=64)
         nc.gpsimd.memset(windows[1][:], 0.0)
-        windows[2] = reused.tile([P, T], F32, name="window2", offset=64, align_bytes=64)
+        windows[2] = on_raw.tile([P, T], F32, name="window2", offset=LAP, align_bytes=64)
         nc.gpsimd.memset(windows[2][:], 0.0)
+
         for u, (t, h) in enumerate(UNITS):
             window = windows[t % WINDOWS]
-            message = stage.tile([P, HALF], F32, name="message")
-            if u == 0:
-                eta = reused.tile([P, HALF], F32, name="eta_first", offset=AT + 4096, align_bytes=64)
+            if t < BY_HALVES:
+                message = keep.tile([P, HALF], F32, name="message%d%d" % (t, h))
+                if u == 0:
+                    eta = on_raw.tile([P, HALF], F32, name="eta00", offset=AT + 2 * SLOT, align_bytes=64)
+                else:
+                    eta = keep.tile([P, HALF], F32, name="eta%d%d" % (t, h))
+                unit(u, eta[:], message[:])
+                place(window, h * HALF, (h + 1) * HALF, eta, message)
             else:
-                eta = stage.tile([P, HALF], F32, name="eta")
-            unit(t, h, eta, message)
-            place(window, h * HALF, (h + 1) * HALF, eta, message)
+                if h == 0:
+                    message = keep.tile([P, J], F32, name="message%d" % t)
+                    eta = keep.tile([P, J], F32, name="eta%d" % t)
+                unit(u, eta[:, h * HALF : (h + 1) * HALF], message[:, h * HALF : (h + 1) * HALF])
+                if h == 1:
+                    place(window, 0, J, eta, message)
             if h == 1:
                 nc.sync.dma_start(out[t * P : (t + 1) * P, :], window[:])
             if u in (1, 2):
-                following = 1 + u
-                quantise_wc(following, cast_wc(following, grouped_tile(following)))
+                quantise_wc(1 + u, cast_wc(1 + u, on_weighted, SLOT * (u - 1)))

@@ -1,7 +1,6 @@
 from contextlib import ExitStack
 
 import concourse.mybir as mybir
-from concourse.masks import make_identity
 
 K, N, T, J = 1024, 512, 2048, 1024
 FLOPS = 3 * 2 * K * N * J
@@ -45,7 +44,7 @@ def tile_list_rgg_none_kernel(
         ring = ctx.enter_context(tc.tile_pool(name="ring", bufs=3))
         psum = ctx.enter_context(tc.psum_pool(name="psum", bufs=1))
         psum_mx = ctx.enter_context(tc.psum_pool(name="psum_mx", bufs=1))
-        on_wgo = ctx.enter_context(tc.tile_pool(name="on_wgo", bufs=1))
+        on_zeros = ctx.enter_context(tc.tile_pool(name="on_zeros", bufs=1))
         on_raw = ctx.enter_context(tc.tile_pool(name="on_raw", bufs=1))
         on_raw_last = ctx.enter_context(tc.tile_pool(name="on_raw_last", bufs=1))
         on_grouped = ctx.enter_context(tc.tile_pool(name="on_grouped", bufs=1))
@@ -60,16 +59,26 @@ def tile_list_rgg_none_kernel(
 
         table_scales = keep.tile([P, T], U8, name="table_scales", align_bytes=64)
         nc.vector.memset(table_scales[0:ROWS_AT, :].bitcast(I32), 0)
-        wgo_rows = on_wgo.tile([P, P], F32, name="wgo_rows", offset=0)
+        wgo_rows = keep.tile([P, P], F32, name="wgo_rows")
         nc.vector.memset(wgo_rows[:], 0.0)
-        squares = keep.tile([P, P + 8], F32, name="squares")
-        nc.vector.memset(squares[:], 0.0)
-        ident = squares[:, 0:P]
+        zeros = on_zeros.tile([P, P], F32, name="zeros", offset=0)
+        nc.vector.memset(zeros[:], 0.0)
+        ident_tile = keep.tile([P, P], F32, name="ident")
+        ident = ident_tile[:]
+        nc.gpsimd.affine_select(
+            out=ident,
+            in_=zeros[:],
+            compare_op=mybir.AluOpType.not_equal,
+            fill=1.0,
+            base=0,
+            pattern=[[-1, P]],
+            channel_multiplier=1,
+        )
+        windows = {0: on_zeros.tile([P, T], F32, name="window0", offset=0)}
+        nc.gpsimd.memset(windows[0][:], 0.0)
 
         warm_tile = keep.tile([P, 1], F32, name="warm_tile")
-        nc.scalar.activation(warm_tile[:], squares[:, P : P + 1], ACT.Sigmoid)
-
-        make_identity(nc, ident, nomemset=True)
+        nc.scalar.activation(warm_tile[:], ident[:, 0:1], ACT.Sigmoid)
 
         def load_planes(name, scales):
             planes = keep.tile([P, PASSES, N], U8, name=name, align_bytes=64)
@@ -123,8 +132,6 @@ def tile_list_rgg_none_kernel(
         nc.tensor.transpose(wgo_psum[:, 0:P], wgo_rows[:], ident)
         wgo_cols = keep.tile([P, J // P], F32, name="wgo_cols")
         nc.scalar.copy(wgo_cols[:], wgo_psum[:, 0 : J // P])
-        windows = {0: on_wgo.tile([P, T], F32, name="window0", offset=0)}
-        nc.gpsimd.memset(windows[0][:], 0.0)
 
         wc_codes = {}
         wc_planes = {}

@@ -20,18 +20,13 @@ P = 128
 PACK = 4
 K_PASS = P * PACK
 PASSES = K // K_PASS
+TILES = N // P
 HALF = 512
-BLOCKS = HALF // P
-SRC, DST = 0, 1
-WC_CHUNKS = ((0, 1), (1, 2), (2, 4))
+FIRST = 256
 ROWS_AT = 96
 BANK = 2048
-SLOT = 2048
 LAP = 64
-AT = 4 * T
-UNITS = [(0, 0), (1, 0), (0, 1), (1, 1), (2, 0), (2, 1), (3, 0), (3, 1)]
-BY_HALVES = 2
-WINDOWS = 3
+KIB = 1024
 
 
 def tile_list_rgg_none_kernel(
@@ -43,25 +38,21 @@ def tile_list_rgg_none_kernel(
         keep = ctx.enter_context(tc.tile_pool(name="keep", bufs=1))
         ring = ctx.enter_context(tc.tile_pool(name="ring", bufs=3))
         psum = ctx.enter_context(tc.psum_pool(name="psum", bufs=1))
-        psum_mx = ctx.enter_context(tc.psum_pool(name="psum_mx", bufs=1))
         on_zeros = ctx.enter_context(tc.tile_pool(name="on_zeros", bufs=1))
-        on_raw = ctx.enter_context(tc.tile_pool(name="on_raw", bufs=1))
-        on_raw_last = ctx.enter_context(tc.tile_pool(name="on_raw_last", bufs=1))
-        on_grouped = ctx.enter_context(tc.tile_pool(name="on_grouped", bufs=1))
-        on_dst_low = ctx.enter_context(tc.tile_pool(name="on_dst_low", bufs=1))
+        on_first = ctx.enter_context(tc.tile_pool(name="on_first", bufs=1))
         on_weighted = ctx.enter_context(tc.tile_pool(name="on_weighted", bufs=1))
+        on_second = ctx.enter_context(tc.tile_pool(name="on_second", bufs=1))
+        on_grouped = ctx.enter_context(tc.tile_pool(name="on_grouped", bufs=1))
+        on_raw = ctx.enter_context(tc.tile_pool(name="on_raw", bufs=1))
 
         src_list = lists.tile([P, J // 16], U16, name="src_list")
         dst_list = lists.tile([P, J // 16], U16, name="dst_list")
 
-        def entries(i, j0, j1):
-            return (src_list, dst_list)[i][:, j0 // 16 : j1 // 16]
-
-        table_scales = keep.tile([P, T], U8, name="table_scales", align_bytes=64)
+        table_scales = keep.tile([P, T], U8, name="table_scales", align_bytes=64)[:]
         nc.vector.memset(table_scales[0:ROWS_AT, :].bitcast(I32), 0)
         wgo_rows = keep.tile([P, P], F32, name="wgo_rows")
         nc.vector.memset(wgo_rows[:], 0.0)
-        zeros = on_zeros.tile([P, P], F32, name="zeros", offset=0)
+        zeros = on_zeros.tile([P, P], F32, name="zeros", offset=4 * T - LAP)
         nc.vector.memset(zeros[:], 0.0)
         ident_tile = keep.tile([P, P], F32, name="ident")
         ident = ident_tile[:]
@@ -74,266 +65,216 @@ def tile_list_rgg_none_kernel(
             pattern=[[-1, P]],
             channel_multiplier=1,
         )
-        windows = {0: on_zeros.tile([P, T], F32, name="window0", offset=0)}
-        nc.gpsimd.memset(windows[0][:], 0.0)
+        windows = []
+        for w in range(2):
+            window = on_zeros.tile([P, T], F32, name="window%d" % w, offset=4 * T * w)
+            nc.gpsimd.memset(window[:], 0.0)
+            windows.append(window)
 
         warm_tile = keep.tile([P, 1], F32, name="warm_tile")
         nc.scalar.activation(warm_tile[:], ident[:, 0:1], ACT.Sigmoid)
 
-        def load_planes(name, scales):
-            planes = keep.tile([P, PASSES, N], U8, name=name, align_bytes=64)
+        def load_planes(planes, scales):
             for q in range(4):
                 nc.sync.dma_start(
                     planes[32 * q : 32 * q + 4, :, :].bitcast(I32),
                     scales[:, 4 * q : 4 * q + 4, :].rearrange("a r n -> r a n").bitcast(I32),
                 )
-            return planes
 
         wc_raw = {}
 
-        def load_wc(c, a, raw):
-            t0, t1 = WC_CHUNKS[c]
+        def load_wc(t0, a, raw):
+            tiles = raw.shape[2] // P
             nc.sync.dma_start(
-                raw, wc[a * K_PASS : (a + 1) * K_PASS, t0 * P : t1 * P].rearrange("(p i) n -> p i n", i=PACK)
+                raw, wc[a * K_PASS : (a + 1) * K_PASS, t0 * P : (t0 + tiles) * P].rearrange("(p i) n -> p i n", i=PACK)
             )
-            for t in range(t0, t1):
-                wc_raw[t, a] = raw[:, :, (t - t0) * P : (t - t0 + 1) * P]
-
-        wb_codes = {}
-        wa_codes = {}
-
-        def load_wb(c, part):
-            cols = slice(c * 2 * P, (c + 1) * 2 * P)
-            nc.sync.dma_start(part[:], wb_words.rearrange("a p n i -> p a (n i)").bitcast(I32)[:, :, cols])
-            for t in range(2):
-                wb_codes[2 * c + t] = part[:, :, t * P : (t + 1) * P]
-
-        def load_wa(c, part):
-            cols = slice(c * P, (c + 1) * P)
-            nc.sync.dma_start(part[:].bitcast(I32), wa_words.rearrange("a p c -> p a c").bitcast(I32)[:, :, cols])
-            for t in range(2):
-                wa_codes[2 * c + t] = part[:, :, 2 * t * P : 2 * (t + 1) * P]
+            for t in range(tiles):
+                wc_raw[t0 + t, a] = raw[:, :, t * P : (t + 1) * P]
 
         nc.sync.dma_start(table_scales[ROWS_AT:P, :].bitcast(I32), tab_scales.rearrange("a g t -> g a t").bitcast(I32))
         nc.sync.dma_start(src_list[:], offs)
         nc.sync.dma_start(dst_list[:], offs2)
         table_words = keep.tile([P, T], I32, name="table_words", align_bytes=64)
         nc.sync.dma_start(table_words[:], tab_words[0].rearrange("p t b -> p (t b)").bitcast(I32))
-        nc.sync.dma_start(wgo_rows[0 : J // P, :], wgo[0, :].rearrange("(c p) -> c p", p=P))
-        wb_planes = load_planes("wb_planes", wb_scales)
-        raw00 = on_raw.tile([P, PACK, P], F32, name="raw00", offset=AT + 3 * SLOT - 2 * LAP, align_bytes=64)
+        raw00 = on_first.tile([P, PACK, P], F32, name="raw00", offset=4 * KIB - LAP, align_bytes=64)
         load_wc(0, 0, raw00[:])
-        raw01 = on_raw_last.tile([P, PACK, P], F32, name="raw01", offset=0, align_bytes=64)
+        raw01 = on_second.tile([P, PACK, P], F32, name="raw01", offset=4 * KIB - LAP, align_bytes=64)
         load_wc(0, 1, raw01[:])
-        wa_planes = load_planes("wa_planes", wa_scales)
-        load_wb(0, keep.tile([P, PASSES, 2 * P], I32, name="wb_first", align_bytes=64))
+        nc.sync.dma_start(wgo_rows[0 : J // P, :], wgo[0, :].rearrange("(c p) -> c p", p=P))
+        wb_planes = keep.tile([P, PASSES, N], U8, name="wb_planes", align_bytes=64)
+        load_planes(wb_planes, wb_scales)
+        raw1 = on_raw.tile([P, PASSES, PACK, P], F32, name="raw1", offset=2 * KIB - LAP, align_bytes=64)
+        for a in range(PASSES):
+            load_wc(1, a, raw1[:, a, :, :])
 
-        wgo_psum = psum.tile([P, HALF], F32, name="wgo_psum")
+        wgo_psum = psum.tile([P, HALF], F32, name="wgo_psum", offset=7 * BANK)
         nc.tensor.transpose(wgo_psum[:, 0:P], wgo_rows[:], ident)
         wgo_cols = keep.tile([P, J // P], F32, name="wgo_cols")
         nc.scalar.copy(wgo_cols[:], wgo_psum[:, 0 : J // P])
 
+        def cast_wc(t, a, grouped):
+            nc.scalar.copy(
+                grouped[:, a, :, :].rearrange("p (g m) i -> p g i m", m=4),
+                wc_raw[t, a].rearrange("p i (g m) -> p g i m", m=4),
+            )
+
         wc_codes = {}
         wc_planes = {}
 
-        def cast_wc(t, pool, offset):
-            grouped = pool.tile([P, PASSES, P, PACK], BF16, name="grouped%d" % t, offset=offset, align_bytes=64)
-            for a in range(PASSES):
-                nc.scalar.copy(
-                    grouped[:, a, :, :].rearrange("p (g m) i -> p g i m", m=4),
-                    wc_raw[t, a].rearrange("p i (g m) -> p g i m", m=4),
-                )
-            return grouped
-
-        def quantise_wc(t, grouped):
-            wc_codes[t] = keep.tile([P, PASSES, P], U32, name="wc_codes%d" % t, align_bytes=64)
-            wc_planes[t] = keep.tile([P, PASSES, P], U8, name="wc_planes%d" % t, align_bytes=64)
+        def quantise_wc(t0, grouped):
+            width = grouped.shape[2]
+            codes = keep.tile([P, PASSES, width], U32, name="wc_codes%d" % t0, align_bytes=64)
+            planes = keep.tile([P, PASSES, width], U8, name="wc_planes%d" % t0, align_bytes=64)
             nc.vector.quantize_mx(
-                out=wc_codes[t][:].rearrange("p a n -> p (a n)").bitcast(FP8X4),
-                scales=wc_planes[t][:].rearrange("p a n -> p (a n)"),
+                out=codes[:].rearrange("p a n -> p (a n)").bitcast(FP8X4),
+                scales=planes[:].rearrange("p a n -> p (a n)"),
                 in_=grouped[:].rearrange("p a n i -> p (a n i)"),
             )
+            for t in range(width // P):
+                wc_codes[t0 + t] = codes[:, :, t * P : (t + 1) * P]
+                wc_planes[t0 + t] = planes[:, :, t * P : (t + 1) * P]
 
-        planes_of = {}
-
-        def gather_scales(name, runs, picked):
-            width = sum(j1 - j0 for i, j0, j1 in runs)
-            moved = keep.tile([P, PASSES, width], U8, name=name, align_bytes=64)
-            c0 = 0
-            for i, j0, j1 in runs:
-                nc.vector.tensor_copy(picked[:, c0 : c0 + j1 - j0], table_scales[:].indirect(entries(i, j0, j1)))
-                for j in range(j0, j1, HALF):
-                    cols = slice(c0 + j - j0, c0 + j - j0 + HALF)
-                    planes_of[i, j // HALF] = [moved[:, a, cols] for a in range(PASSES)]
-                c0 = c0 + j1 - j0
-            for q in range(4):
-                nc.sync.dma_start(
-                    moved[32 * q : 32 * q + 4, :, :].bitcast(I32),
-                    picked[ROWS_AT + 8 * q : ROWS_AT + 8 * (q + 1), :].bitcast(I32),
-                )
-
-        codes_of = {}
-
-        def gather_words(i, h, pairs):
-            nc.vector.tensor_copy(pairs[:], table_words[:].bitcast(U32).indirect(entries(i, h * HALF, (h + 1) * HALF)))
-            return pairs
-
-        def part_first(pairs):
-            by_pass = []
-            for a in range(PASSES):
-                codes = keep.tile([P, 2 * HALF], U8, name="codes_first%d" % a, align_bytes=64)
-                nc.vector.tensor_copy(
-                    codes[:].bitcast(U16), pairs[:].bitcast(U16).rearrange("p (j d) -> p d j", d=PASSES)[:, a, :]
-                )
-                by_pass.append(codes[:])
-            codes_of[SRC, 0] = by_pass
-
-        def part_words(i, h, pairs, codes):
+        def part_words(pairs, j0, j1, codes):
             nc.vector.tensor_copy(
-                codes[:].bitcast(U16).rearrange("p d (g j) -> p g d j", g=2),
-                pairs[:].bitcast(U16).rearrange("p (g j d) -> p g d j", g=2, d=PASSES),
+                codes.bitcast(U16).rearrange("p d (g j) -> p g d j", g=2),
+                pairs[:, j0:j1].bitcast(U16).rearrange("p (g j d) -> p g d j", g=2, d=PASSES),
             )
-            codes_of[i, h] = [codes[:, a, :] for a in range(PASSES)]
 
-        def messages(u):
-            t, h = UNITS[u]
-            bank = psum_mx.tile([P, BLOCKS, P], F32, name="ms%d" % u, offset=BANK * (0 if u == 0 else 2))
-            if u == 0:
-                steps = [(b, a, b + a == 0, b + a == BLOCKS) for a in range(PASSES) for b in range(BLOCKS)]
-            else:
-                steps = [(b, a, a == 1, a == 0) for b in range(BLOCKS) for a in (1, 0)]
-            for b, a, start, stop in steps:
-                nc.tensor.matmul_mx(
-                    out=bank[:, b, :],
-                    lhsT=codes_of[SRC, h][a][:, 2 * b * P : 2 * (b + 1) * P].bitcast(FP4X4),
-                    lhsT_scale=planes_of[SRC, h][a][:, b * P : (b + 1) * P],
-                    rhs=wc_codes[t][:, a, :].bitcast(FP8X4),
-                    rhs_scale=wc_planes[t][:, a, :],
-                    start=start,
-                    stop=stop,
-                )
-            if u == 0:
-                weighted = on_raw.tile([P, BLOCKS, P], F32, name="weighted0", offset=AT + SLOT, align_bytes=64)
-            elif u in (1, 2):
-                weighted = on_weighted.tile(
-                    [P, BLOCKS, P], F32, name="weighted%d" % u, offset=SLOT * (u - 1), align_bytes=64
-                )
-            else:
-                weighted = ring.tile([P, BLOCKS, P], F32, name="weighted")
-            for b in range(BLOCKS):
-                col = h * BLOCKS + b
-                nc.scalar.activation(weighted[:, b, :], bank[:, b, :], ACT.Copy, scale=wgo_cols[:, col : col + 1])
-            return weighted
+        def codes_at(parts, a, j0, j1):
+            for p0, p1, codes in parts:
+                if p0 <= j0 and j1 <= p1:
+                    return codes[:, a, 2 * (j0 - p0) : 2 * (j1 - p0)].bitcast(FP4X4)
+            raise ValueError("no tile holds these edges")
 
-        def gate_source(u):
-            t, h = UNITS[u]
+        picked = keep.tile([P, 2 * J], U8, name="picked", align_bytes=64)
+        nc.vector.tensor_copy(picked[:, 0:J], table_scales.indirect(src_list[:]))
+        nc.vector.tensor_copy(picked[:, J : 2 * J], table_scales.indirect(dst_list[:]))
+        moved = keep.tile([P, PASSES, 2 * J], U8, name="moved", align_bytes=64)
+        for q in range(4):
+            nc.sync.dma_start(
+                moved[32 * q : 32 * q + 4, :, :].bitcast(I32),
+                picked[ROWS_AT + 8 * q : ROWS_AT + 8 * (q + 1), :].bitcast(I32),
+            )
+        def gather_words(pairs, offsets):
+            nc.vector.tensor_copy(pairs[:], table_words[:].bitcast(U32).indirect(offsets))
+
+        src_low_pairs = keep.tile([P, HALF], U32, name="src_low_pairs", align_bytes=64)
+        gather_words(src_low_pairs, src_list[:, 0 : HALF // 16])
+        grouped0 = on_grouped.tile([P, PASSES, P, PACK], BF16, name="grouped0", offset=4 * KIB - LAP, align_bytes=64)
+        for a in range(PASSES):
+            cast_wc(0, a, grouped0)
+        wb_codes = on_first.tile([P, PASSES, N], I32, name="wb_codes", offset=0, align_bytes=64)
+        nc.sync.dma_start(wb_codes[:], wb_words.rearrange("a p n i -> p a (n i)").bitcast(I32))
+        wa_codes = on_first.tile([P, PASSES, 2 * N], U8, name="wa_codes", offset=5 * KIB, align_bytes=64)
+        nc.sync.dma_start(wa_codes[:].bitcast(I32), wa_words.rearrange("a p c -> p a c").bitcast(I32))
+        wa_planes = on_first.tile([P, PASSES, N], U8, name="wa_planes", offset=4 * KIB, align_bytes=64)
+        load_planes(wa_planes, wa_scales)
+        quantise_wc(0, grouped0)
+        for a in range(PASSES):
+            raw = on_grouped.tile([P, PACK, 2 * P], F32, name="raw2%d" % a, offset=a * 5 * KIB, align_bytes=64)
+            load_wc(2, a, raw[:])
+        src_low = on_second.tile([P, PASSES, 2 * HALF], U8, name="src_low", offset=2 * KIB, align_bytes=64)
+        part_words(src_low_pairs, 0, HALF, src_low[:])
+        dst_pairs = on_second.tile([P, J], U32, name="dst_pairs", offset=4 * KIB, align_bytes=64)
+        gather_words(dst_pairs, dst_list[:])
+        grouped1 = keep.tile([P, PASSES, P, PACK], BF16, name="grouped1", align_bytes=64)
+        for a in range(PASSES):
+            cast_wc(1, a, grouped1)
+        quantise_wc(1, grouped1)
+        dst_low = on_raw.tile([P, PASSES, 2 * HALF], U8, name="dst_low", offset=0, align_bytes=64)
+        part_words(dst_pairs, 0, HALF, dst_low[:])
+        src_high_pairs = on_raw.tile([P, HALF], U32, name="src_high_pairs", offset=2 * KIB, align_bytes=64)
+        gather_words(src_high_pairs, src_list[:, HALF // 16 : J // 16])
+        dst_high = on_raw.tile([P, PASSES, 2 * HALF], U8, name="dst_high", offset=4 * KIB, align_bytes=64)
+        part_words(dst_pairs, HALF, J, dst_high[:])
+        src_high = keep.tile([P, PASSES, 2 * HALF], U8, name="src_high", align_bytes=64)
+        part_words(src_high_pairs, 0, HALF, src_high[:])
+        src_parts = [(0, HALF, src_low), (HALF, J, src_high)]
+        dst_parts = [(0, HALF, dst_low), (HALF, J, dst_high)]
+        window = on_second.tile([P, T], F32, name="window2", offset=8 * KIB - LAP, align_bytes=64)
+        nc.gpsimd.memset(window[:], 0.0)
+        windows.append(window)
+
+        def messages(n, t, j0, j1, weighted, message):
+            blocks = (j1 - j0) // P
+            groups = 2 if n == 0 else 1
+            per = blocks // groups
+            for g in range(groups):
+                bank = psum.tile([P, per, P], F32, name="ms%d%d" % (n, g), offset=BANK * (g if n == 0 else 3 + n % 2))
+                for b in range(per):
+                    e0 = j0 + (g * per + b) * P
+                    for a in range(PASSES):
+                        nc.tensor.matmul_mx(
+                            out=bank[:, b, :],
+                            lhsT=codes_at(src_parts, a, e0, e0 + P),
+                            lhsT_scale=moved[:, a, e0 : e0 + P],
+                            rhs=wc_codes[t][:, a, :].bitcast(FP8X4),
+                            rhs_scale=wc_planes[t][:, a, :],
+                            start=(a == 0),
+                            stop=(a == PASSES - 1),
+                        )
+                for b in range(per):
+                    col = j0 // P + g * per + b
+                    nc.scalar.activation(
+                        weighted[:, g * per + b, :], bank[:, b, :], ACT.Copy, scale=wgo_cols[:, col : col + 1]
+                    )
+            turned = psum.tile([P, j1 - j0], F32, name="turned%d" % n, offset=BANK * (6 + n % 2))[:]
+            for b in range(blocks):
+                nc.tensor.transpose(turned[:, b * P : (b + 1) * P], weighted[:, b, :], ident)
+            nc.scalar.copy(message, turned)
+
+        def gate(n, t, j0, j1, eta):
             rows = slice(t * P, (t + 1) * P)
-            za = psum_mx.tile([P, 2 * HALF if u == 0 else HALF], F32, name="za%d" % u, offset=BANK)[:, 0:HALF]
-            for a in range(PASSES):
-                nc.tensor.matmul_mx(
-                    out=za,
-                    lhsT=wb_codes[t][:, a, :].bitcast(FP8X4),
-                    lhsT_scale=wb_planes[:, a, rows],
-                    rhs=codes_of[SRC, h][a].bitcast(FP4X4),
-                    rhs_scale=planes_of[SRC, h][a],
-                    start=(a == 0),
-                    stop=False,
-                )
-            return za
-
-        def gate_target(u, za, eta):
-            t, h = UNITS[u]
-            rows = slice(t * P, (t + 1) * P)
-            for a in range(PASSES):
-                nc.tensor.matmul_mx(
-                    out=za,
-                    lhsT=wa_codes[t][:, a, :].bitcast(FP4X4),
-                    lhsT_scale=wa_planes[:, a, rows],
-                    rhs=codes_of[DST, h][a].bitcast(FP4X4),
-                    rhs_scale=planes_of[DST, h][a],
-                    start=False,
-                    stop=(a == PASSES - 1),
-                )
+            width = 4 * HALF if n == 0 else j1 - j0
+            za = psum.tile([P, width], F32, name="za%d" % n, offset=BANK * (2 + 3 * (n % 2)))[:, 0 : j1 - j0]
+            cuts = [j0, j1]
+            for e0, e1 in zip(cuts, cuts[1:]):
+                for a in range(PASSES):
+                    nc.tensor.matmul_mx(
+                        out=za[:, e0 - j0 : e1 - j0],
+                        lhsT=wb_codes[:, a, rows].bitcast(FP8X4),
+                        lhsT_scale=wb_planes[:, a, rows],
+                        rhs=codes_at(src_parts, a, e0, e1),
+                        rhs_scale=moved[:, a, e0:e1],
+                        start=(a == 0),
+                        stop=False,
+                    )
+                for a in range(PASSES):
+                    nc.tensor.matmul_mx(
+                        out=za[:, e0 - j0 : e1 - j0],
+                        lhsT=wa_codes[:, a, 2 * t * P : 2 * (t + 1) * P].bitcast(FP4X4),
+                        lhsT_scale=wa_planes[:, a, rows],
+                        rhs=codes_at(dst_parts, a, e0, e1),
+                        rhs_scale=moved[:, a, J + e0 : J + e1],
+                        start=False,
+                        stop=(a == PASSES - 1),
+                    )
             nc.scalar.activation(eta, za, ACT.Sigmoid)
 
-        def turn(u, weighted, message):
-            bank = psum_mx.tile([P, HALF], F32, name="turned%d" % u, offset=BANK * 3 * (u % 2))
-            for b in range(BLOCKS):
-                nc.tensor.transpose(bank[:, b * P : (b + 1) * P], weighted[:, b, :], ident)
-            nc.scalar.copy(message, bank[:])
-
-        def unit(u, eta, message):
-            if u == 0:
-                za = gate_source(u)
-                weighted = messages(u)
-            else:
-                weighted = messages(u)
-                za = gate_source(u)
-            if u < 2:
-                gate_target(u, za, eta)
-                turn(u, weighted, message)
-            else:
-                turn(u, weighted, message)
-                gate_target(u, za, eta)
-
-        def place(window, j0, j1, eta, message):
-            nc.vector.tensor_tensor(window[:].indirect(entries(DST, j0, j1)), eta[:], message[:], MULT)
-
-        grouped0 = cast_wc(0, on_grouped, AT)
-        picked_early = keep.tile([P, J + HALF], U8, name="picked_early", align_bytes=64)
-        gather_scales("moved_early", [(SRC, 0, J), (DST, 0, HALF)], picked_early)
-        load_wa(0, on_raw.tile([P, PASSES, 4 * P], U8, name="wa_first", offset=AT + 4 * SLOT - 3 * LAP, align_bytes=64))
-        raw1 = on_raw.tile([P, PASSES, PACK, P], F32, name="raw1", offset=AT + SLOT - LAP, align_bytes=64)
-        for a in range(PASSES):
-            load_wc(1, a, raw1[:, a, :, :])
-        src_low = gather_words(SRC, 0, keep.tile([P, HALF], U32, name="src_low", align_bytes=64))
-        dst_low = gather_words(
-            DST, 0, on_dst_low.tile([P, HALF], U32, name="dst_low", offset=2 * SLOT - LAP, align_bytes=64)
-        )
-        part_first(src_low)
-        quantise_wc(0, grouped0)
-        part_words(DST, 0, dst_low, on_raw_last.tile([P, PASSES, 2 * HALF], U8, name="codes_dst_low", offset=0, align_bytes=64))
-        for a in range(PASSES):
-            rest = on_dst_low.tile(
-                [P, PACK, 2 * P], F32, name="raw2%d" % a, offset=a * (3 * SLOT - 2 * LAP), align_bytes=64
+        def place(t, j0, j1, eta, message):
+            nc.vector.tensor_tensor(
+                windows[t % 3][:].indirect(dst_list[:, j0 // 16 : j1 // 16]), eta, message, MULT
             )
-            load_wc(2, a, rest[:])
-        src_high = gather_words(SRC, 1, on_grouped.tile([P, HALF], U32, name="src_high", offset=AT, align_bytes=64))
-        picked_late = on_dst_low.tile([P, HALF], U8, name="picked_late", offset=2 * SLOT, align_bytes=64)
-        gather_scales("moved_late", [(DST, HALF, J)], picked_late)
-        grouped1 = cast_wc(1, on_grouped, AT + SLOT)
-        quantise_wc(1, grouped1)
-        dst_high = gather_words(DST, 1, on_raw.tile([P, HALF], U32, name="dst_high", offset=AT, align_bytes=64))
-        codes_src_high = on_grouped.tile(
-            [P, PASSES, 2 * HALF], U8, name="codes_src_high", offset=AT + SLOT + LAP + SLOT // 2, align_bytes=64
-        )
-        part_words(SRC, 1, src_high, codes_src_high)
-        part_words(DST, 1, dst_high, keep.tile([P, PASSES, 2 * HALF], U8, name="codes_dst_high", align_bytes=64))
-        load_wb(1, on_grouped.tile([P, PASSES, 2 * P], I32, name="wb_rest", offset=AT + LAP, align_bytes=64))
-        load_wa(1, on_grouped.tile([P, PASSES, 4 * P], U8, name="wa_rest", offset=AT + SLOT + LAP, align_bytes=64))
-        windows[1] = on_grouped.tile([P, T], F32, name="window1", offset=LAP, align_bytes=64)
-        nc.gpsimd.memset(windows[1][:], 0.0)
-        windows[2] = on_raw.tile([P, T], F32, name="window2", offset=LAP, align_bytes=64)
-        nc.gpsimd.memset(windows[2][:], 0.0)
 
-        for u, (t, h) in enumerate(UNITS):
-            window = windows[t % WINDOWS]
-            if t < BY_HALVES:
-                message = keep.tile([P, HALF], F32, name="message%d%d" % (t, h))
-                if u == 0:
-                    eta = on_raw.tile([P, HALF], F32, name="eta00", offset=AT + 2 * SLOT, align_bytes=64)
+        scatters = [(0, 0, HALF), (1, 0, HALF), (0, HALF, J), (1, HALF, J), (2, 0, J), (3, 0, J)]
+        n = 0
+        for s, (t, j0, j1) in enumerate(scatters):
+            message = keep.tile([P, j1 - j0], F32, name="message%d" % s)
+            eta = keep.tile([P, j1 - j0], F32, name="eta%d" % s)
+            cuts = [j0, HALF, j1] if j0 < HALF < j1 else [j0, j1]
+            for e0, e1 in zip(cuts, cuts[1:]):
+                if n in (1, 2):
+                    weighted = on_weighted.tile([P, 4, P], F32, name="weighted%d" % n, offset=2 * KIB * (n - 1), align_bytes=64)
                 else:
-                    eta = keep.tile([P, HALF], F32, name="eta%d%d" % (t, h))
-                unit(u, eta[:], message[:])
-                place(window, h * HALF, (h + 1) * HALF, eta, message)
-            else:
-                if h == 0:
-                    message = keep.tile([P, J], F32, name="message%d" % t)
-                    eta = keep.tile([P, J], F32, name="eta%d" % t)
-                unit(u, eta[:, h * HALF : (h + 1) * HALF], message[:, h * HALF : (h + 1) * HALF])
-                if h == 1:
-                    place(window, 0, J, eta, message)
-            if h == 1:
-                nc.sync.dma_start(out[t * P : (t + 1) * P, :], window[:])
-            if u in (1, 2):
-                quantise_wc(1 + u, cast_wc(1 + u, on_weighted, SLOT * (u - 1)))
+                    weighted = ring.tile([P, 4, P], F32, name="weighted")
+                messages(n, t, e0, e1, weighted, message[:, e0 - j0 : e1 - j0])
+                gate(n, t, e0, e1, eta[:, e0 - j0 : e1 - j0])
+                n = n + 1
+            place(t, j0, j1, eta[:], message[:])
+            if j1 == J:
+                nc.sync.dma_start(out[t * P : (t + 1) * P, :], windows[t % 3][:])
+            if s in (1, 2):
+                lent = on_weighted.tile([P, PASSES, P, PACK], BF16, name="grouped%d" % (s + 1), offset=2 * KIB * (s - 1), align_bytes=64)
+                for a in range(PASSES):
+                    cast_wc(s + 1, a, lent)
+                quantise_wc(s + 1, lent)

@@ -43,6 +43,7 @@ def tile_list_rgg_none_kernel(
         on_weighted = ctx.enter_context(tc.tile_pool(name="on_weighted", bufs=1))
         on_second = ctx.enter_context(tc.tile_pool(name="on_second", bufs=1))
         on_grouped = ctx.enter_context(tc.tile_pool(name="on_grouped", bufs=1))
+        on_later = ctx.enter_context(tc.tile_pool(name="on_later", bufs=1))
         on_raw = ctx.enter_context(tc.tile_pool(name="on_raw", bufs=1))
 
         src_list = lists.tile([P, J // 16], U16, name="src_list")
@@ -50,7 +51,7 @@ def tile_list_rgg_none_kernel(
 
         table_scales = keep.tile([P, T], U8, name="table_scales", align_bytes=64)[:]
         nc.vector.memset(table_scales[0:ROWS_AT, :].bitcast(I32), 0)
-        wgo_rows = keep.tile([P, P], F32, name="wgo_rows")
+        wgo_rows = on_raw.tile([P, P], F32, name="wgo_rows", offset=6 * KIB, align_bytes=64)
         nc.vector.memset(wgo_rows[:], 0.0)
         zeros = on_zeros.tile([P, P], F32, name="zeros", offset=4 * T - LAP)
         nc.vector.memset(zeros[:], 0.0)
@@ -146,15 +147,23 @@ def tile_list_rgg_none_kernel(
                     return codes[:, a, 2 * (j0 - p0) : 2 * (j1 - p0)].bitcast(FP4X4)
             raise ValueError("no tile holds these edges")
 
-        picked = keep.tile([P, 2 * J], U8, name="picked", align_bytes=64)
-        nc.vector.tensor_copy(picked[:, 0:J], table_scales.indirect(src_list[:]))
-        nc.vector.tensor_copy(picked[:, J : 2 * J], table_scales.indirect(dst_list[:]))
-        moved = keep.tile([P, PASSES, 2 * J], U8, name="moved", align_bytes=64)
-        for q in range(4):
-            nc.sync.dma_start(
-                moved[32 * q : 32 * q + 4, :, :].bitcast(I32),
-                picked[ROWS_AT + 8 * q : ROWS_AT + 8 * (q + 1), :].bitcast(I32),
-            )
+        def move_scales(picked, moved):
+            for q in range(4):
+                nc.sync.dma_start(
+                    moved[32 * q : 32 * q + 4, :, :].bitcast(I32),
+                    picked[ROWS_AT + 8 * q : ROWS_AT + 8 * (q + 1), :].bitcast(I32),
+                )
+
+        src_picked = keep.tile([P, J], U8, name="src_picked", align_bytes=64)
+        nc.vector.tensor_copy(src_picked[:], table_scales.indirect(src_list[:]))
+        src_planes = keep.tile([P, PASSES, J], U8, name="src_planes", align_bytes=64)
+        move_scales(src_picked, src_planes)
+        dst_picked = keep.tile([P, J], U8, name="dst_picked", align_bytes=64)
+        nc.vector.tensor_copy(dst_picked[:], table_scales.indirect(dst_list[:]))
+        wb_all = wb_words.rearrange("a p n i -> p a (n i)").bitcast(I32)
+        wb_codes = [on_raw.tile([P, PASSES, 2 * P], I32, name="wb_first", offset=6 * KIB + 5 * LAP, align_bytes=64)]
+        nc.sync.dma_start(wb_codes[0][:], wb_all[:, :, 0 : 2 * P])
+
         def gather_words(pairs, offsets):
             nc.vector.tensor_copy(pairs[:], table_words[:].bitcast(U32).indirect(offsets))
 
@@ -163,11 +172,12 @@ def tile_list_rgg_none_kernel(
         grouped0 = on_grouped.tile([P, PASSES, P, PACK], BF16, name="grouped0", offset=4 * KIB - LAP, align_bytes=64)
         for a in range(PASSES):
             cast_wc(0, a, grouped0)
-        wb_codes = on_first.tile([P, PASSES, N], I32, name="wb_codes", offset=0, align_bytes=64)
-        nc.sync.dma_start(wb_codes[:], wb_words.rearrange("a p n i -> p a (n i)").bitcast(I32))
-        wa_codes = on_first.tile([P, PASSES, 2 * N], U8, name="wa_codes", offset=5 * KIB, align_bytes=64)
-        nc.sync.dma_start(wa_codes[:].bitcast(I32), wa_words.rearrange("a p c -> p a c").bitcast(I32))
-        wa_planes = on_first.tile([P, PASSES, N], U8, name="wa_planes", offset=4 * KIB, align_bytes=64)
+        dst_planes = on_first.tile([P, PASSES, J], U8, name="dst_planes", offset=2 * KIB, align_bytes=64)
+        move_scales(dst_picked, dst_planes)
+        wa_all = wa_words.rearrange("a p c -> p a c").bitcast(I32)
+        wa_codes = [on_first.tile([P, PASSES, 4 * P], U8, name="wa_first", offset=4 * KIB, align_bytes=64)]
+        nc.sync.dma_start(wa_codes[0][:].bitcast(I32), wa_all[:, :, 0:P])
+        wa_planes = on_first.tile([P, PASSES, N], U8, name="wa_planes", offset=5 * KIB, align_bytes=64)
         load_planes(wa_planes, wa_scales)
         quantise_wc(0, grouped0)
         for a in range(PASSES):
@@ -177,10 +187,14 @@ def tile_list_rgg_none_kernel(
         part_words(src_low_pairs, 0, HALF, src_low[:])
         dst_pairs = on_second.tile([P, J], U32, name="dst_pairs", offset=4 * KIB, align_bytes=64)
         gather_words(dst_pairs, dst_list[:])
-        grouped1 = keep.tile([P, PASSES, P, PACK], BF16, name="grouped1", align_bytes=64)
+        grouped1 = on_later.tile([P, PASSES, P, PACK], BF16, name="grouped1", offset=KIB, align_bytes=64)
         for a in range(PASSES):
             cast_wc(1, a, grouped1)
         quantise_wc(1, grouped1)
+        wb_codes.append(on_later.tile([P, PASSES, 2 * P], I32, name="wb_rest", offset=0, align_bytes=64))
+        nc.sync.dma_start(wb_codes[1][:], wb_all[:, :, 2 * P : 4 * P])
+        wa_codes.append(on_later.tile([P, PASSES, 4 * P], U8, name="wa_rest", offset=2 * KIB, align_bytes=64))
+        nc.sync.dma_start(wa_codes[1][:].bitcast(I32), wa_all[:, :, P : 2 * P])
         dst_low = on_raw.tile([P, PASSES, 2 * HALF], U8, name="dst_low", offset=0, align_bytes=64)
         part_words(dst_pairs, 0, HALF, dst_low[:])
         src_high_pairs = on_raw.tile([P, HALF], U32, name="src_high_pairs", offset=2 * KIB, align_bytes=64)
@@ -207,7 +221,7 @@ def tile_list_rgg_none_kernel(
                         nc.tensor.matmul_mx(
                             out=bank[:, b, :],
                             lhsT=codes_at(src_parts, a, e0, e0 + P),
-                            lhsT_scale=moved[:, a, e0 : e0 + P],
+                            lhsT_scale=src_planes[:, a, e0 : e0 + P],
                             rhs=wc_codes[t][:, a, :].bitcast(FP8X4),
                             rhs_scale=wc_planes[t][:, a, :],
                             start=(a == 0),
@@ -232,20 +246,20 @@ def tile_list_rgg_none_kernel(
                 for a in range(PASSES):
                     nc.tensor.matmul_mx(
                         out=za[:, e0 - j0 : e1 - j0],
-                        lhsT=wb_codes[:, a, rows].bitcast(FP8X4),
+                        lhsT=wb_codes[t // 2][:, a, (t % 2) * P : (t % 2 + 1) * P].bitcast(FP8X4),
                         lhsT_scale=wb_planes[:, a, rows],
                         rhs=codes_at(src_parts, a, e0, e1),
-                        rhs_scale=moved[:, a, e0:e1],
+                        rhs_scale=src_planes[:, a, e0:e1],
                         start=(a == 0),
                         stop=False,
                     )
                 for a in range(PASSES):
                     nc.tensor.matmul_mx(
                         out=za[:, e0 - j0 : e1 - j0],
-                        lhsT=wa_codes[:, a, 2 * t * P : 2 * (t + 1) * P].bitcast(FP4X4),
+                        lhsT=wa_codes[t // 2][:, a, 2 * (t % 2) * P : 2 * (t % 2 + 1) * P].bitcast(FP4X4),
                         lhsT_scale=wa_planes[:, a, rows],
                         rhs=codes_at(dst_parts, a, e0, e1),
-                        rhs_scale=moved[:, a, J + e0 : J + e1],
+                        rhs_scale=dst_planes[:, a, e0:e1],
                         start=False,
                         stop=(a == PASSES - 1),
                     )

@@ -55,6 +55,9 @@ def tile_list_rgg_none_kernel(
         nc.vector.memset(wgo_rows[:], 0.0)
         zeros = on_zeros.tile([P, P], F32, name="zeros", offset=4 * T - LAP)
         nc.vector.memset(zeros[:], 0.0)
+        warm_tile = keep.tile([P, 1], F32, name="warm_tile")
+        nc.scalar.activation(warm_tile[:], zeros[:, 0:1], ACT.Sigmoid)
+
         ident_tile = keep.tile([P, P], F32, name="ident")
         ident = ident_tile[:]
         nc.gpsimd.affine_select(
@@ -71,9 +74,6 @@ def tile_list_rgg_none_kernel(
             window = on_zeros.tile([P, T], F32, name="window%d" % w, offset=4 * T * w)
             nc.gpsimd.memset(window[:], 0.0)
             windows.append(window)
-
-        warm_tile = keep.tile([P, 1], F32, name="warm_tile")
-        nc.scalar.activation(warm_tile[:], ident[:, 0:1], ACT.Sigmoid)
 
         def load_planes(planes, scales):
             for q in range(4):

@@ -209,7 +209,7 @@ def tile_list_rgg_none_kernel(
         nc.gpsimd.memset(window[:], 0.0)
         windows.append(window)
 
-        def messages(n, t, j0, j1, weighted, message):
+        def messages(n, t, j0, j1, weighted):
             blocks = (j1 - j0) // P
             groups = 2 if n == 0 else 1
             per = blocks // groups
@@ -232,6 +232,9 @@ def tile_list_rgg_none_kernel(
                     nc.scalar.activation(
                         weighted[:, g * per + b, :], bank[:, b, :], ACT.Copy, scale=wgo_cols[:, col : col + 1]
                     )
+
+        def turn(n, j0, j1, weighted, message):
+            blocks = (j1 - j0) // P
             turned = psum.tile([P, j1 - j0], F32, name="turned%d" % n, offset=BANK * (6 + n % 2))[:]
             for b in range(blocks):
                 nc.tensor.transpose(turned[:, b * P : (b + 1) * P], weighted[:, b, :], ident)
@@ -281,8 +284,13 @@ def tile_list_rgg_none_kernel(
                     weighted = on_weighted.tile([P, 4, P], F32, name="weighted%d" % n, offset=2 * KIB * (n - 1), align_bytes=64)
                 else:
                     weighted = ring.tile([P, 4, P], F32, name="weighted")
-                messages(n, t, e0, e1, weighted, message[:, e0 - j0 : e1 - j0])
-                gate(n, t, e0, e1, eta[:, e0 - j0 : e1 - j0])
+                messages(n, t, e0, e1, weighted)
+                if n == 0:
+                    turn(n, e0, e1, weighted, message[:, e0 - j0 : e1 - j0])
+                    gate(n, t, e0, e1, eta[:, e0 - j0 : e1 - j0])
+                else:
+                    gate(n, t, e0, e1, eta[:, e0 - j0 : e1 - j0])
+                    turn(n, e0, e1, weighted, message[:, e0 - j0 : e1 - j0])
                 n = n + 1
             place(t, j0, j1, eta[:], message[:])
             if j1 == J:

from contextlib import ExitStack

import concourse.mybir as mybir

K, N, T, J = 1024, 512, 2048, 1024
FLOPS = 3 * 2 * K * N * J

F32 = mybir.dt.float32
BF16 = mybir.dt.bfloat16
I32 = mybir.dt.int32
U32 = mybir.dt.uint32
U16 = mybir.dt.uint16
U8 = mybir.dt.uint8
FP8X4 = mybir.dt.float8_e4m3fn_x4
FP4X4 = mybir.dt.float4_e2m1fn_x4
ACT = mybir.ActivationFunctionType
MULT = mybir.AluOpType.mult

P = 128
PACK = 4
K_PASS = P * PACK
PASSES = K // K_PASS
TILES = N // P
HALF = 512
FIRST = 256
ROWS_AT = 96
BANK = 2048
LAP = 64
KIB = 1024


def tile_list_rgg_none_kernel(
    tc, tab_words, tab_scales, wa_words, wa_scales, wb_words, wb_scales, wc, wgo, offs, offs2, out
):
    nc = tc.nc
    with ExitStack() as ctx:
        lists = ctx.enter_context(tc.tile_pool(name="lists", bufs=1))
        keep = ctx.enter_context(tc.tile_pool(name="keep", bufs=1))
        ring = ctx.enter_context(tc.tile_pool(name="ring", bufs=3))
        psum = ctx.enter_context(tc.psum_pool(name="psum", bufs=1))
        on_zeros = ctx.enter_context(tc.tile_pool(name="on_zeros", bufs=1))
        on_first = ctx.enter_context(tc.tile_pool(name="on_first", bufs=1))
        on_weighted = ctx.enter_context(tc.tile_pool(name="on_weighted", bufs=1))
        on_second = ctx.enter_context(tc.tile_pool(name="on_second", bufs=1))
        on_grouped = ctx.enter_context(tc.tile_pool(name="on_grouped", bufs=1))
        on_later = ctx.enter_context(tc.tile_pool(name="on_later", bufs=1))
        on_raw = ctx.enter_context(tc.tile_pool(name="on_raw", bufs=1))

        src_list = lists.tile([P, J // 16], U16, name="src_list")
        dst_list = lists.tile([P, J // 16], U16, name="dst_list")

        table_scales = keep.tile([P, T], U8, name="table_scales", align_bytes=64)[:]
        nc.vector.memset(table_scales[0:ROWS_AT, :].bitcast(I32), 0)
        wgo_rows = on_raw.tile([P, P], F32, name="wgo_rows", offset=6 * KIB, align_bytes=64)
        nc.vector.memset(wgo_rows[:], 0.0)
        zeros = on_zeros.tile([P, P], F32, name="zeros", offset=4 * T - LAP)
        nc.vector.memset(zeros[:], 0.0)
        warm_tile = keep.tile([P, 1], F32, name="warm_tile")
        nc.scalar.activation(warm_tile[:], zeros[:, 0:1], ACT.Sigmoid)

        ident_tile = keep.tile([P, P], F32, name="ident")
        ident = ident_tile[:]
        nc.gpsimd.affine_select(
            out=ident,
            in_=zeros[:],
            compare_op=mybir.AluOpType.not_equal,
            fill=1.0,
            base=0,
            pattern=[[-1, P]],
            channel_multiplier=1,
        )
        windows = []
        for w in range(2):
            window = on_zeros.tile([P, T], F32, name="window%d" % w, offset=4 * T * w)
            nc.gpsimd.memset(window[:], 0.0)
            windows.append(window)

        def load_planes(planes, scales):
            for q in range(4):
                nc.sync.dma_start(
                    planes[32 * q : 32 * q + 4, :, :].bitcast(I32),
                    scales[:, 4 * q : 4 * q + 4, :].rearrange("a r n -> r a n").bitcast(I32),
                )

        wc_raw = {}

        def load_wc(t0, a, raw):
            tiles = raw.shape[2] // P
            nc.sync.dma_start(
                raw, wc[a * K_PASS : (a + 1) * K_PASS, t0 * P : (t0 + tiles) * P].rearrange("(p i) n -> p i n", i=PACK)
            )
            for t in range(tiles):
                wc_raw[t0 + t, a] = raw[:, :, t * P : (t + 1) * P]

        nc.sync.dma_start(table_scales[ROWS_AT:P, :].bitcast(I32), tab_scales.rearrange("a g t -> g a t").bitcast(I32))
        nc.sync.dma_start(src_list[:], offs)
        nc.sync.dma_start(dst_list[:], offs2)
        table_words = keep.tile([P, T], I32, name="table_words", align_bytes=64)
        nc.sync.dma_start(table_words[:], tab_words[0].rearrange("p t b -> p (t b)").bitcast(I32))
        raw00 = on_first.tile([P, PACK, P], F32, name="raw00", offset=4 * KIB - LAP, align_bytes=64)
        load_wc(0, 0, raw00[:])
        raw01 = on_second.tile([P, PACK, P], F32, name="raw01", offset=4 * KIB - LAP, align_bytes=64)
        load_wc(0, 1, raw01[:])
        nc.sync.dma_start(wgo_rows[0 : J // P, :], wgo[0, :].rearrange("(c p) -> c p", p=P))
        wb_planes = keep.tile([P, PASSES, N], U8, name="wb_planes", align_bytes=64)
        load_planes(wb_planes, wb_scales)
        raw1 = on_raw.tile([P, PASSES, PACK, P], F32, name="raw1", offset=2 * KIB - LAP, align_bytes=64)
        for a in range(PASSES):
            load_wc(1, a, raw1[:, a, :, :])

        wgo_psum = psum.tile([P, HALF], F32, name="wgo_psum", offset=7 * BANK)
        nc.tensor.transpose(wgo_psum[:, 0:P], wgo_rows[:], ident)
        wgo_cols = keep.tile([P, J // P], F32, name="wgo_cols")
        nc.scalar.copy(wgo_cols[:], wgo_psum[:, 0 : J // P])

        def cast_wc(t, a, grouped):
            nc.scalar.copy(
                grouped[:, a, :, :].rearrange("p (g m) i -> p g i m", m=4),
                wc_raw[t, a].rearrange("p i (g m) -> p g i m", m=4),
            )

        wc_codes = {}
        wc_planes = {}

        def quantise_wc(t0, grouped):
            width = grouped.shape[2]
            codes = keep.tile([P, PASSES, width], U32, name="wc_codes%d" % t0, align_bytes=64)
            planes = keep.tile([P, PASSES, width], U8, name="wc_planes%d" % t0, align_bytes=64)
            nc.vector.quantize_mx(
                out=codes[:].rearrange("p a n -> p (a n)").bitcast(FP8X4),
                scales=planes[:].rearrange("p a n -> p (a n)"),
                in_=grouped[:].rearrange("p a n i -> p (a n i)"),
            )
            for t in range(width // P):
                wc_codes[t0 + t] = codes[:, :, t * P : (t + 1) * P]
                wc_planes[t0 + t] = planes[:, :, t * P : (t + 1) * P]

        def part_words(pairs, j0, j1, codes):
            nc.vector.tensor_copy(
                codes.bitcast(U16).rearrange("p d (g j) -> p g d j", g=2),
                pairs[:, j0:j1].bitcast(U16).rearrange("p (g j d) -> p g d j", g=2, d=PASSES),
            )

        def codes_at(parts, a, j0, j1):
            for p0, p1, codes in parts:
                if p0 <= j0 and j1 <= p1:
                    return codes[:, a, 2 * (j0 - p0) : 2 * (j1 - p0)].bitcast(FP4X4)
            raise ValueError("no tile holds these edges")

        def move_scales(picked, moved):
            for q in range(4):
                nc.sync.dma_start(
                    moved[32 * q : 32 * q + 4, :, :].bitcast(I32),
                    picked[ROWS_AT + 8 * q : ROWS_AT + 8 * (q + 1), :].bitcast(I32),
                )

        src_picked = keep.tile([P, J], U8, name="src_picked", align_bytes=64)
        nc.vector.tensor_copy(src_picked[:], table_scales.indirect(src_list[:]))
        src_planes = keep.tile([P, PASSES, J], U8, name="src_planes", align_bytes=64)
        move_scales(src_picked, src_planes)
        dst_picked = keep.tile([P, J], U8, name="dst_picked", align_bytes=64)
        nc.vector.tensor_copy(dst_picked[:], table_scales.indirect(dst_list[:]))
        wb_all = wb_words.rearrange("a p n i -> p a (n i)").bitcast(I32)
        wb_codes = [on_raw.tile([P, PASSES, 2 * P], I32, name="wb_first", offset=6 * KIB + 5 * LAP, align_bytes=64)]
        nc.sync.dma_start(wb_codes[0][:], wb_all[:, :, 0 : 2 * P])

        def gather_words(pairs, offsets):
            nc.vector.tensor_copy(pairs[:], table_words[:].bitcast(U32).indirect(offsets))

        src_low_pairs = keep.tile([P, HALF], U32, name="src_low_pairs", align_bytes=64)
        gather_words(src_low_pairs, src_list[:, 0 : HALF // 16])
        grouped0 = on_grouped.tile([P, PASSES, P, PACK], BF16, name="grouped0", offset=4 * KIB - LAP, align_bytes=64)
        for a in range(PASSES):
            cast_wc(0, a, grouped0)
        dst_planes = on_first.tile([P, PASSES, J], U8, name="dst_planes", offset=2 * KIB, align_bytes=64)
        move_scales(dst_picked, dst_planes)
        wa_all = wa_words.rearrange("a p c -> p a c").bitcast(I32)
        wa_codes = [on_first.tile([P, PASSES, 4 * P], U8, name="wa_first", offset=4 * KIB, align_bytes=64)]
        nc.sync.dma_start(wa_codes[0][:].bitcast(I32), wa_all[:, :, 0:P])
        wa_planes = on_first.tile([P, PASSES, N], U8, name="wa_planes", offset=5 * KIB, align_bytes=64)
        load_planes(wa_planes, wa_scales)
        quantise_wc(0, grouped0)
        for a in range(PASSES):
            raw = on_grouped.tile([P, PACK, 2 * P], F32, name="raw2%d" % a, offset=a * 5 * KIB, align_bytes=64)
            load_wc(2, a, raw[:])
        src_low = on_second.tile([P, PASSES, 2 * HALF], U8, name="src_low", offset=2 * KIB, align_bytes=64)
        part_words(src_low_pairs, 0, HALF, src_low[:])
        dst_pairs = on_second.tile([P, J], U32, name="dst_pairs", offset=4 * KIB, align_bytes=64)
        gather_words(dst_pairs, dst_list[:])
        grouped1 = on_later.tile([P, PASSES, P, PACK], BF16, name="grouped1", offset=KIB, align_bytes=64)
        for a in range(PASSES):
            cast_wc(1, a, grouped1)
        quantise_wc(1, grouped1)
        wb_codes.append(on_later.tile([P, PASSES, 2 * P], I32, name="wb_rest", offset=0, align_bytes=64))
        nc.sync.dma_start(wb_codes[1][:], wb_all[:, :, 2 * P : 4 * P])
        wa_codes.append(on_later.tile([P, PASSES, 4 * P], U8, name="wa_rest", offset=2 * KIB, align_bytes=64))
        nc.sync.dma_start(wa_codes[1][:].bitcast(I32), wa_all[:, :, P : 2 * P])
        dst_low = on_raw.tile([P, PASSES, 2 * HALF], U8, name="dst_low", offset=0, align_bytes=64)
        part_words(dst_pairs, 0, HALF, dst_low[:])
        src_high_pairs = on_raw.tile([P, HALF], U32, name="src_high_pairs", offset=2 * KIB, align_bytes=64)
        gather_words(src_high_pairs, src_list[:, HALF // 16 : J // 16])
        dst_high = on_raw.tile([P, PASSES, 2 * HALF], U8, name="dst_high", offset=4 * KIB, align_bytes=64)
        part_words(dst_pairs, HALF, J, dst_high[:])
        src_high = keep.tile([P, PASSES, 2 * HALF], U8, name="src_high", align_bytes=64)
        part_words(src_high_pairs, 0, HALF, src_high[:])
        src_parts = [(0, HALF, src_low), (HALF, J, src_high)]
        dst_parts = [(0, HALF, dst_low), (HALF, J, dst_high)]
        window = on_second.tile([P, T], F32, name="window2", offset=8 * KIB - LAP, align_bytes=64)
        nc.gpsimd.memset(window[:], 0.0)
        windows.append(window)

        def messages(n, t, j0, j1, weighted):
            blocks = (j1 - j0) // P
            groups = 2 if n == 0 else 1
            per = blocks // groups
            for g in range(groups):
                bank = psum.tile([P, per, P], F32, name="ms%d%d" % (n, g), offset=BANK * (g if n == 0 else 3 + n % 2))
                for b in range(per):
                    e0 = j0 + (g * per + b) * P
                    for a in range(PASSES):
                        nc.tensor.matmul_mx(
                            out=bank[:, b, :],
                            lhsT=codes_at(src_parts, a, e0, e0 + P),
                            lhsT_scale=src_planes[:, a, e0 : e0 + P],
                            rhs=wc_codes[t][:, a, :].bitcast(FP8X4),
                            rhs_scale=wc_planes[t][:, a, :],
                            start=(a == 0),
                            stop=(a == PASSES - 1),
                        )
                for b in range(per):
                    col = j0 // P + g * per + b
                    nc.scalar.activation(
                        weighted[:, g * per + b, :], bank[:, b, :], ACT.Copy, scale=wgo_cols[:, col : col + 1]
                    )

        def turn(n, j0, j1, weighted, message):
            blocks = (j1 - j0) // P
            turned = psum.tile([P, j1 - j0], F32, name="turned%d" % n, offset=BANK * (6 + n % 2))[:]
            for b in range(blocks):
                nc.tensor.transpose(turned[:, b * P : (b + 1) * P], weighted[:, b, :], ident)
            nc.scalar.copy(message, turned)

        def gate(n, t, j0, j1, eta):
            rows = slice(t * P, (t + 1) * P)
            width = 4 * HALF if n == 0 else j1 - j0
            za = psum.tile([P, width], F32, name="za%d" % n, offset=BANK * (2 + 3 * (n % 2)))[:, 0 : j1 - j0]
            cuts = [j0, j1]
            for e0, e1 in zip(cuts, cuts[1:]):
                for a in range(PASSES):
                    nc.tensor.matmul_mx(
                        out=za[:, e0 - j0 : e1 - j0],
                        lhsT=wb_codes[t // 2][:, a, (t % 2) * P : (t % 2 + 1) * P].bitcast(FP8X4),
                        lhsT_scale=wb_planes[:, a, rows],
                        rhs=codes_at(src_parts, a, e0, e1),
                        rhs_scale=src_planes[:, a, e0:e1],
                        start=(a == 0),
                        stop=False,
                    )
                for a in range(PASSES):
                    nc.tensor.matmul_mx(
                        out=za[:, e0 - j0 : e1 - j0],
                        lhsT=wa_codes[t // 2][:, a, 2 * (t % 2) * P : 2 * (t % 2 + 1) * P].bitcast(FP4X4),
                        lhsT_scale=wa_planes[:, a, rows],
                        rhs=codes_at(dst_parts, a, e0, e1),
                        rhs_scale=dst_planes[:, a, e0:e1],
                        start=False,
                        stop=(a == PASSES - 1),
                    )
            nc.scalar.activation(eta, za, ACT.Sigmoid)

        def place(t, j0, j1, eta, message):
            nc.vector.tensor_tensor(
                windows[t % 3][:].indirect(dst_list[:, j0 // 16 : j1 // 16]), eta, message, MULT
            )

        scatters = [(0, 0, HALF), (1, 0, HALF), (0, HALF, J), (1, HALF, J), (2, 0, J), (3, 0, J)]
        n = 0
        for s, (t, j0, j1) in enumerate(scatters):
            message = keep.tile([P, j1 - j0], F32, name="message%d" % s)
            eta = keep.tile([P, j1 - j0], F32, name="eta%d" % s)
            cuts = [j0, HALF, j1] if j0 < HALF < j1 else [j0, j1]
            for e0, e1 in zip(cuts, cuts[1:]):
                if n in (1, 2):
                    weighted = on_weighted.tile([P, 4, P], F32, name="weighted%d" % n, offset=2 * KIB * (n - 1), align_bytes=64)
                else:
                    weighted = ring.tile([P, 4, P], F32, name="weighted")
                messages(n, t, e0, e1, weighted)
                if n == 0:
                    turn(n, e0, e1, weighted, message[:, e0 - j0 : e1 - j0])
                    gate(n, t, e0, e1, eta[:, e0 - j0 : e1 - j0])
                else:
                    gate(n, t, e0, e1, eta[:, e0 - j0 : e1 - j0])
                    turn(n, e0, e1, weighted, message[:, e0 - j0 : e1 - j0])
                n = n + 1
            place(t, j0, j1, eta[:], message[:])
            if j1 == J:
                nc.sync.dma_start(out[t * P : (t + 1) * P, :], windows[t % 3][:])
            if s in (1, 2):
                lent = on_weighted.tile([P, PASSES, P, PACK], BF16, name="grouped%d" % (s + 1), offset=2 * KIB * (s - 1), align_bytes=64)
                for a in range(PASSES):
                    cast_wc(s + 1, a, lent)
                quantise_wc(s + 1, lent)
